import numpy as np
import ml_dtypes


def mxq(x, axis, fmt="e4m3"):
    dtype, down = {"e4m3": (ml_dtypes.float8_e4m3fn, 7), "e5m2": (ml_dtypes.float8_e5m2, 14)}[fmt]
    v = np.moveaxis(np.asarray(x, np.float32).astype(ml_dtypes.bfloat16).astype(np.float64), axis, -1)
    blocks = v.reshape(v.shape[:-1] + (-1, 32))
    amax = np.abs(blocks).max(-1, keepdims=True)
    byte = np.maximum(np.where(amax > 0, np.frexp(amax)[1] - 1 + 127, 0) - down, 1)
    scale = np.exp2(byte - 127.0)
    codes = (blocks / scale).astype(np.float32).astype(dtype).astype(np.float64)
    return np.moveaxis((codes * scale).reshape(v.shape), -1, axis)


WIDE = False


def mx_kscale(k):
    if not WIDE:
        return np.ones(k)
    levels = np.array([10, -10, 5, -5, 0])
    if k % 512:
        return np.exp2(np.random.permutation(np.resize(levels, k // 32))).repeat(32)
    a = np.empty((k // 512, 16))
    for p in range(k // 512):
        a[p, :8] = np.random.permutation(np.resize(levels, 8))
        for g in range(8):
            far = levels[np.abs(levels - a[p, g]) >= 10]
            a[p, g + 8] = far[np.random.randint(len(far))]
    return np.exp2(a.ravel()).repeat(32)


def f64(x):
    return np.asarray(x).astype(np.float64)


def striped(idx):
    return np.tile(idx.reshape(-1, 16).T, (8, 1)).astype(np.uint16)


def unstriped(offs):
    return offs[:16].T.reshape(-1).astype(np.int64)


def silu(v):
    return v / (1.0 + np.exp(-np.maximum(v, -700.0)))


K, T, E, C, H, N = 512, 640, 10, 128, 512, 128


def by_expert(wq, xq):
    return np.concatenate([wq[e].T @ xq[:, e * C:(e + 1) * C] for e in range(E)], axis=1)


def setup_inputs():
    n = np.random.standard_normal
    s = mx_kscale(K)[:, None]
    u = mx_kscale(H)
    first = np.random.permutation(np.repeat(np.arange(E), T // E))
    second = (first + 1 + np.random.permutation(np.repeat(np.arange(E - 1), -(-T // (E - 1)))[:T])) % E
    while np.bincount(second, minlength=E).max() != T // E:
        load = np.bincount(second, minlength=E); hi, lo = int(load.argmax()), int(load.argmin())
        t = np.flatnonzero((second == hi) & (first != lo))[0]; second[t] = lo
    slot_token = np.empty(E * C, np.int64); pos = np.empty((2, T), np.int64); fill = np.zeros(E, np.int64)
    place = np.stack([np.random.permutation(C) for _ in range(E)])
    for r, deal in enumerate((first, second)):
        for t in np.random.permutation(T):
            e = deal[t]; j = e * C + place[e, fill[e]]; fill[e] += 1; slot_token[j] = t; pos[r, t] = j
    g = np.random.uniform(0.2, 0.8, T)
    w_slot = np.empty(E * C); w_slot[pos[0]] = g; w_slot[pos[1]] = 1.0 - g
    return {
        "xT": (n((K, T)) * s).astype(np.float32),
        "w1": (n((E, K, H)) / np.sqrt(K) / s[None] * u[None, None, :]).astype(np.float32),
        "w2": (n((E, H, N)) / np.sqrt(H) / u[None, :, None]).astype(np.float32),
        "gate": np.tile(w_slot, (K, 1)).astype(np.float32),
        "offs": striped(slot_token),
        "pos1": striped(pos[0]),
        "pos2": striped(pos[1]),
    }


def reference(xT, w1, w2, gate, offs, pos1, pos2):
    idx = unstriped(offs)
    xq = mxq(f64(gate) * f64(xT)[:, idx], 0, "e4m3")
    h = silu(by_expert(mxq(f64(w1), 1, "e4m3"), xq))
    y = by_expert(mxq(f64(w2), 1, "e4m3"), mxq(h, 0, "e4m3"))
    return y[:, unstriped(pos1)] + y[:, unstriped(pos2)]

@@ -1,0 +1,157 @@
+from contextlib import ExitStack
+
+import concourse.mybir as mybir
+
+K, T, E, C, H, N = 512, 640, 10, 128, 512, 128
+S = E * C
+P = 128
+PACK = 4
+FLOPS = 2 * S * (K * H + H * N)
+BYTES = 4 * (K * T + E * K * H + E * H * N + S + N * T) + 2 * P * (S + 2 * T) // 16
+
+F32 = mybir.dt.float32
+BF16 = mybir.dt.bfloat16
+U32 = mybir.dt.uint32
+U16 = mybir.dt.uint16
+U8 = mybir.dt.uint8
+FP8X4 = mybir.dt.float8_e4m3fn_x4
+MULT = mybir.AluOpType.mult
+ADD = mybir.AluOpType.add
+SILU = mybir.ActivationFunctionType.Silu
+
+GATHER_CUTS = (0, 256, 768, 1280)
+W1_VECTOR_SHARE = (0, 64, 128, 48, 112, 112, 128, 16, 96, 64)
+X_ENGINES = "SSSSS"
+W2_ENGINES = "SSVSV"
+LOAD_ORDER = "offs x0 g0 x1 x2 x3 g1 g2 a0 a1 a2 a3 b0 a4 b1 a5 pos a6 a7 a8 b2 a9 b3 b4".split()
+STEPS = "G0 X0 G1 X1 W0 Z0 W1 G2 X2 Q0 H0 Q1 W2 W3 Z1 Q2 Q3 H1 Z2 X3 W4 Q4 H2 U0 W5 I0 V0 I1 H3 Q5 Z3 X4 W6 I2 Q6 W7 Z4 H4 U1 Q7 I3 W8 H5 V1 U2 H6 Q8 H7 V2 W9 H8 U3 Y0 I4 Q9 I5 I6 H9 I7 U4 I8 Y1 V3 Y2 Y3 V4 I9 Y4".split()
+OUT_CUTS = (0, 320, 640)
+RING = 2
+A_BANKS = 4
+Y_BANKS = 3
+
+
+def tile_moe_pre_mlp_silu_kernel(tc, xT, w1, w2, gate, offs, pos1, pos2, out):
+    nc = tc.nc
+    with ExitStack() as ctx:
+        held = ctx.enter_context(tc.tile_pool(name="held", bufs=1))
+        psum = ctx.enter_context(tc.psum_pool(name="psum", bufs=1))
+
+        offs_sb = held.tile([P, S // 16], U16, name="offs_sb")
+        pos1_sb = held.tile([P, T // 16], U16, name="pos1_sb")
+        pos2_sb = held.tile([P, T // 16], U16, name="pos2_sb")
+        chunks = list(zip(GATHER_CUTS[:-1], GATHER_CUTS[1:]))
+        x_rows = [held.tile([P, T], F32, name="x_rows%d" % j) for j in range(PACK)]
+        gate_sb = [held.tile([P, b - a], F32, name="gate%d" % a) for a, b in chunks]
+        w1_raw = [held.tile([P, PACK, H], F32, name="w1_raw%d" % e) for e in range(E)]
+        w2_raw = [held.tile([P, 2, PACK, N], F32, name="w2_raw%d" % q) for q in range(E // 2)]
+        x_view = xT.rearrange("(p j) t -> p j t", j=PACK)
+
+        for what in LOAD_ORDER:
+            if what == "offs":
+                nc.sync.dma_start(offs_sb[:], offs)
+            elif what == "pos":
+                nc.sync.dma_start(pos1_sb[:], pos1)
+                nc.sync.dma_start(pos2_sb[:], pos2)
+            else:
+                i = int(what[1])
+                if what[0] == "x":
+                    nc.sync.dma_start(x_rows[i][:], x_view[:, i, :])
+                elif what[0] == "g":
+                    nc.sync.dma_start(gate_sb[i][:], gate[0:P, chunks[i][0]:chunks[i][1]])
+                elif what[0] == "a":
+                    nc.sync.dma_start(w1_raw[i][:], w1[i].rearrange("(p j) c -> p j c", j=PACK))
+                else:
+                    nc.sync.dma_start(w2_raw[i][:].rearrange("p e j n -> p e (j n)"),
+                                      w2[2 * i:2 * i + 2].rearrange("e (p j) n -> p e (j n)", j=PACK))
+
+        def operand(name, count, width):
+            codes = [held.tile([P, width], U32, name="%s_codes%d" % (name, i), align_bytes=64) for i in range(count)]
+            scales = [held.tile([P, width], U8, name="%s_scales%d" % (name, i), align_bytes=64) for i in range(count)]
+            return codes, scales
+
+        x_codes, x_scales = operand("x", E // 2, 2 * C)
+        w1_codes, w1_scales = operand("w1", E, H)
+        h_codes, h_scales = operand("h", E, C)
+        w2_codes, w2_scales = operand("w2", E // 2, 2 * N)
+        picked = [held.tile([P, PACK, b - a], F32, name="picked%d" % a) for a, b in chunks]
+        x_bf = [held.tile([P, 2 * C, PACK], BF16, name="x_bf%d" % q, align_bytes=64) for q in range(E // 2)]
+        h_bf = [held.tile([P, C, PACK], BF16, name="h_bf%d" % e, align_bytes=64) for e in range(E)]
+        stage = [held.tile([P, PACK * H], BF16, name="stage%d" % r, align_bytes=64) for r in range(RING)]
+        a_ps = [psum.tile([P, PACK, C], F32, name="a_ps%d" % r) for r in range(A_BANKS)]
+        y_ps = [psum.tile([P, 2 * C], F32, name="y_ps%d" % r) for r in range(Y_BANKS)]
+        y_all = held.tile([P, S], F32, name="y_all")
+        staged = [s for s in STEPS if s[0] in "WU"]
+
+        def cast(engine, dst, src):
+            if engine == "S":
+                nc.scalar.copy(dst, src)
+            else:
+                nc.vector.tensor_copy(dst, src)
+
+        def quantize(codes, scales, src):
+            nc.vector.quantize_mx(out=codes[:].bitcast(FP8X4), scales=scales[:], in_=src)
+
+        for step in STEPS:
+            kind, i = step[0], int(step[1])
+            if kind == "G":
+                a, b = chunks[i]
+                for j in range(PACK):
+                    nc.vector.tensor_tensor(picked[i][:, j, :], x_rows[j][:].indirect(offs_sb[:, a // 16:b // 16]),
+                                            gate_sb[i][:], MULT)
+            elif kind == "X":
+                g = max(n for n, (a, b) in enumerate(chunks) if a <= 2 * C * i)
+                lo = 2 * C * i - chunks[g][0]
+                cast(X_ENGINES[i], x_bf[i][:].rearrange("p (c i) j -> p c j i", i=4),
+                     picked[g][:, :, lo:lo + 2 * C].rearrange("p j (c i) -> p c j i", i=4))
+            elif kind == "Z":
+                quantize(x_codes[i], x_scales[i], x_bf[i][:].rearrange("p c j -> p (c j)"))
+            elif kind == "W":
+                buf = stage[staged.index(step) % RING]
+                dst = buf[:].rearrange("p (t m j) -> p m j t", t=PACK, j=PACK)
+                src = w1_raw[i][:].rearrange("p j (m t) -> p m j t", t=PACK)
+                cut = P - W1_VECTOR_SHARE[i]
+                if cut > 0:
+                    nc.scalar.copy(dst[:, 0:cut], src[:, 0:cut])
+                if cut < P:
+                    nc.vector.tensor_copy(dst[:, cut:P], src[:, cut:P])
+            elif kind == "Q":
+                buf = stage[staged.index("W%d" % i) % RING]
+                quantize(w1_codes[i], w1_scales[i], buf[:])
+                slots = slice((i % 2) * C, (i % 2 + 1) * C)
+                for t in range(PACK):
+                    cols = slice(t * P, (t + 1) * P)
+                    nc.tensor.matmul_mx(out=a_ps[i % A_BANKS][:, t, :], lhsT=w1_codes[i][:, cols].bitcast(FP8X4),
+                                        lhsT_scale=w1_scales[i][:, cols],
+                                        rhs=x_codes[i // 2][:, slots].bitcast(FP8X4),
+                                        rhs_scale=x_scales[i // 2][:, slots], start=True, stop=True)
+            elif kind == "H":
+                nc.scalar.activation(h_bf[i][:], a_ps[i % A_BANKS][:].rearrange("p t c -> p c t"), SILU)
+            elif kind == "I":
+                quantize(h_codes[i], h_scales[i], h_bf[i][:].rearrange("p c t -> p (c t)"))
+            elif kind == "U":
+                buf = stage[staged.index(step) % RING]
+                cast(W2_ENGINES[i],
+                     buf[:, 0:2 * N * PACK].rearrange("p (e c i j) -> p e c j i", e=2, i=4, j=PACK),
+                     w2_raw[i][:].rearrange("p e j (c i) -> p e c j i", i=4))
+            elif kind == "V":
+                buf = stage[staged.index("U%d" % i) % RING]
+                quantize(w2_codes[i], w2_scales[i], buf[:, 0:2 * N * PACK])
+            else:
+                for r in range(2):
+                    cols = slice(r * N, (r + 1) * N)
+                    nc.tensor.matmul_mx(out=y_ps[i % Y_BANKS][:, r * C:(r + 1) * C],
+                                        lhsT=w2_codes[i][:, cols].bitcast(FP8X4), lhsT_scale=w2_scales[i][:, cols],
+                                        rhs=h_codes[2 * i + r][:].bitcast(FP8X4), rhs_scale=h_scales[2 * i + r][:],
+                                        start=True, stop=True)
+                nc.scalar.copy(y_all[:, 2 * i * C:(2 * i + 2) * C], y_ps[i % Y_BANKS][:])
+
+        pieces = list(zip(OUT_CUTS[:-1], OUT_CUTS[1:]))
+        for a, b in pieces:
+            first = held.tile([P, b - a], F32, name="first%d" % a)
+            second = held.tile([P, b - a], F32, name="second%d" % a)
+            total = held.tile([P, b - a], F32, name="total%d" % a)
+            nc.vector.tensor_copy(first[:], y_all[:].indirect(pos1_sb[:, a // 16:b // 16]))
+            nc.vector.tensor_copy(second[:], y_all[:].indirect(pos2_sb[:, a // 16:b // 16]))
+            nc.vector.tensor_tensor(total[:], first[:], second[:], ADD)
+            nc.sync.dma_start(out[:, a:b], total[:])

@@ -19,14 +19,16 @@ MULT = mybir.AluOpType.mult
 ADD = mybir.AluOpType.add
 SILU = mybir.ActivationFunctionType.Silu
 
-GATHER_CUTS = (0, 256, 768, 1280)
-W1_VECTOR_SHARE = (0, 64, 128, 48, 112, 112, 128, 16, 96, 64)
-X_ENGINES = "SSSSS"
-W2_ENGINES = "SSVSV"
-LOAD_ORDER = "offs x0 g0 x1 x2 x3 g1 g2 a0 a1 a2 a3 b0 a4 b1 a5 pos a6 a7 a8 b2 a9 b3 b4".split()
-STEPS = "G0 X0 G1 X1 W0 Z0 W1 G2 X2 Q0 H0 Q1 W2 W3 Z1 Q2 Q3 H1 Z2 X3 W4 Q4 H2 U0 W5 I0 V0 I1 H3 Q5 Z3 X4 W6 I2 Q6 W7 Z4 H4 U1 Q7 I3 W8 H5 V1 U2 H6 Q8 H7 V2 W9 H8 U3 Y0 I4 Q9 I5 I6 H9 I7 U4 I8 Y1 V3 Y2 Y3 V4 I9 Y4".split()
+GATHER_CUTS = (0, 256, 512, 768, 1024, 1280)
+W1_ENGINES = "BSSVSSBBVS"
+W2_GROUPS = ((0, 1), (2, 3), (4, 5), (6, 7), (8,), (9,))
+X_ENGINES = "SBVVB"
+W2_ENGINES = "VBVBVV"
+LOAD_ORDER = "offs g0 x0 x1 x2 g1 a0 g2 x3 g3 a1 b0 g4 a2 a3 a4 a5 a6 a7 a8 pos a9 b1 b2 b3 b4 b5".split()
+STEPS = "W0 G0 G1 W1 X0 W2 G2 Z0 X1 G3 W3 X2 Q0 W4 Q1 Z1 W5 Q2 Q3 H0 H1 G4 W6 I0 H2 H3 Z2 U0 I1 Q4 X3 Q5 V0 Z3 I2 W7 X4 Z4 U1 Q6 W8 U2 Q7 W9 V1 U3 H4 I3 I4 H5 Y0 Q8 Q9 H6 V2 U4 H7 H8 H9 I5 Y1 Y2 V3 I6 U5 I7 V4 I8 Y3 I9 V5 Y4 Y5".split()
 OUT_CUTS = (0, 320, 640)
-RING = 2
+REUSE = {"H7":"W9","X2":"W2","H1":"W5","H4":"W9","H0":"W2","H5":"U2","H2":"W5","X4":"W6","H3":"W5","X0":"W0","H9":"U3"}
+RING = 4
 A_BANKS = 4
 Y_BANKS = 3
 
@@ -43,8 +45,8 @@ def tile_moe_pre_mlp_silu_kernel(tc, xT, w1, w2, gate, offs, pos1, pos2, out):
         chunks = list(zip(GATHER_CUTS[:-1], GATHER_CUTS[1:]))
         x_rows = [held.tile([P, T], F32, name="x_rows%d" % j) for j in range(PACK)]
         gate_sb = [held.tile([P, b - a], F32, name="gate%d" % a) for a, b in chunks]
-        w1_raw = [held.tile([P, PACK, H], F32, name="w1_raw%d" % e) for e in range(E)]
-        w2_raw = [held.tile([P, 2, PACK, N], F32, name="w2_raw%d" % q) for q in range(E // 2)]
+        w1_raw = [held.tile([P, PACK, H], F32, name="w1_raw%d" % e, align_bytes=64) for e in range(E)]
+        w2_raw = [held.tile([P, len(g), PACK, N], F32, name="w2_raw%d" % g[0], align_bytes=64) for g in W2_GROUPS]
         x_view = xT.rearrange("(p j) t -> p j t", j=PACK)
 
         for what in LOAD_ORDER:
@@ -63,7 +65,7 @@ def tile_moe_pre_mlp_silu_kernel(tc, xT, w1, w2, gate, offs, pos1, pos2, out):
                     nc.sync.dma_start(w1_raw[i][:], w1[i].rearrange("(p j) c -> p j c", j=PACK))
                 else:
                     nc.sync.dma_start(w2_raw[i][:].rearrange("p e j n -> p e (j n)"),
-                                      w2[2 * i:2 * i + 2].rearrange("e (p j) n -> p e (j n)", j=PACK))
+                                      w2[W2_GROUPS[i][0]:W2_GROUPS[i][-1] + 1].rearrange("e (p j) n -> p e (j n)", j=PACK))
 
         def operand(name, count, width):
             codes = [held.tile([P, width], U32, name="%s_codes%d" % (name, i), align_bytes=64) for i in range(count)]
@@ -73,10 +75,24 @@ def tile_moe_pre_mlp_silu_kernel(tc, xT, w1, w2, gate, offs, pos1, pos2, out):
         x_codes, x_scales = operand("x", E // 2, 2 * C)
         w1_codes, w1_scales = operand("w1", E, H)
         h_codes, h_scales = operand("h", E, C)
-        w2_codes, w2_scales = operand("w2", E // 2, 2 * N)
+        w2_codes, w2_scales = operand("w2", len(W2_GROUPS), 2 * N)
         picked = [held.tile([P, PACK, b - a], F32, name="picked%d" % a) for a, b in chunks]
-        x_bf = [held.tile([P, 2 * C, PACK], BF16, name="x_bf%d" % q, align_bytes=64) for q in range(E // 2)]
-        h_bf = [held.tile([P, C, PACK], BF16, name="h_bf%d" % e, align_bytes=64) for e in range(E)]
+        used = {}
+
+        def rounded(step, slots):
+            if step not in REUSE:
+                return held.tile([P, slots, PACK], BF16, name="bf_" + step, align_bytes=64)[:]
+            host = REUSE[step]
+            if host[0] == "W":
+                words = w1_raw[int(host[1])][:].rearrange("p j c -> p (j c)")
+            else:
+                words = w2_raw[int(host[1])][:].rearrange("p e j n -> p (e j n)")
+            start = used.get(host, 0)
+            used[host] = start + slots * PACK // 2
+            return words[:, start:used[host]].bitcast(BF16).rearrange("p (c j) -> p c j", j=PACK)
+
+        x_bf = [rounded("X%d" % q, 2 * C) for q in range(E // 2)]
+        h_bf = [rounded("H%d" % e, C) for e in range(E)]
         stage = [held.tile([P, PACK * H], BF16, name="stage%d" % r, align_bytes=64) for r in range(RING)]
         a_ps = [psum.tile([P, PACK, C], F32, name="a_ps%d" % r) for r in range(A_BANKS)]
         y_ps = [psum.tile([P, 2 * C], F32, name="y_ps%d" % r) for r in range(Y_BANKS)]
@@ -89,8 +105,14 @@ def tile_moe_pre_mlp_silu_kernel(tc, xT, w1, w2, gate, offs, pos1, pos2, out):
             else:
                 nc.vector.tensor_copy(dst, src)
 
+        def shares(engine, count):
+            if engine == "B":
+                return [("S", 0, count // 2), ("V", count // 2, count)]
+            return [(engine, 0, count)]
+
         def quantize(codes, scales, src):
-            nc.vector.quantize_mx(out=codes[:].bitcast(FP8X4), scales=scales[:], in_=src)
+            width = src.shape[1] // PACK
+            nc.vector.quantize_mx(out=codes[:, 0:width].bitcast(FP8X4), scales=scales[:, 0:width], in_=src)
 
         for step in STEPS:
             kind, i = step[0], int(step[1])
@@ -102,19 +124,17 @@ def tile_moe_pre_mlp_silu_kernel(tc, xT, w1, w2, gate, offs, pos1, pos2, out):
             elif kind == "X":
                 g = max(n for n, (a, b) in enumerate(chunks) if a <= 2 * C * i)
                 lo = 2 * C * i - chunks[g][0]
-                cast(X_ENGINES[i], x_bf[i][:].rearrange("p (c i) j -> p c j i", i=4),
-                     picked[g][:, :, lo:lo + 2 * C].rearrange("p j (c i) -> p c j i", i=4))
+                for engine, a, b in shares(X_ENGINES[i], 2 * C):
+                    cast(engine, x_bf[i][:, a:b, :].rearrange("p (c i) j -> p c j i", i=4),
+                         picked[g][:, :, lo + a:lo + b].rearrange("p j (c i) -> p c j i", i=4))
             elif kind == "Z":
-                quantize(x_codes[i], x_scales[i], x_bf[i][:].rearrange("p c j -> p (c j)"))
+                quantize(x_codes[i], x_scales[i], x_bf[i].rearrange("p c j -> p (c j)"))
             elif kind == "W":
                 buf = stage[staged.index(step) % RING]
                 dst = buf[:].rearrange("p (t m j) -> p m j t", t=PACK, j=PACK)
                 src = w1_raw[i][:].rearrange("p j (m t) -> p m j t", t=PACK)
-                cut = P - W1_VECTOR_SHARE[i]
-                if cut > 0:
-                    nc.scalar.copy(dst[:, 0:cut], src[:, 0:cut])
-                if cut < P:
-                    nc.vector.tensor_copy(dst[:, cut:P], src[:, cut:P])
+                for engine, a, b in shares(W1_ENGINES[i], PACK):
+                    cast(engine, dst[:, :, :, a:b], src[:, :, :, a:b])
             elif kind == "Q":
                 buf = stage[staged.index("W%d" % i) % RING]
                 quantize(w1_codes[i], w1_scales[i], buf[:])
@@ -126,25 +146,32 @@ def tile_moe_pre_mlp_silu_kernel(tc, xT, w1, w2, gate, offs, pos1, pos2, out):
                                         rhs=x_codes[i // 2][:, slots].bitcast(FP8X4),
                                         rhs_scale=x_scales[i // 2][:, slots], start=True, stop=True)
             elif kind == "H":
-                nc.scalar.activation(h_bf[i][:], a_ps[i % A_BANKS][:].rearrange("p t c -> p c t"), SILU)
+                nc.scalar.activation(h_bf[i], a_ps[i % A_BANKS][:].rearrange("p t c -> p c t"), SILU)
             elif kind == "I":
-                quantize(h_codes[i], h_scales[i], h_bf[i][:].rearrange("p c t -> p (c t)"))
+                quantize(h_codes[i], h_scales[i], h_bf[i].rearrange("p c t -> p (c t)"))
             elif kind == "U":
                 buf = stage[staged.index(step) % RING]
-                cast(W2_ENGINES[i],
-                     buf[:, 0:2 * N * PACK].rearrange("p (e c i j) -> p e c j i", e=2, i=4, j=PACK),
-                     w2_raw[i][:].rearrange("p e j (c i) -> p e c j i", i=4))
+                size = len(W2_GROUPS[i])
+                dst = buf[:, 0:size * N * PACK].rearrange("p (e c i j) -> p e c j i", e=size, i=4, j=PACK)
+                src = w2_raw[i][:].rearrange("p e j (c i) -> p e c j i", i=4)
+                if size == 2:
+                    for engine, a, b in shares(W2_ENGINES[i], 2):
+                        cast(engine, dst[:, a:b], src[:, a:b])
+                else:
+                    for engine, a, b in shares(W2_ENGINES[i], N // 4):
+                        cast(engine, dst[:, 0, a:b], src[:, 0, a:b])
             elif kind == "V":
                 buf = stage[staged.index("U%d" % i) % RING]
-                quantize(w2_codes[i], w2_scales[i], buf[:, 0:2 * N * PACK])
+                quantize(w2_codes[i], w2_scales[i], buf[:, 0:len(W2_GROUPS[i]) * N * PACK])
             else:
-                for r in range(2):
+                for r, e in enumerate(W2_GROUPS[i]):
                     cols = slice(r * N, (r + 1) * N)
                     nc.tensor.matmul_mx(out=y_ps[i % Y_BANKS][:, r * C:(r + 1) * C],
                                         lhsT=w2_codes[i][:, cols].bitcast(FP8X4), lhsT_scale=w2_scales[i][:, cols],
-                                        rhs=h_codes[2 * i + r][:].bitcast(FP8X4), rhs_scale=h_scales[2 * i + r][:],
+                                        rhs=h_codes[e][:].bitcast(FP8X4), rhs_scale=h_scales[e][:],
                                         start=True, stop=True)
-                nc.scalar.copy(y_all[:, 2 * i * C:(2 * i + 2) * C], y_ps[i % Y_BANKS][:])
+                nc.scalar.copy(y_all[:, W2_GROUPS[i][0] * C:(W2_GROUPS[i][-1] + 1) * C],
+                               y_ps[i % Y_BANKS][:, 0:len(W2_GROUPS[i]) * C])
 
         pieces = list(zip(OUT_CUTS[:-1], OUT_CUTS[1:]))
         for a, b in pieces:

@@ -6,8 +6,11 @@ K, T, E, C, H, N = 512, 640, 10, 128, 512, 128
 S = E * C
 P = 128
 PACK = 4
+LINE = 4
+PER_COLUMN = 16
+PAIR = 2 * C
 FLOPS = 2 * S * (K * H + H * N)
-BYTES = 4 * (K * T + E * K * H + E * H * N + S + N * T) + 2 * P * (S + 2 * T) // 16
+BYTES = 4 * (K * T + E * K * H + E * H * N + S + N * T) + 2 * P * (S + 2 * T) // PER_COLUMN
 
 F32 = mybir.dt.float32
 BF16 = mybir.dt.bfloat16
@@ -19,15 +22,28 @@ MULT = mybir.AluOpType.mult
 ADD = mybir.AluOpType.add
 SILU = mybir.ActivationFunctionType.Silu
 
-GATHER_CUTS = (0, 256, 512, 768, 1024, 1280)
-W1_ENGINES = "BSSVSSBBVS"
+GATHER_CUTS = (0, 256, 768, 1280)
 W2_GROUPS = ((0, 1), (2, 3), (4, 5), (6, 7), (8,), (9,))
-X_ENGINES = "SBVVB"
-W2_ENGINES = "VBVBVV"
-LOAD_ORDER = "offs g0 x0 x1 x2 g1 a0 g2 x3 g3 a1 b0 g4 a2 a3 a4 a5 a6 a7 a8 pos a9 b1 b2 b3 b4 b5".split()
-STEPS = "W0 G0 G1 W1 X0 W2 G2 Z0 X1 G3 W3 X2 Q0 W4 Q1 Z1 W5 Q2 Q3 H0 H1 G4 W6 I0 H2 H3 Z2 U0 I1 Q4 X3 Q5 V0 Z3 I2 W7 X4 Z4 U1 Q6 W8 U2 Q7 W9 V1 U3 H4 I3 I4 H5 Y0 Q8 Q9 H6 V2 U4 H7 H8 H9 I5 Y1 Y2 V3 I6 U5 I7 V4 I8 Y3 I9 V5 Y4 Y5".split()
 OUT_CUTS = (0, 320, 640)
-REUSE = {"H7":"W9","X2":"W2","H1":"W5","H4":"W9","H0":"W2","H5":"U2","H2":"W5","X4":"W6","H3":"W5","X0":"W0","H9":"U3"}
+
+W1_ENGINES = "SSSBVVSSVS"
+X_ENGINES = "BSBBV"
+W2_ENGINES = "BVVVBV"
+
+LOAD_ORDER = (
+    "offs x0 g0 pos x1 g1 g2 a0 x2 a1 a2 x3 a3 a4 a5 a6 b0 a7 b1 a8 a9 b2 b3 b4 b5"
+).split()
+
+STEPS = (
+    "G0 W0 W1 G1 W2 X0 Z0 W3 X1 X2 Z1 G2 Q0 W4 H0 X3 Q1 Z2 W5 Q2 H1 Q3 W6 U0 X4 I0 H2 Q4 V0 I1 Z3 Q5 Q6 "
+    "U1 H3 I2 I3 W7 H4 U2 H5 W8 V1 I4 Y0 Q7 I5 U3 H6 Z4 V2 I6 Y1 W9 H7 I7 U4 Q8 Q9 H8 V3 U5 Y2 H9 I8 V4 "
+    "Y3 V5 I9 Y4 Y5"
+).split()
+
+REUSE = {
+    "X0": "W1", "X1": "W2", "X3": "W3", "X4": "W6",
+    "H1": "W4", "H3": "W6", "H4": "U1", "H5": "U1", "H7": "W9", "H8": "W9", "H9": "W9",
+}
 RING = 4
 A_BANKS = 4
 Y_BANKS = 3
@@ -39,65 +55,70 @@ def tile_moe_pre_mlp_silu_kernel(tc, xT, w1, w2, gate, offs, pos1, pos2, out):
         held = ctx.enter_context(tc.tile_pool(name="held", bufs=1))
         psum = ctx.enter_context(tc.psum_pool(name="psum", bufs=1))
 
-        offs_sb = held.tile([P, S // 16], U16, name="offs_sb")
-        pos1_sb = held.tile([P, T // 16], U16, name="pos1_sb")
-        pos2_sb = held.tile([P, T // 16], U16, name="pos2_sb")
-        chunks = list(zip(GATHER_CUTS[:-1], GATHER_CUTS[1:]))
+        offs_sb = held.tile([P, S // PER_COLUMN], U16, name="offs_sb")
+        pos1_sb = held.tile([P, T // PER_COLUMN], U16, name="pos1_sb")
+        pos2_sb = held.tile([P, T // PER_COLUMN], U16, name="pos2_sb")
+        runs = list(zip(GATHER_CUTS[:-1], GATHER_CUTS[1:]))
         x_rows = [held.tile([P, T], F32, name="x_rows%d" % j) for j in range(PACK)]
-        gate_sb = [held.tile([P, b - a], F32, name="gate%d" % a) for a, b in chunks]
+        gate_sb = [held.tile([P, hi - lo], F32, name="gate%d" % lo) for lo, hi in runs]
         w1_raw = [held.tile([P, PACK, H], F32, name="w1_raw%d" % e, align_bytes=64) for e in range(E)]
-        w2_raw = [held.tile([P, len(g), PACK, N], F32, name="w2_raw%d" % g[0], align_bytes=64) for g in W2_GROUPS]
-        x_view = xT.rearrange("(p j) t -> p j t", j=PACK)
+        w2_raw = [held.tile([P, len(group), PACK, N], F32, name="w2_raw%d" % group[0], align_bytes=64)
+                  for group in W2_GROUPS]
 
-        for what in LOAD_ORDER:
-            if what == "offs":
+        for load in LOAD_ORDER:
+            if load == "offs":
                 nc.sync.dma_start(offs_sb[:], offs)
-            elif what == "pos":
+            elif load == "pos":
                 nc.sync.dma_start(pos1_sb[:], pos1)
                 nc.sync.dma_start(pos2_sb[:], pos2)
+            elif load[0] == "x":
+                j = int(load[1])
+                nc.sync.dma_start(x_rows[j][:], xT.rearrange("(p j) t -> p j t", j=PACK)[:, j, :])
+            elif load[0] == "g":
+                lo, hi = runs[int(load[1])]
+                nc.sync.dma_start(gate_sb[int(load[1])][:], gate[0:P, lo:hi])
+            elif load[0] == "a":
+                e = int(load[1])
+                nc.sync.dma_start(w1_raw[e][:], w1[e].rearrange("(p j) c -> p j c", j=PACK))
             else:
-                i = int(what[1])
-                if what[0] == "x":
-                    nc.sync.dma_start(x_rows[i][:], x_view[:, i, :])
-                elif what[0] == "g":
-                    nc.sync.dma_start(gate_sb[i][:], gate[0:P, chunks[i][0]:chunks[i][1]])
-                elif what[0] == "a":
-                    nc.sync.dma_start(w1_raw[i][:], w1[i].rearrange("(p j) c -> p j c", j=PACK))
-                else:
-                    nc.sync.dma_start(w2_raw[i][:].rearrange("p e j n -> p e (j n)"),
-                                      w2[W2_GROUPS[i][0]:W2_GROUPS[i][-1] + 1].rearrange("e (p j) n -> p e (j n)", j=PACK))
+                group = W2_GROUPS[int(load[1])]
+                nc.sync.dma_start(w2_raw[int(load[1])][:].rearrange("p e j n -> p e (j n)"),
+                                  w2[group[0]:group[-1] + 1].rearrange("e (p j) n -> p e (j n)", j=PACK))
 
-        def operand(name, count, width):
-            codes = [held.tile([P, width], U32, name="%s_codes%d" % (name, i), align_bytes=64) for i in range(count)]
-            scales = [held.tile([P, width], U8, name="%s_scales%d" % (name, i), align_bytes=64) for i in range(count)]
+        def mx_operands(name, count, width):
+            codes = [held.tile([P, width], U32, name="%s_codes%d" % (name, n), align_bytes=64) for n in range(count)]
+            scales = [held.tile([P, width], U8, name="%s_scales%d" % (name, n), align_bytes=64) for n in range(count)]
             return codes, scales
 
-        x_codes, x_scales = operand("x", E // 2, 2 * C)
-        w1_codes, w1_scales = operand("w1", E, H)
-        h_codes, h_scales = operand("h", E, C)
-        w2_codes, w2_scales = operand("w2", len(W2_GROUPS), 2 * N)
-        picked = [held.tile([P, PACK, b - a], F32, name="picked%d" % a) for a, b in chunks]
-        used = {}
+        x_codes, x_scales = mx_operands("x", E // 2, PAIR)
+        w1_codes, w1_scales = mx_operands("w1", E, H)
+        h_codes, h_scales = mx_operands("h", E, C)
+        w2_codes, w2_scales = mx_operands("w2", len(W2_GROUPS), 2 * N)
+        picked = [held.tile([P, PACK, hi - lo], F32, name="picked%d" % lo) for lo, hi in runs]
+        taken = {}
 
         def rounded(step, slots):
             if step not in REUSE:
                 return held.tile([P, slots, PACK], BF16, name="bf_" + step, align_bytes=64)[:]
             host = REUSE[step]
             if host[0] == "W":
-                words = w1_raw[int(host[1])][:].rearrange("p j c -> p (j c)")
+                room = w1_raw[int(host[1])][:].rearrange("p j c -> p (j c)")
             else:
-                words = w2_raw[int(host[1])][:].rearrange("p e j n -> p (e j n)")
-            start = used.get(host, 0)
-            used[host] = start + slots * PACK // 2
-            return words[:, start:used[host]].bitcast(BF16).rearrange("p (c j) -> p c j", j=PACK)
+                room = w2_raw[int(host[1])][:].rearrange("p e j n -> p (e j n)")
+            start = taken.get(host, 0)
+            taken[host] = start + slots * PACK // 2
+            return room[:, start:taken[host]].bitcast(BF16).rearrange("p (c j) -> p c j", j=PACK)
 
-        x_bf = [rounded("X%d" % q, 2 * C) for q in range(E // 2)]
+        x_bf = [rounded("X%d" % q, PAIR) for q in range(E // 2)]
         h_bf = [rounded("H%d" % e, C) for e in range(E)]
         stage = [held.tile([P, PACK * H], BF16, name="stage%d" % r, align_bytes=64) for r in range(RING)]
         a_ps = [psum.tile([P, PACK, C], F32, name="a_ps%d" % r) for r in range(A_BANKS)]
-        y_ps = [psum.tile([P, 2 * C], F32, name="y_ps%d" % r) for r in range(Y_BANKS)]
+        y_ps = [psum.tile([P, PAIR], F32, name="y_ps%d" % r) for r in range(Y_BANKS)]
         y_all = held.tile([P, S], F32, name="y_all")
-        staged = [s for s in STEPS if s[0] in "WU"]
+        staged = [step for step in STEPS if step[0] in "WU"]
+
+        def stage_of(step):
+            return stage[staged.index(step) % RING]
 
         def cast(engine, dst, src):
             if engine == "S":
@@ -105,80 +126,93 @@ def tile_moe_pre_mlp_silu_kernel(tc, xT, w1, w2, gate, offs, pos1, pos2, out):
             else:
                 nc.vector.tensor_copy(dst, src)
 
-        def shares(engine, count):
-            if engine == "B":
+        def shares(engines, count):
+            if engines == "B":
                 return [("S", 0, count // 2), ("V", count // 2, count)]
-            return [(engine, 0, count)]
+            return [(engines, 0, count)]
 
         def quantize(codes, scales, src):
             width = src.shape[1] // PACK
             nc.vector.quantize_mx(out=codes[:, 0:width].bitcast(FP8X4), scales=scales[:, 0:width], in_=src)
 
-        for step in STEPS:
-            kind, i = step[0], int(step[1])
-            if kind == "G":
-                a, b = chunks[i]
-                for j in range(PACK):
-                    nc.vector.tensor_tensor(picked[i][:, j, :], x_rows[j][:].indirect(offs_sb[:, a // 16:b // 16]),
-                                            gate_sb[i][:], MULT)
-            elif kind == "X":
-                g = max(n for n, (a, b) in enumerate(chunks) if a <= 2 * C * i)
-                lo = 2 * C * i - chunks[g][0]
-                for engine, a, b in shares(X_ENGINES[i], 2 * C):
-                    cast(engine, x_bf[i][:, a:b, :].rearrange("p (c i) j -> p c j i", i=4),
-                         picked[g][:, :, lo + a:lo + b].rearrange("p j (c i) -> p c j i", i=4))
-            elif kind == "Z":
-                quantize(x_codes[i], x_scales[i], x_bf[i].rearrange("p c j -> p (c j)"))
-            elif kind == "W":
-                buf = stage[staged.index(step) % RING]
-                dst = buf[:].rearrange("p (t m j) -> p m j t", t=PACK, j=PACK)
-                src = w1_raw[i][:].rearrange("p j (m t) -> p m j t", t=PACK)
-                for engine, a, b in shares(W1_ENGINES[i], PACK):
-                    cast(engine, dst[:, :, :, a:b], src[:, :, :, a:b])
-            elif kind == "Q":
-                buf = stage[staged.index("W%d" % i) % RING]
-                quantize(w1_codes[i], w1_scales[i], buf[:])
-                slots = slice((i % 2) * C, (i % 2 + 1) * C)
-                for t in range(PACK):
-                    cols = slice(t * P, (t + 1) * P)
-                    nc.tensor.matmul_mx(out=a_ps[i % A_BANKS][:, t, :], lhsT=w1_codes[i][:, cols].bitcast(FP8X4),
-                                        lhsT_scale=w1_scales[i][:, cols],
-                                        rhs=x_codes[i // 2][:, slots].bitcast(FP8X4),
-                                        rhs_scale=x_scales[i // 2][:, slots], start=True, stop=True)
-            elif kind == "H":
-                nc.scalar.activation(h_bf[i], a_ps[i % A_BANKS][:].rearrange("p t c -> p c t"), SILU)
-            elif kind == "I":
-                quantize(h_codes[i], h_scales[i], h_bf[i].rearrange("p c t -> p (c t)"))
-            elif kind == "U":
-                buf = stage[staged.index(step) % RING]
-                size = len(W2_GROUPS[i])
-                dst = buf[:, 0:size * N * PACK].rearrange("p (e c i j) -> p e c j i", e=size, i=4, j=PACK)
-                src = w2_raw[i][:].rearrange("p e j (c i) -> p e c j i", i=4)
-                if size == 2:
-                    for engine, a, b in shares(W2_ENGINES[i], 2):
-                        cast(engine, dst[:, a:b], src[:, a:b])
-                else:
-                    for engine, a, b in shares(W2_ENGINES[i], N // 4):
-                        cast(engine, dst[:, 0, a:b], src[:, 0, a:b])
-            elif kind == "V":
-                buf = stage[staged.index("U%d" % i) % RING]
-                quantize(w2_codes[i], w2_scales[i], buf[:, 0:len(W2_GROUPS[i]) * N * PACK])
-            else:
-                for r, e in enumerate(W2_GROUPS[i]):
-                    cols = slice(r * N, (r + 1) * N)
-                    nc.tensor.matmul_mx(out=y_ps[i % Y_BANKS][:, r * C:(r + 1) * C],
-                                        lhsT=w2_codes[i][:, cols].bitcast(FP8X4), lhsT_scale=w2_scales[i][:, cols],
-                                        rhs=h_codes[e][:].bitcast(FP8X4), rhs_scale=h_scales[e][:],
-                                        start=True, stop=True)
-                nc.scalar.copy(y_all[:, W2_GROUPS[i][0] * C:(W2_GROUPS[i][-1] + 1) * C],
-                               y_ps[i % Y_BANKS][:, 0:len(W2_GROUPS[i]) * C])
+        def gather_x(n):
+            lo, hi = runs[n]
+            for j in range(PACK):
+                tokens = x_rows[j][:].indirect(offs_sb[:, lo // PER_COLUMN:hi // PER_COLUMN])
+                nc.vector.tensor_tensor(picked[n][:, j, :], tokens, gate_sb[n][:], MULT)
 
-        pieces = list(zip(OUT_CUTS[:-1], OUT_CUTS[1:]))
-        for a, b in pieces:
-            first = held.tile([P, b - a], F32, name="first%d" % a)
-            second = held.tile([P, b - a], F32, name="second%d" % a)
-            total = held.tile([P, b - a], F32, name="total%d" % a)
-            nc.vector.tensor_copy(first[:], y_all[:].indirect(pos1_sb[:, a // 16:b // 16]))
-            nc.vector.tensor_copy(second[:], y_all[:].indirect(pos2_sb[:, a // 16:b // 16]))
-            nc.vector.tensor_tensor(total[:], first[:], second[:], ADD)
-            nc.sync.dma_start(out[:, a:b], total[:])
+        def round_x(q):
+            n = max(m for m, (lo, hi) in enumerate(runs) if lo <= PAIR * q)
+            base = PAIR * q - runs[n][0]
+            for engine, lo, hi in shares(X_ENGINES[q], PAIR):
+                cast(engine, x_bf[q][:, lo:hi, :].rearrange("p (c i) j -> p c j i", i=LINE),
+                     picked[n][:, :, base + lo:base + hi].rearrange("p j (c i) -> p c j i", i=LINE))
+
+        def quantize_x(q):
+            quantize(x_codes[q], x_scales[q], x_bf[q].rearrange("p c j -> p (c j)"))
+
+        def round_w1(e):
+            buf = stage_of("W%d" % e)
+            if W1_ENGINES[e] == "S":
+                nc.scalar.copy(buf[:].rearrange("p (u v m j) -> p u m j v", u=2, v=2, j=PACK),
+                               w1_raw[e][:].rearrange("p j (m u v) -> p u m j v", u=2, v=2))
+            else:
+                dst = buf[:].rearrange("p (t m j) -> p m j t", t=PACK, j=PACK)
+                src = w1_raw[e][:].rearrange("p j (m t) -> p m j t", t=PACK)
+                cast("S" if W1_ENGINES[e] == "B" else "V", dst[:, :, :, 0:2], src[:, :, :, 0:2])
+                cast("V", dst[:, :, :, 2:4], src[:, :, :, 2:4])
+
+        def first_product(e):
+            quantize(w1_codes[e], w1_scales[e], stage_of("W%d" % e)[:])
+            slots = slice((e % 2) * C, (e % 2 + 1) * C)
+            for t in range(PACK):
+                cols = slice(t * P, (t + 1) * P)
+                nc.tensor.matmul_mx(out=a_ps[e % A_BANKS][:, t, :], lhsT=w1_codes[e][:, cols].bitcast(FP8X4),
+                                    lhsT_scale=w1_scales[e][:, cols],
+                                    rhs=x_codes[e // 2][:, slots].bitcast(FP8X4),
+                                    rhs_scale=x_scales[e // 2][:, slots], start=True, stop=True)
+
+        def activate(e):
+            nc.scalar.activation(h_bf[e], a_ps[e % A_BANKS][:].rearrange("p t c -> p c t"), SILU)
+
+        def quantize_h(e):
+            quantize(h_codes[e], h_scales[e], h_bf[e].rearrange("p c t -> p (c t)"))
+
+        def round_w2(n):
+            size = len(W2_GROUPS[n])
+            dst = stage_of("U%d" % n)[:, 0:size * N * PACK].rearrange("p (e c i j) -> p e c j i", e=size, i=LINE, j=PACK)
+            src = w2_raw[n][:].rearrange("p e j (c i) -> p e c j i", i=LINE)
+            if size == 1:
+                dst, src = dst[:, 0], src[:, 0]
+            for engine, lo, hi in shares(W2_ENGINES[n], dst.shape[1]):
+                cast(engine, dst[:, lo:hi], src[:, lo:hi])
+
+        def quantize_w2(n):
+            quantize(w2_codes[n], w2_scales[n], stage_of("U%d" % n)[:, 0:len(W2_GROUPS[n]) * N * PACK])
+
+        def second_product(n):
+            group = W2_GROUPS[n]
+            bank = y_ps[n % Y_BANKS]
+            for r, e in enumerate(group):
+                cols = slice(r * N, (r + 1) * N)
+                nc.tensor.matmul_mx(out=bank[:, r * C:(r + 1) * C], lhsT=w2_codes[n][:, cols].bitcast(FP8X4),
+                                    lhsT_scale=w2_scales[n][:, cols], rhs=h_codes[e][:].bitcast(FP8X4),
+                                    rhs_scale=h_scales[e][:], start=True, stop=True)
+            nc.scalar.copy(y_all[:, group[0] * C:(group[-1] + 1) * C], bank[:, 0:len(group) * C])
+
+        work = {"G": gather_x, "X": round_x, "Z": quantize_x, "W": round_w1, "Q": first_product, "H": activate,
+                "I": quantize_h, "U": round_w2, "V": quantize_w2, "Y": second_product}
+        for step in STEPS:
+            work[step[0]](int(step[1]))
+
+        halves = list(zip(OUT_CUTS[:-1], OUT_CUTS[1:]))
+        first = [held.tile([P, hi - lo], F32, name="first%d" % lo) for lo, hi in halves]
+        second = [held.tile([P, hi - lo], F32, name="second%d" % lo) for lo, hi in halves]
+        total = [held.tile([P, hi - lo], F32, name="total%d" % lo) for lo, hi in halves]
+        for n, (lo, hi) in enumerate(halves):
+            columns = slice(lo // PER_COLUMN, hi // PER_COLUMN)
+            nc.vector.tensor_copy(first[n][:], y_all[:].indirect(pos1_sb[:, columns]))
+            nc.vector.tensor_copy(second[n][:], y_all[:].indirect(pos2_sb[:, columns]))
+        for n, (lo, hi) in enumerate(halves):
+            nc.vector.tensor_tensor(total[n][:], first[n][:], second[n][:], ADD)
+            nc.sync.dma_start(out[:, lo:hi], total[n][:])

@@ -8,7 +8,8 @@ P = 128
 PACK = 4
 LINE = 4
 PER_COLUMN = 16
-PAIR = 2 * C
+QUADRANT = 32
+BANK = 512
 FLOPS = 2 * S * (K * H + H * N)
 BYTES = 4 * (K * T + E * K * H + E * H * N + S + N * T) + 2 * P * (S + 2 * T) // PER_COLUMN
 
@@ -22,31 +23,16 @@ MULT = mybir.AluOpType.mult
 ADD = mybir.AluOpType.add
 SILU = mybir.ActivationFunctionType.Silu
 
-GATHER_CUTS = (0, 256, 768, 1280)
+RUN_CUTS = (0, 256, 768, 1280)
+FIRST_HOST = 4
+X_HOST = {1: 3}
 W2_GROUPS = ((0, 1), (2, 3), (4, 5), (6, 7), (8,), (9,))
+W2_AFTER = (4, 5, 7, 9, 9, 9)
+Y_GROUPS = ((0, 1, 2, 3), (4, 5, 6, 7), (8,), (9,))
+SHARED_FROM = 5
 OUT_CUTS = (0, 320, 640)
-
-W1_ENGINES = "SSSBVVSSVS"
-X_ENGINES = "BSBBV"
-W2_ENGINES = "BVVVBV"
-
-LOAD_ORDER = (
-    "offs x0 g0 pos x1 g1 g2 a0 x2 a1 a2 x3 a3 a4 a5 a6 b0 a7 b1 a8 a9 b2 b3 b4 b5"
-).split()
-
-STEPS = (
-    "G0 W0 W1 G1 W2 X0 Z0 W3 X1 X2 Z1 G2 Q0 W4 H0 X3 Q1 Z2 W5 Q2 H1 Q3 W6 U0 X4 I0 H2 Q4 V0 I1 Z3 Q5 Q6 "
-    "U1 H3 I2 I3 W7 H4 U2 H5 W8 V1 I4 Y0 Q7 I5 U3 H6 Z4 V2 I6 Y1 W9 H7 I7 U4 Q8 Q9 H8 V3 U5 Y2 H9 I8 V4 "
-    "Y3 V5 I9 Y4 Y5"
-).split()
-
-REUSE = {
-    "X0": "W1", "X1": "W2", "X3": "W3", "X4": "W6",
-    "H1": "W4", "H3": "W6", "H4": "U1", "H5": "U1", "H7": "W9", "H8": "W9", "H9": "W9",
-}
 RING = 4
 A_BANKS = 4
-Y_BANKS = 3
 
 
 def tile_moe_pre_mlp_silu_kernel(tc, xT, w1, w2, gate, offs, pos1, pos2, out):
@@ -58,161 +44,221 @@ def tile_moe_pre_mlp_silu_kernel(tc, xT, w1, w2, gate, offs, pos1, pos2, out):
         offs_sb = held.tile([P, S // PER_COLUMN], U16, name="offs_sb")
         pos1_sb = held.tile([P, T // PER_COLUMN], U16, name="pos1_sb")
         pos2_sb = held.tile([P, T // PER_COLUMN], U16, name="pos2_sb")
-        runs = list(zip(GATHER_CUTS[:-1], GATHER_CUTS[1:]))
+        runs = list(zip(RUN_CUTS[:-1], RUN_CUTS[1:]))
         x_rows = [held.tile([P, T], F32, name="x_rows%d" % j) for j in range(PACK)]
         gate_sb = [held.tile([P, hi - lo], F32, name="gate%d" % lo) for lo, hi in runs]
-        w1_raw = [held.tile([P, PACK, H], F32, name="w1_raw%d" % e, align_bytes=64) for e in range(E)]
+        gate_square = held.tile([P, P], F32, name="gate_square")
+        gate_columns = held.tile([P, E], F32, name="gate_columns")
+        ones = held.tile([P, P], F32, name="ones")
+        column = held.tile([P, P], F32, name="column", align_bytes=64)
+        row = held.tile([P, P], F32, name="row", align_bytes=64)
+        identity = held.tile([P, P], F32, name="identity")
+        w1_raw = [held.tile([P, PACK, H], F32, name="w1_raw%d" % e, align_bytes=64) for e in range(E - 1)]
+        w1_raw.append(held.tile([P, PACK, H], F32, name="w1_last", tag="last", align_bytes=64))
         w2_raw = [held.tile([P, len(group), PACK, N], F32, name="w2_raw%d" % group[0], align_bytes=64)
                   for group in W2_GROUPS]
 
-        for load in LOAD_ORDER:
-            if load == "offs":
-                nc.sync.dma_start(offs_sb[:], offs)
-            elif load == "pos":
-                nc.sync.dma_start(pos1_sb[:], pos1)
-                nc.sync.dma_start(pos2_sb[:], pos2)
-            elif load[0] == "x":
-                j = int(load[1])
-                nc.sync.dma_start(x_rows[j][:], xT.rearrange("(p j) t -> p j t", j=PACK)[:, j, :])
-            elif load[0] == "g":
-                lo, hi = runs[int(load[1])]
-                nc.sync.dma_start(gate_sb[int(load[1])][:], gate[0:P, lo:hi])
-            elif load[0] == "a":
-                e = int(load[1])
-                nc.sync.dma_start(w1_raw[e][:], w1[e].rearrange("(p j) c -> p j c", j=PACK))
-            else:
-                group = W2_GROUPS[int(load[1])]
-                nc.sync.dma_start(w2_raw[int(load[1])][:].rearrange("p e j n -> p e (j n)"),
-                                  w2[group[0]:group[-1] + 1].rearrange("e (p j) n -> p e (j n)", j=PACK))
+        def load_x(j):
+            nc.sync.dma_start(x_rows[j][:], xT.rearrange("(p j) t -> p j t", j=PACK)[:, j, :])
 
-        def mx_operands(name, count, width):
-            codes = [held.tile([P, width], U32, name="%s_codes%d" % (name, n), align_bytes=64) for n in range(count)]
-            scales = [held.tile([P, width], U8, name="%s_scales%d" % (name, n), align_bytes=64) for n in range(count)]
+        def load_w1(e):
+            nc.sync.dma_start(w1_raw[e][:], w1[e].rearrange("(p j) c -> p j c", j=PACK))
+
+        def load_w2(n):
+            group = W2_GROUPS[n]
+            nc.sync.dma_start(w2_raw[n][:].rearrange("p e j n -> p e (j n)"),
+                              w2[group[0]:group[-1] + 1].rearrange("e (p j) n -> p e (j n)", j=PACK))
+
+        def w2_after(e):
+            return [n for n, group in enumerate(W2_GROUPS) if W2_AFTER[n] == e]
+
+        nc.sync.dma_start(gate_square[:], gate.rearrange("k (e c) -> (k e) c", c=C)[0:P, :])
+        nc.sync.dma_start(offs_sb[:], offs)
+        load_x(0)
+        load_w1(0)
+        load_x(1)
+        load_w1(1)
+        load_x(2)
+        load_x(3)
+        nc.sync.dma_start(pos1_sb[:], pos1)
+        nc.sync.dma_start(pos2_sb[:], pos2)
+        for e in range(2, E):
+            load_w1(e)
+            for n in w2_after(e):
+                load_w2(n)
+
+        def mx_operands(name, widths):
+            codes = [held.tile([P, w], U32, name="%s_codes%d" % (name, n), align_bytes=64)
+                     for n, w in enumerate(widths)]
+            scales = [held.tile([P, w], U8, name="%s_scales%d" % (name, n), align_bytes=64)
+                      for n, w in enumerate(widths)]
             return codes, scales
 
-        x_codes, x_scales = mx_operands("x", E // 2, PAIR)
-        w1_codes, w1_scales = mx_operands("w1", E, H)
-        h_codes, h_scales = mx_operands("h", E, C)
-        w2_codes, w2_scales = mx_operands("w2", len(W2_GROUPS), 2 * N)
+        x_codes, x_scales = mx_operands("x", [hi - lo for lo, hi in runs])
+        w1_codes, w1_scales = mx_operands("w1", [H] * E)
+        h_codes, h_scales = mx_operands("h", [C] * E)
+        w2_codes, w2_scales = mx_operands("w2", [len(group) * N for group in W2_GROUPS])
+
+        def freed(e, start, words):
+            return w1_raw[e][:].rearrange("p j c -> p (j c)")[:, start:start + words]
+
         picked = [held.tile([P, PACK, hi - lo], F32, name="picked%d" % lo) for lo, hi in runs]
-        taken = {}
-
-        def rounded(step, slots):
-            if step not in REUSE:
-                return held.tile([P, slots, PACK], BF16, name="bf_" + step, align_bytes=64)[:]
-            host = REUSE[step]
-            if host[0] == "W":
-                room = w1_raw[int(host[1])][:].rearrange("p j c -> p (j c)")
-            else:
-                room = w2_raw[int(host[1])][:].rearrange("p e j n -> p (e j n)")
-            start = taken.get(host, 0)
-            taken[host] = start + slots * PACK // 2
-            return room[:, start:taken[host]].bitcast(BF16).rearrange("p (c j) -> p c j", j=PACK)
-
-        x_bf = [rounded("X%d" % q, PAIR) for q in range(E // 2)]
-        h_bf = [rounded("H%d" % e, C) for e in range(E)]
-        stage = [held.tile([P, PACK * H], BF16, name="stage%d" % r, align_bytes=64) for r in range(RING)]
+        x_bf = [freed(X_HOST[n], 2 * H, (hi - lo) * PACK // 2).bitcast(BF16) if n in X_HOST else
+                held.tile([P, (hi - lo) * PACK], BF16, name="x_bf%d" % lo, align_bytes=64)[:]
+                for n, (lo, hi) in enumerate(runs)]
+        h_words = C * PACK // 2
+        h_bf = [freed(max(e + 1, FIRST_HOST), e % PACK * h_words, h_words).bitcast(BF16) for e in range(E - 1)]
+        h_bf.append(held.tile([P, C * PACK], BF16, name="h_last", align_bytes=64)[:])
+        w1_bf = [held.tile([P, PACK * H], BF16, name="w1_bf%d" % r, align_bytes=64) for r in range(RING)]
+        w2_bf = [held.tile([P, len(group) * PACK * N], BF16, name="w2_bf%d" % group[0], align_bytes=64)
+                 for group in W2_GROUPS]
         a_ps = [psum.tile([P, PACK, C], F32, name="a_ps%d" % r) for r in range(A_BANKS)]
-        y_ps = [psum.tile([P, PAIR], F32, name="y_ps%d" % r) for r in range(Y_BANKS)]
-        y_all = held.tile([P, S], F32, name="y_all")
-        staged = [step for step in STEPS if step[0] in "WU"]
+        y_ps = [psum.tile([P, BANK], F32, name="y_ps%d" % r) for r in range(len(Y_GROUPS))]
 
-        def stage_of(step):
-            return stage[staged.index(step) % RING]
+        def quantize(codes, scales, src):
+            nc.vector.quantize_mx(out=codes[:].bitcast(FP8X4), scales=scales[:], in_=src)
 
-        def cast(engine, dst, src):
-            if engine == "S":
+        def spread_gate():
+            nc.vector.memset(ones[:], 1.0)
+            nc.vector.memset(identity[:], 0.0)
+            nc.vector.tensor_tensor_scan(column[:], ones[:], ones[:], 0.0, MULT, ADD)
+            nc.vector.transpose(row[:], column[:])
+            for q in range(0, P, QUADRANT):
+                part = slice(q, q + QUADRANT)
+                nc.vector.tensor_tensor(identity[part, part], column[part, part], row[part, part],
+                                        mybir.AluOpType.is_equal)
+            turned = y_ps[-1]
+            nc.tensor.transpose(turned[:, 0:P], gate_square[:], identity[:])
+            nc.vector.tensor_copy(gate_columns[:], turned[:, 0:E])
+            for n, (lo, hi) in enumerate(runs):
+                bank = y_ps[n]
+                for e in range(lo // C, hi // C):
+                    nc.tensor.transpose(bank[:, e * C - lo:(e + 1) * C - lo],
+                                        gate_columns[:, e:e + 1].to_broadcast([P, P]), identity[:])
+                nc.scalar.copy(gate_sb[n][:], bank[:, 0:hi - lo])
+
+        def gather_x(n, j):
+            lo, hi = runs[n]
+            tokens = x_rows[j][:].indirect(offs_sb[:, lo // PER_COLUMN:hi // PER_COLUMN])
+            nc.vector.tensor_tensor(picked[n][:, j, :], tokens, gate_sb[n][:], MULT)
+
+        def round_x(n):
+            dst = x_bf[n].rearrange("p (c i j) -> p c j i", i=LINE, j=PACK)
+            src = picked[n][:].rearrange("p j (c i) -> p c j i", i=LINE)
+            if n in X_HOST:
                 nc.scalar.copy(dst, src)
             else:
                 nc.vector.tensor_copy(dst, src)
 
-        def shares(engines, count):
-            if engines == "B":
-                return [("S", 0, count // 2), ("V", count // 2, count)]
-            return [(engines, 0, count)]
-
-        def quantize(codes, scales, src):
-            width = src.shape[1] // PACK
-            nc.vector.quantize_mx(out=codes[:, 0:width].bitcast(FP8X4), scales=scales[:, 0:width], in_=src)
-
-        def gather_x(n):
-            lo, hi = runs[n]
-            for j in range(PACK):
-                tokens = x_rows[j][:].indirect(offs_sb[:, lo // PER_COLUMN:hi // PER_COLUMN])
-                nc.vector.tensor_tensor(picked[n][:, j, :], tokens, gate_sb[n][:], MULT)
-
-        def round_x(q):
-            n = max(m for m, (lo, hi) in enumerate(runs) if lo <= PAIR * q)
-            base = PAIR * q - runs[n][0]
-            for engine, lo, hi in shares(X_ENGINES[q], PAIR):
-                cast(engine, x_bf[q][:, lo:hi, :].rearrange("p (c i) j -> p c j i", i=LINE),
-                     picked[n][:, :, base + lo:base + hi].rearrange("p j (c i) -> p c j i", i=LINE))
-
-        def quantize_x(q):
-            quantize(x_codes[q], x_scales[q], x_bf[q].rearrange("p c j -> p (c j)"))
+        def quantize_x(n):
+            quantize(x_codes[n], x_scales[n], x_bf[n])
 
         def round_w1(e):
-            buf = stage_of("W%d" % e)
-            if W1_ENGINES[e] == "S":
+            buf = w1_bf[e % RING]
+            if e < SHARED_FROM:
                 nc.scalar.copy(buf[:].rearrange("p (u v m j) -> p u m j v", u=2, v=2, j=PACK),
                                w1_raw[e][:].rearrange("p j (m u v) -> p u m j v", u=2, v=2))
             else:
                 dst = buf[:].rearrange("p (t m j) -> p m j t", t=PACK, j=PACK)
                 src = w1_raw[e][:].rearrange("p j (m t) -> p m j t", t=PACK)
-                cast("S" if W1_ENGINES[e] == "B" else "V", dst[:, :, :, 0:2], src[:, :, :, 0:2])
-                cast("V", dst[:, :, :, 2:4], src[:, :, :, 2:4])
+                nc.scalar.copy(dst[:, :, :, 0:2], src[:, :, :, 0:2])
+                nc.vector.tensor_copy(dst[:, :, :, 2:4], src[:, :, :, 2:4])
+
+        def quantize_w1(e):
+            quantize(w1_codes[e], w1_scales[e], w1_bf[e % RING][:])
+
+        def run_of(e):
+            return max(m for m, (lo, hi) in enumerate(runs) if lo <= e * C)
 
         def first_product(e):
-            quantize(w1_codes[e], w1_scales[e], stage_of("W%d" % e)[:])
-            slots = slice((e % 2) * C, (e % 2 + 1) * C)
+            n = run_of(e)
+            slots = slice(e * C - runs[n][0], (e + 1) * C - runs[n][0])
             for t in range(PACK):
                 cols = slice(t * P, (t + 1) * P)
                 nc.tensor.matmul_mx(out=a_ps[e % A_BANKS][:, t, :], lhsT=w1_codes[e][:, cols].bitcast(FP8X4),
                                     lhsT_scale=w1_scales[e][:, cols],
-                                    rhs=x_codes[e // 2][:, slots].bitcast(FP8X4),
-                                    rhs_scale=x_scales[e // 2][:, slots], start=True, stop=True)
+                                    rhs=x_codes[n][:, slots].bitcast(FP8X4),
+                                    rhs_scale=x_scales[n][:, slots], start=True, stop=True)
 
         def activate(e):
-            nc.scalar.activation(h_bf[e], a_ps[e % A_BANKS][:].rearrange("p t c -> p c t"), SILU)
+            nc.scalar.activation(h_bf[e].rearrange("p (c t) -> p c t", t=PACK),
+                                 a_ps[e % A_BANKS][:].rearrange("p t c -> p c t"), SILU)
 
         def quantize_h(e):
-            quantize(h_codes[e], h_scales[e], h_bf[e].rearrange("p c t -> p (c t)"))
+            quantize(h_codes[e], h_scales[e], h_bf[e])
 
         def round_w2(n):
             size = len(W2_GROUPS[n])
-            dst = stage_of("U%d" % n)[:, 0:size * N * PACK].rearrange("p (e c i j) -> p e c j i", e=size, i=LINE, j=PACK)
-            src = w2_raw[n][:].rearrange("p e j (c i) -> p e c j i", i=LINE)
-            if size == 1:
-                dst, src = dst[:, 0], src[:, 0]
-            for engine, lo, hi in shares(W2_ENGINES[n], dst.shape[1]):
-                cast(engine, dst[:, lo:hi], src[:, lo:hi])
+            nc.vector.tensor_copy(w2_bf[n][:].rearrange("p (e c i j) -> p e c j i", e=size, i=LINE, j=PACK),
+                                  w2_raw[n][:].rearrange("p e j (c i) -> p e c j i", i=LINE))
 
         def quantize_w2(n):
-            quantize(w2_codes[n], w2_scales[n], stage_of("U%d" % n)[:, 0:len(W2_GROUPS[n]) * N * PACK])
+            quantize(w2_codes[n], w2_scales[n], w2_bf[n][:])
 
         def second_product(n):
-            group = W2_GROUPS[n]
-            bank = y_ps[n % Y_BANKS]
-            for r, e in enumerate(group):
+            for r, e in enumerate(W2_GROUPS[n]):
+                b = [m for m, group in enumerate(Y_GROUPS) if e in group][0]
+                first_e = Y_GROUPS[b][0]
                 cols = slice(r * N, (r + 1) * N)
-                nc.tensor.matmul_mx(out=bank[:, r * C:(r + 1) * C], lhsT=w2_codes[n][:, cols].bitcast(FP8X4),
-                                    lhsT_scale=w2_scales[n][:, cols], rhs=h_codes[e][:].bitcast(FP8X4),
-                                    rhs_scale=h_scales[e][:], start=True, stop=True)
-            nc.scalar.copy(y_all[:, group[0] * C:(group[-1] + 1) * C], bank[:, 0:len(group) * C])
+                nc.tensor.matmul_mx(out=y_ps[b][:, (e - first_e) * C:(e - first_e + 1) * C],
+                                    lhsT=w2_codes[n][:, cols].bitcast(FP8X4), lhsT_scale=w2_scales[n][:, cols],
+                                    rhs=h_codes[e][:].bitcast(FP8X4), rhs_scale=h_scales[e][:],
+                                    start=True, stop=True)
 
-        work = {"G": gather_x, "X": round_x, "Z": quantize_x, "W": round_w1, "Q": first_product, "H": activate,
-                "I": quantize_h, "U": round_w2, "V": quantize_w2, "Y": second_product}
-        for step in STEPS:
-            work[step[0]](int(step[1]))
+        spread_gate()
+        for j in range(PACK - 1):
+            for n in range(len(runs)):
+                gather_x(n, j)
+        for n in range(len(runs)):
+            gather_x(n, PACK - 1)
+            if n not in X_HOST:
+                round_x(n)
+                quantize_x(n)
+        waiting = []
+        for e in range(E):
+            round_w1(e)
+            quantize_w1(e)
+            for n in X_HOST:
+                if X_HOST[n] == e:
+                    round_x(n)
+                    quantize_x(n)
+            waiting.append(e)
+            ready = [d for d in range(E - 1) if max(d + 1, FIRST_HOST) == e]
+            for d in [d for d in waiting if X_HOST.get(run_of(d), 0) <= e and d < e]:
+                first_product(d)
+                waiting.remove(d)
+            for d in ready:
+                activate(d)
+            for d in [d for d in waiting if X_HOST.get(run_of(d), 0) <= e]:
+                first_product(d)
+                waiting.remove(d)
+            groups = w2_after(e) if e < E - 1 else []
+            for n in groups:
+                round_w2(n)
+            for d in ready:
+                quantize_h(d)
+            for n in groups:
+                quantize_w2(n)
+                second_product(n)
+        activate(E - 1)
+        tail = w2_after(E - 1)
+        round_w2(tail[0])
+        quantize_h(E - 1)
+        for n in tail:
+            if n + 1 in tail:
+                round_w2(n + 1)
+            quantize_w2(n)
+            second_product(n)
+        y_all = held.tile([P, S], F32, name="y_all", tag="last", align_bytes=64)
+        for b, group in enumerate(Y_GROUPS):
+            nc.scalar.copy(y_all[:, group[0] * C:(group[-1] + 1) * C], y_ps[b][:, 0:len(group) * C])
 
         halves = list(zip(OUT_CUTS[:-1], OUT_CUTS[1:]))
         first = [held.tile([P, hi - lo], F32, name="first%d" % lo) for lo, hi in halves]
-        second = [held.tile([P, hi - lo], F32, name="second%d" % lo) for lo, hi in halves]
         total = [held.tile([P, hi - lo], F32, name="total%d" % lo) for lo, hi in halves]
         for n, (lo, hi) in enumerate(halves):
-            columns = slice(lo // PER_COLUMN, hi // PER_COLUMN)
-            nc.vector.tensor_copy(first[n][:], y_all[:].indirect(pos1_sb[:, columns]))
-            nc.vector.tensor_copy(second[n][:], y_all[:].indirect(pos2_sb[:, columns]))
+            nc.vector.tensor_copy(first[n][:], y_all[:].indirect(pos1_sb[:, lo // PER_COLUMN:hi // PER_COLUMN]))
         for n, (lo, hi) in enumerate(halves):
-            nc.vector.tensor_tensor(total[n][:], first[n][:], second[n][:], ADD)
+            nc.vector.tensor_tensor(total[n][:], y_all[:].indirect(pos2_sb[:, lo // PER_COLUMN:hi // PER_COLUMN]),
+                                    first[n][:], ADD)
             nc.sync.dma_start(out[:, lo:hi], total[n][:])

@@ -4,6 +4,7 @@ import concourse.mybir as mybir
 
 K, T, E, C, H, N = 512, 640, 10, 128, 512, 128
 S = E * C
+PAIRS = E // 2
 P = 128
 PACK = 4
 LINE = 4
@@ -25,13 +26,18 @@ SILU = mybir.ActivationFunctionType.Silu
 
 RUN_CUTS = (0, 256, 768, 1280)
 FIRST_HOST = 4
-X_HOST = {1: 3}
+X_HOST = {2: 4}
 W2_GROUPS = ((0, 1), (2, 3), (4, 5), (6, 7), (8,), (9,))
-W2_AFTER = (4, 5, 7, 9, 9, 9)
+W2_AFTER = (4, 6, 9, 9, 9, 9)
 Y_GROUPS = ((0, 1, 2, 3), (4, 5, 6, 7), (8,), (9,))
-SHARED_FROM = 5
+ON_VECTOR = (5, 7, 9)
 OUT_CUTS = (0, 320, 640)
-RING = 4
+X_AFTER = (1, 2)
+POS_AFTER = 1
+W2_ON_SCALAR = (3,)
+SINGLY_FROM = 8
+Y_AFTER = 7
+RING = 2
 A_BANKS = 4
 
 
@@ -53,8 +59,8 @@ def tile_moe_pre_mlp_silu_kernel(tc, xT, w1, w2, gate, offs, pos1, pos2, out):
         column = held.tile([P, P], F32, name="column", align_bytes=64)
         row = held.tile([P, P], F32, name="row", align_bytes=64)
         identity = held.tile([P, P], F32, name="identity")
-        w1_raw = [held.tile([P, PACK, H], F32, name="w1_raw%d" % e, align_bytes=64) for e in range(E - 1)]
-        w1_raw.append(held.tile([P, PACK, H], F32, name="w1_last", tag="last", align_bytes=64))
+        w1_raw = [held.tile([P, PACK, H], F32, name="w1_raw%d" % e, tag="w1_raw%d" % e, align_bytes=64)
+                  for e in range(E)]
         w2_raw = [held.tile([P, len(group), PACK, N], F32, name="w2_raw%d" % group[0], align_bytes=64)
                   for group in W2_GROUPS]
 
@@ -75,15 +81,16 @@ def tile_moe_pre_mlp_silu_kernel(tc, xT, w1, w2, gate, offs, pos1, pos2, out):
         nc.sync.dma_start(gate_square[:], gate.rearrange("k (e c) -> (k e) c", c=C)[0:P, :])
         nc.sync.dma_start(offs_sb[:], offs)
         load_x(0)
-        load_w1(0)
+        nc.sync.dma_start(gate_sb[0][:], gate[0:P, runs[0][0]:runs[0][1]])
         load_x(1)
-        load_w1(1)
-        load_x(2)
-        load_x(3)
-        nc.sync.dma_start(pos1_sb[:], pos1)
-        nc.sync.dma_start(pos2_sb[:], pos2)
-        for e in range(2, E):
+        for e in range(E):
             load_w1(e)
+            for j in range(2, PACK):
+                if X_AFTER[j - 2] == e:
+                    load_x(j)
+            if e == POS_AFTER:
+                nc.sync.dma_start(pos1_sb[:], pos1)
+                nc.sync.dma_start(pos2_sb[:], pos2)
             for n in w2_after(e):
                 load_w2(n)
 
@@ -95,9 +102,13 @@ def tile_moe_pre_mlp_silu_kernel(tc, xT, w1, w2, gate, offs, pos1, pos2, out):
             return codes, scales
 
         x_codes, x_scales = mx_operands("x", [hi - lo for lo, hi in runs])
-        w1_codes, w1_scales = mx_operands("w1", [H] * E)
-        h_codes, h_scales = mx_operands("h", [C] * E)
+        w1_codes, w1_scales = mx_operands("w1", [2 * H] * (PAIRS - 1))
+        w1_scales.append(held.tile([P, 2 * H], U8, name="last_scales", align_bytes=64))
+        h_codes, h_scales = mx_operands("h", [2 * C] * PAIRS)
         w2_codes, w2_scales = mx_operands("w2", [len(group) * N for group in W2_GROUPS])
+
+        def host_of(q):
+            return max(2 * q + 2, FIRST_HOST)
 
         def freed(e, start, words):
             return w1_raw[e][:].rearrange("p j c -> p (j c)")[:, start:start + words]
@@ -107,16 +118,20 @@ def tile_moe_pre_mlp_silu_kernel(tc, xT, w1, w2, gate, offs, pos1, pos2, out):
                 held.tile([P, (hi - lo) * PACK], BF16, name="x_bf%d" % lo, align_bytes=64)[:]
                 for n, (lo, hi) in enumerate(runs)]
         h_words = C * PACK // 2
-        h_bf = [freed(max(e + 1, FIRST_HOST), e % PACK * h_words, h_words).bitcast(BF16) for e in range(E - 1)]
-        h_bf.append(held.tile([P, C * PACK], BF16, name="h_last", align_bytes=64)[:])
-        w1_bf = [held.tile([P, PACK * H], BF16, name="w1_bf%d" % r, align_bytes=64) for r in range(RING)]
-        w2_bf = [held.tile([P, len(group) * PACK * N], BF16, name="w2_bf%d" % group[0], align_bytes=64)
-                 for group in W2_GROUPS]
+        h_bf = [freed(host_of(q), q % 2 * 2 * h_words, 2 * h_words).bitcast(BF16) for q in range(PAIRS - 1)]
+        h_bf.append(held.tile([P, 2 * C * PACK], BF16, name="h_last", align_bytes=64)[:])
+        w1_bf = [held.tile([P, 2 * PACK * H], BF16, name="w1_bf%d" % r, tag="w1_bf%d" % r, align_bytes=64)
+                 for r in range(RING)]
+        w2_bf = [held.tile([P, len(group) * PACK * N], BF16, name="w2_bf%d" % n, align_bytes=64)[:]
+                 for n, group in enumerate(W2_GROUPS)]
         a_ps = [psum.tile([P, PACK, C], F32, name="a_ps%d" % r) for r in range(A_BANKS)]
         y_ps = [psum.tile([P, BANK], F32, name="y_ps%d" % r) for r in range(len(Y_GROUPS))]
 
         def quantize(codes, scales, src):
-            nc.vector.quantize_mx(out=codes[:].bitcast(FP8X4), scales=scales[:], in_=src)
+            nc.vector.quantize_mx(out=codes.bitcast(FP8X4), scales=scales, in_=src)
+
+        def columns(experts, width):
+            return slice(experts[0] % 2 * width, (experts[-1] % 2 + 1) * width)
 
         def spread_gate():
             nc.vector.memset(ones[:], 1.0)
@@ -127,10 +142,10 @@ def tile_moe_pre_mlp_silu_kernel(tc, xT, w1, w2, gate, offs, pos1, pos2, out):
                 part = slice(q, q + QUADRANT)
                 nc.vector.tensor_tensor(identity[part, part], column[part, part], row[part, part],
                                         mybir.AluOpType.is_equal)
-            turned = y_ps[-1]
+            turned = a_ps[0][:].rearrange("p t c -> p (t c)")
             nc.tensor.transpose(turned[:, 0:P], gate_square[:], identity[:])
             nc.vector.tensor_copy(gate_columns[:], turned[:, 0:E])
-            for n, (lo, hi) in enumerate(runs):
+            for n, (lo, hi) in list(enumerate(runs))[1:]:
                 bank = y_ps[n]
                 for e in range(lo // C, hi // C):
                     nc.tensor.transpose(bank[:, e * C - lo:(e + 1) * C - lo],
@@ -151,21 +166,21 @@ def tile_moe_pre_mlp_silu_kernel(tc, xT, w1, w2, gate, offs, pos1, pos2, out):
                 nc.vector.tensor_copy(dst, src)
 
         def quantize_x(n):
-            quantize(x_codes[n], x_scales[n], x_bf[n])
+            quantize(x_codes[n][:], x_scales[n][:], x_bf[n])
 
         def round_w1(e):
-            buf = w1_bf[e % RING]
-            if e < SHARED_FROM:
-                nc.scalar.copy(buf[:].rearrange("p (u v m j) -> p u m j v", u=2, v=2, j=PACK),
-                               w1_raw[e][:].rearrange("p j (m u v) -> p u m j v", u=2, v=2))
+            buf = w1_bf[e // 2 % RING][:, columns([e], PACK * H)]
+            dst = buf.rearrange("p (u v m j) -> p u m j v", u=2, v=2, j=PACK)
+            src = w1_raw[e][:].rearrange("p j (m u v) -> p u m j v", u=2, v=2)
+            if e in ON_VECTOR:
+                nc.vector.tensor_copy(dst, src)
             else:
-                dst = buf[:].rearrange("p (t m j) -> p m j t", t=PACK, j=PACK)
-                src = w1_raw[e][:].rearrange("p j (m t) -> p m j t", t=PACK)
-                nc.scalar.copy(dst[:, :, :, 0:2], src[:, :, :, 0:2])
-                nc.vector.tensor_copy(dst[:, :, :, 2:4], src[:, :, :, 2:4])
+                nc.scalar.copy(dst, src)
 
-        def quantize_w1(e):
-            quantize(w1_codes[e], w1_scales[e], w1_bf[e % RING][:])
+        def quantize_w1(experts):
+            q = experts[0] // 2
+            quantize(w1_codes[q][:, columns(experts, H)], w1_scales[q][:, columns(experts, H)],
+                     w1_bf[q % RING][:, columns(experts, PACK * H)])
 
         def run_of(e):
             return max(m for m, (lo, hi) in enumerate(runs) if lo <= e * C)
@@ -174,26 +189,32 @@ def tile_moe_pre_mlp_silu_kernel(tc, xT, w1, w2, gate, offs, pos1, pos2, out):
             n = run_of(e)
             slots = slice(e * C - runs[n][0], (e + 1) * C - runs[n][0])
             for t in range(PACK):
-                cols = slice(t * P, (t + 1) * P)
-                nc.tensor.matmul_mx(out=a_ps[e % A_BANKS][:, t, :], lhsT=w1_codes[e][:, cols].bitcast(FP8X4),
-                                    lhsT_scale=w1_scales[e][:, cols],
+                cols = slice(e % 2 * H + t * P, e % 2 * H + (t + 1) * P)
+                nc.tensor.matmul_mx(out=a_ps[e % A_BANKS][:, t, :], lhsT=w1_codes[e // 2][:, cols].bitcast(FP8X4),
+                                    lhsT_scale=w1_scales[e // 2][:, cols],
                                     rhs=x_codes[n][:, slots].bitcast(FP8X4),
                                     rhs_scale=x_scales[n][:, slots], start=True, stop=True)
 
         def activate(e):
-            nc.scalar.activation(h_bf[e].rearrange("p (c t) -> p c t", t=PACK),
+            nc.scalar.activation(h_bf[e // 2][:, columns([e], PACK * C)].rearrange("p (c t) -> p c t", t=PACK),
                                  a_ps[e % A_BANKS][:].rearrange("p t c -> p c t"), SILU)
 
-        def quantize_h(e):
-            quantize(h_codes[e], h_scales[e], h_bf[e])
+        def quantize_h(experts):
+            q = experts[0] // 2
+            quantize(h_codes[q][:, columns(experts, C)], h_scales[q][:, columns(experts, C)],
+                     h_bf[q][:, columns(experts, PACK * C)])
 
         def round_w2(n):
             size = len(W2_GROUPS[n])
-            nc.vector.tensor_copy(w2_bf[n][:].rearrange("p (e c i j) -> p e c j i", e=size, i=LINE, j=PACK),
-                                  w2_raw[n][:].rearrange("p e j (c i) -> p e c j i", i=LINE))
+            dst = w2_bf[n].rearrange("p (e c i j) -> p e c j i", e=size, i=LINE, j=PACK)
+            src = w2_raw[n][:].rearrange("p e j (c i) -> p e c j i", i=LINE)
+            if n in W2_ON_SCALAR:
+                nc.scalar.copy(dst, src)
+            else:
+                nc.vector.tensor_copy(dst, src)
 
         def quantize_w2(n):
-            quantize(w2_codes[n], w2_scales[n], w2_bf[n][:])
+            quantize(w2_codes[n][:], w2_scales[n][:], w2_bf[n])
 
         def second_product(n):
             for r, e in enumerate(W2_GROUPS[n]):
@@ -202,7 +223,8 @@ def tile_moe_pre_mlp_silu_kernel(tc, xT, w1, w2, gate, offs, pos1, pos2, out):
                 cols = slice(r * N, (r + 1) * N)
                 nc.tensor.matmul_mx(out=y_ps[b][:, (e - first_e) * C:(e - first_e + 1) * C],
                                     lhsT=w2_codes[n][:, cols].bitcast(FP8X4), lhsT_scale=w2_scales[n][:, cols],
-                                    rhs=h_codes[e][:].bitcast(FP8X4), rhs_scale=h_scales[e][:],
+                                    rhs=h_codes[e // 2][:, columns([e], C)].bitcast(FP8X4),
+                                    rhs_scale=h_scales[e // 2][:, columns([e], C)],
                                     start=True, stop=True)
 
         spread_gate()
@@ -215,43 +237,65 @@ def tile_moe_pre_mlp_silu_kernel(tc, xT, w1, w2, gate, offs, pos1, pos2, out):
                 round_x(n)
                 quantize_x(n)
         waiting = []
+        done = []
         for e in range(E):
             round_w1(e)
-            quantize_w1(e)
+            if e == E - 1:
+                w1_codes.append(held.tile([P, 2 * H], U32, name="last_codes", tag="w1_raw%d" % e, align_bytes=64))
+                quantize_w1([e - 1])
+                first_product(e - 1)
+            together = [e - 1, e] if e % 2 and e < SINGLY_FROM else [e] if e >= SINGLY_FROM and e != E - 2 else []
+            if together:
+                quantize_w1(together)
             for n in X_HOST:
                 if X_HOST[n] == e:
                     round_x(n)
                     quantize_x(n)
-            waiting.append(e)
-            ready = [d for d in range(E - 1) if max(d + 1, FIRST_HOST) == e]
-            for d in [d for d in waiting if X_HOST.get(run_of(d), 0) <= e and d < e]:
+            ready = [q for q in range(PAIRS - 1) if host_of(q) == e]
+            for d in [d for d in waiting if X_HOST.get(run_of(d), 0) <= e]:
                 first_product(d)
                 waiting.remove(d)
-            for d in ready:
-                activate(d)
+            for q in ready:
+                activate(2 * q)
+                activate(2 * q + 1)
+            waiting.extend(together)
             for d in [d for d in waiting if X_HOST.get(run_of(d), 0) <= e]:
                 first_product(d)
                 waiting.remove(d)
             groups = w2_after(e) if e < E - 1 else []
             for n in groups:
                 round_w2(n)
-            for d in ready:
-                quantize_h(d)
+            for q in ready:
+                if q < PAIRS - 2:
+                    quantize_h([2 * q, 2 * q + 1])
+                    done.extend([2 * q, 2 * q + 1])
             for n in groups:
                 quantize_w2(n)
-                second_product(n)
+            for n in range(len(W2_GROUPS)):
+                if W2_AFTER[n] <= e < E - 1 and W2_GROUPS[n][-1] in done and "w%d" % n not in done:
+                    second_product(n)
+                    done.append("w%d" % n)
+        h_codes[PAIRS - 2] = held.tile([P, 2 * C], U32, name="late_codes", tag="w1_bf%d" % ((PAIRS - 1) % RING),
+                                       align_bytes=64)
+        quantize_h([E - 4, E - 3])
+        activate(E - 2)
         activate(E - 1)
+        quantize_h([E - 2])
         tail = w2_after(E - 1)
         round_w2(tail[0])
-        quantize_h(E - 1)
+        quantize_h([E - 1])
         for n in tail:
             if n + 1 in tail:
                 round_w2(n + 1)
             quantize_w2(n)
             second_product(n)
-        y_all = held.tile([P, S], F32, name="y_all", tag="last", align_bytes=64)
+        y_all = held.tile([P, S], F32, name="y_all", tag="w1_raw%d" % Y_AFTER, align_bytes=64)
         for b, group in enumerate(Y_GROUPS):
-            nc.scalar.copy(y_all[:, group[0] * C:(group[-1] + 1) * C], y_ps[b][:, 0:len(group) * C])
+            dst, src = y_all[:, group[0] * C:(group[-1] + 1) * C], y_ps[b][:, 0:len(group) * C]
+            if group is Y_GROUPS[-1]:
+                nc.vector.tensor_copy(dst, src)
+            else:
+                nc.scalar.copy(dst, src)
 
         halves = list(zip(OUT_CUTS[:-1], OUT_CUTS[1:]))
         first = [held.tile([P, hi - lo], F32, name="first%d" % lo) for lo, hi in halves]

@@ -22,21 +22,19 @@ U8 = mybir.dt.uint8
 FP8X4 = mybir.dt.float8_e4m3fn_x4
 MULT = mybir.AluOpType.mult
 ADD = mybir.AluOpType.add
+EQUAL = mybir.AluOpType.is_equal
 SILU = mybir.ActivationFunctionType.Silu
 
-RUN_CUTS = (0, 256, 768, 1280)
-FIRST_HOST = 4
-X_HOST = {2: 4}
-W2_GROUPS = ((0, 1), (2, 3), (4, 5), (6, 7), (8,), (9,))
-W2_AFTER = (4, 6, 9, 9, 9, 9)
-Y_GROUPS = ((0, 1, 2, 3), (4, 5, 6, 7), (8,), (9,))
-ON_VECTOR = (5, 7, 9)
-OUT_CUTS = (0, 320, 640)
-X_AFTER = (1, 2)
-POS_AFTER = 1
-W2_ON_SCALAR = (3,)
-SINGLY_FROM = 8
-Y_AFTER = 7
+RUNS = ((0, 2 * C), (2 * C, 2 * C + BANK), (2 * C + BANK, S))
+LAST_RUN = len(RUNS) - 1
+W2_GROUPS = tuple((2 * q, 2 * q + 1) for q in range(PAIRS - 1)) + ((E - 2,), (E - 1,))
+Y_GROUPS = (tuple(range(0, 4)), tuple(range(4, 8)), (E - 2,), (E - 1,))
+OUT_PARTS = ((0, 384), (384, T))
+
+VECTOR_FROM = 5
+FIRST_SILU_AFTER = 4
+FIRST_Y_AFTER = 7
+W2_LAG = 3
 RING = 2
 A_BANKS = 4
 
@@ -50,15 +48,9 @@ def tile_moe_pre_mlp_silu_kernel(tc, xT, w1, w2, gate, offs, pos1, pos2, out):
         offs_sb = held.tile([P, S // PER_COLUMN], U16, name="offs_sb")
         pos1_sb = held.tile([P, T // PER_COLUMN], U16, name="pos1_sb")
         pos2_sb = held.tile([P, T // PER_COLUMN], U16, name="pos2_sb")
-        runs = list(zip(RUN_CUTS[:-1], RUN_CUTS[1:]))
         x_rows = [held.tile([P, T], F32, name="x_rows%d" % j) for j in range(PACK)]
-        gate_sb = [held.tile([P, hi - lo], F32, name="gate%d" % lo) for lo, hi in runs]
+        gate_sb = [held.tile([P, hi - lo], F32, name="gate%d" % lo) for lo, hi in RUNS]
         gate_square = held.tile([P, P], F32, name="gate_square")
-        gate_columns = held.tile([P, E], F32, name="gate_columns")
-        ones = held.tile([P, P], F32, name="ones")
-        column = held.tile([P, P], F32, name="column", align_bytes=64)
-        row = held.tile([P, P], F32, name="row", align_bytes=64)
-        identity = held.tile([P, P], F32, name="identity")
         w1_raw = [held.tile([P, PACK, H], F32, name="w1_raw%d" % e, tag="w1_raw%d" % e, align_bytes=64)
                   for e in range(E)]
         w2_raw = [held.tile([P, len(group), PACK, N], F32, name="w2_raw%d" % group[0], align_bytes=64)
@@ -67,127 +59,122 @@ def tile_moe_pre_mlp_silu_kernel(tc, xT, w1, w2, gate, offs, pos1, pos2, out):
         def load_x(j):
             nc.sync.dma_start(x_rows[j][:], xT.rearrange("(p j) t -> p j t", j=PACK)[:, j, :])
 
-        def load_w1(e):
-            nc.sync.dma_start(w1_raw[e][:], w1[e].rearrange("(p j) c -> p j c", j=PACK))
+        def w2_behind(e):
+            return [n for n, group in enumerate(W2_GROUPS) if min(group[0] + W2_LAG, E - 1) == e]
 
-        def load_w2(n):
-            group = W2_GROUPS[n]
-            nc.sync.dma_start(w2_raw[n][:].rearrange("p e j n -> p e (j n)"),
-                              w2[group[0]:group[-1] + 1].rearrange("e (p j) n -> p e (j n)", j=PACK))
-
-        def w2_after(e):
-            return [n for n, group in enumerate(W2_GROUPS) if W2_AFTER[n] == e]
-
-        nc.sync.dma_start(gate_square[:], gate.rearrange("k (e c) -> (k e) c", c=C)[0:P, :])
+        nc.scalar.dma_start(gate_square[:], gate.rearrange("k (e c) -> (k e) c", c=C)[0:P, :])
         nc.sync.dma_start(offs_sb[:], offs)
         load_x(0)
-        nc.sync.dma_start(gate_sb[0][:], gate[0:P, runs[0][0]:runs[0][1]])
+        nc.sync.dma_start(gate_sb[0][:], gate[0:P, RUNS[0][0]:RUNS[0][1]])
         load_x(1)
         for e in range(E):
-            load_w1(e)
-            for j in range(2, PACK):
-                if X_AFTER[j - 2] == e:
-                    load_x(j)
-            if e == POS_AFTER:
+            nc.sync.dma_start(w1_raw[e][:], w1[e].rearrange("(p j) c -> p j c", j=PACK))
+            if 2 <= e + 1 < PACK:
+                load_x(e + 1)
+            if e == 1:
                 nc.sync.dma_start(pos1_sb[:], pos1)
                 nc.sync.dma_start(pos2_sb[:], pos2)
-            for n in w2_after(e):
-                load_w2(n)
+            for n in w2_behind(e):
+                group = W2_GROUPS[n]
+                nc.sync.dma_start(w2_raw[n][:].rearrange("p e j n -> p e (j n)"),
+                                  w2[group[0]:group[-1] + 1].rearrange("e (p j) n -> p e (j n)", j=PACK))
 
-        def mx_operands(name, widths):
-            codes = [held.tile([P, w], U32, name="%s_codes%d" % (name, n), align_bytes=64)
-                     for n, w in enumerate(widths)]
-            scales = [held.tile([P, w], U8, name="%s_scales%d" % (name, n), align_bytes=64)
-                      for n, w in enumerate(widths)]
-            return codes, scales
+        def words(name, width, tag=None):
+            return held.tile([P, width], U32, name=name, tag=tag or name, align_bytes=64)
 
-        x_codes, x_scales = mx_operands("x", [hi - lo for lo, hi in runs])
-        w1_codes, w1_scales = mx_operands("w1", [2 * H] * (PAIRS - 1))
-        w1_scales.append(held.tile([P, 2 * H], U8, name="last_scales", align_bytes=64))
-        h_codes, h_scales = mx_operands("h", [2 * C] * PAIRS)
-        w2_codes, w2_scales = mx_operands("w2", [len(group) * N for group in W2_GROUPS])
+        def scale_bytes(name, width):
+            return held.tile([P, width], U8, name=name, align_bytes=64)
 
-        def host_of(q):
-            return max(2 * q + 2, FIRST_HOST)
+        def rounded(name, width):
+            return held.tile([P, width], BF16, name=name, tag=name, align_bytes=64)
 
-        def freed(e, start, words):
-            return w1_raw[e][:].rearrange("p j c -> p (j c)")[:, start:start + words]
+        def freed(e, start, width):
+            return w1_raw[e][:].rearrange("p j c -> p (j c)")[:, start // 2:(start + width) // 2].bitcast(BF16)
 
-        picked = [held.tile([P, PACK, hi - lo], F32, name="picked%d" % lo) for lo, hi in runs]
-        x_bf = [freed(X_HOST[n], 2 * H, (hi - lo) * PACK // 2).bitcast(BF16) if n in X_HOST else
-                held.tile([P, (hi - lo) * PACK], BF16, name="x_bf%d" % lo, align_bytes=64)[:]
-                for n, (lo, hi) in enumerate(runs)]
-        h_words = C * PACK // 2
-        h_bf = [freed(host_of(q), q % 2 * 2 * h_words, 2 * h_words).bitcast(BF16) for q in range(PAIRS - 1)]
-        h_bf.append(held.tile([P, 2 * C * PACK], BF16, name="h_last", align_bytes=64)[:])
-        w1_bf = [held.tile([P, 2 * PACK * H], BF16, name="w1_bf%d" % r, tag="w1_bf%d" % r, align_bytes=64)
-                 for r in range(RING)]
-        w2_bf = [held.tile([P, len(group) * PACK * N], BF16, name="w2_bf%d" % n, align_bytes=64)[:]
-                 for n, group in enumerate(W2_GROUPS)]
+        def silu_after(q):
+            return max(2 * q + 2, FIRST_SILU_AFTER)
+
+        picked = [held.tile([P, PACK, hi - lo], F32, name="picked%d" % lo) for lo, hi in RUNS]
+        x_bf = [rounded("x_bf%d" % lo, PACK * (hi - lo))[:] for lo, hi in RUNS[:LAST_RUN]]
+        last_run_after = RUNS[LAST_RUN][0] // C - 1
+        x_bf.append(freed(last_run_after, 0, PACK * BANK))
+        h_width = 2 * PACK * C
+        h_bf = [freed(silu_after(q), q % 2 * h_width, h_width) for q in range(PAIRS - 1)]
+        h_bf.append(rounded("h_last", h_width)[:])
+        w1_bf = [rounded("w1_bf%d" % r, 2 * PACK * H) for r in range(RING)]
+        w2_bf = [rounded("w2_bf%d" % group[0], len(group) * PACK * N) for group in W2_GROUPS]
+        x_codes = [words("x_codes%d" % lo, hi - lo) for lo, hi in RUNS]
+        x_scales = [scale_bytes("x_scales%d" % lo, hi - lo) for lo, hi in RUNS]
+        w1_codes = {q: words("w1_codes%d" % q, 2 * H) for q in range(PAIRS - 1)}
+        w1_scales = [scale_bytes("w1_scales%d" % q, 2 * H) for q in range(PAIRS)]
+        h_codes = {q: words("h_codes%d" % q, 2 * C) for q in range(PAIRS) if q != PAIRS - 2}
+        h_scales = [scale_bytes("h_scales%d" % q, 2 * C) for q in range(PAIRS)]
+        w2_codes = [words("w2_codes%d" % group[0], len(group) * N) for group in W2_GROUPS]
+        w2_scales = [scale_bytes("w2_scales%d" % group[0], len(group) * N) for group in W2_GROUPS]
         a_ps = [psum.tile([P, PACK, C], F32, name="a_ps%d" % r) for r in range(A_BANKS)]
         y_ps = [psum.tile([P, BANK], F32, name="y_ps%d" % r) for r in range(len(Y_GROUPS))]
+
+        def copy(on_vector, dst, src):
+            if on_vector:
+                nc.vector.tensor_copy(dst, src)
+            else:
+                nc.scalar.copy(dst, src)
 
         def quantize(codes, scales, src):
             nc.vector.quantize_mx(out=codes.bitcast(FP8X4), scales=scales, in_=src)
 
-        def columns(experts, width):
+        def part(experts, width):
             return slice(experts[0] % 2 * width, (experts[-1] % 2 + 1) * width)
 
-        def spread_gate():
+        def build_identity():
+            ones = held.tile([P, P], F32, name="ones")
+            column = held.tile([P, P], F32, name="column", align_bytes=64)
+            row = held.tile([P, P], F32, name="row", align_bytes=64)
+            identity = held.tile([P, P], F32, name="identity")
             nc.vector.memset(ones[:], 1.0)
             nc.vector.memset(identity[:], 0.0)
             nc.vector.tensor_tensor_scan(column[:], ones[:], ones[:], 0.0, MULT, ADD)
             nc.vector.transpose(row[:], column[:])
-            for q in range(0, P, QUADRANT):
-                part = slice(q, q + QUADRANT)
-                nc.vector.tensor_tensor(identity[part, part], column[part, part], row[part, part],
-                                        mybir.AluOpType.is_equal)
-            turned = a_ps[0][:].rearrange("p t c -> p (t c)")
-            nc.tensor.transpose(turned[:, 0:P], gate_square[:], identity[:])
-            nc.vector.tensor_copy(gate_columns[:], turned[:, 0:E])
-            for n, (lo, hi) in list(enumerate(runs))[1:]:
-                bank = y_ps[n]
+            for start in range(0, P, QUADRANT):
+                block = slice(start, start + QUADRANT)
+                nc.vector.tensor_tensor(identity[block, block], column[block, block], row[block, block], EQUAL)
+            return identity
+
+        def spread_gate():
+            identity = build_identity()
+            skipped = RUNS[1][0] // C
+            gate_columns = held.tile([P, E - skipped], F32, name="gate_columns")
+            nc.tensor.transpose(a_ps[0][:, 0, :], gate_square[:], identity[:])
+            nc.vector.tensor_copy(gate_columns[:], a_ps[0][:, 0, skipped:E])
+            for n in range(1, len(RUNS)):
+                lo, hi = RUNS[n]
                 for e in range(lo // C, hi // C):
-                    nc.tensor.transpose(bank[:, e * C - lo:(e + 1) * C - lo],
-                                        gate_columns[:, e:e + 1].to_broadcast([P, P]), identity[:])
-                nc.scalar.copy(gate_sb[n][:], bank[:, 0:hi - lo])
+                    nc.tensor.transpose(y_ps[n][:, e * C - lo:(e + 1) * C - lo],
+                                        gate_columns[:, e - skipped:e - skipped + 1].to_broadcast([P, P]), identity[:])
+                nc.scalar.copy(gate_sb[n][:], y_ps[n][:])
 
         def gather_x(n, j):
-            lo, hi = runs[n]
+            lo, hi = RUNS[n]
             tokens = x_rows[j][:].indirect(offs_sb[:, lo // PER_COLUMN:hi // PER_COLUMN])
             nc.vector.tensor_tensor(picked[n][:, j, :], tokens, gate_sb[n][:], MULT)
 
-        def round_x(n):
-            dst = x_bf[n].rearrange("p (c i j) -> p c j i", i=LINE, j=PACK)
-            src = picked[n][:].rearrange("p j (c i) -> p c j i", i=LINE)
-            if n in X_HOST:
-                nc.scalar.copy(dst, src)
-            else:
-                nc.vector.tensor_copy(dst, src)
-
-        def quantize_x(n):
+        def round_and_quantize_x(n):
+            nc.vector.tensor_copy(x_bf[n].rearrange("p (c i j) -> p c j i", i=LINE, j=PACK),
+                                  picked[n][:].rearrange("p j (c i) -> p c j i", i=LINE))
             quantize(x_codes[n][:], x_scales[n][:], x_bf[n])
 
         def round_w1(e):
-            buf = w1_bf[e // 2 % RING][:, columns([e], PACK * H)]
-            dst = buf.rearrange("p (u v m j) -> p u m j v", u=2, v=2, j=PACK)
-            src = w1_raw[e][:].rearrange("p j (m u v) -> p u m j v", u=2, v=2)
-            if e in ON_VECTOR:
-                nc.vector.tensor_copy(dst, src)
-            else:
-                nc.scalar.copy(dst, src)
+            dst = w1_bf[e // 2 % RING][:, part([e], PACK * H)].rearrange("p (u v m j) -> p u m j v", u=2, v=2, j=PACK)
+            copy(e % 2 == 1 and e >= VECTOR_FROM, dst, w1_raw[e][:].rearrange("p j (m u v) -> p u m j v", u=2, v=2))
 
         def quantize_w1(experts):
             q = experts[0] // 2
-            quantize(w1_codes[q][:, columns(experts, H)], w1_scales[q][:, columns(experts, H)],
-                     w1_bf[q % RING][:, columns(experts, PACK * H)])
-
-        def run_of(e):
-            return max(m for m, (lo, hi) in enumerate(runs) if lo <= e * C)
+            quantize(w1_codes[q][:, part(experts, H)], w1_scales[q][:, part(experts, H)],
+                     w1_bf[q % RING][:, part(experts, PACK * H)])
 
         def first_product(e):
-            n = run_of(e)
-            slots = slice(e * C - runs[n][0], (e + 1) * C - runs[n][0])
+            n = max(m for m, (lo, hi) in enumerate(RUNS) if lo <= e * C)
+            slots = slice(e * C - RUNS[n][0], (e + 1) * C - RUNS[n][0])
             for t in range(PACK):
                 cols = slice(e % 2 * H + t * P, e % 2 * H + (t + 1) * P)
                 nc.tensor.matmul_mx(out=a_ps[e % A_BANKS][:, t, :], lhsT=w1_codes[e // 2][:, cols].bitcast(FP8X4),
@@ -196,113 +183,92 @@ def tile_moe_pre_mlp_silu_kernel(tc, xT, w1, w2, gate, offs, pos1, pos2, out):
                                     rhs_scale=x_scales[n][:, slots], start=True, stop=True)
 
         def activate(e):
-            nc.scalar.activation(h_bf[e // 2][:, columns([e], PACK * C)].rearrange("p (c t) -> p c t", t=PACK),
+            nc.scalar.activation(h_bf[e // 2][:, part([e], PACK * C)].rearrange("p (c t) -> p c t", t=PACK),
                                  a_ps[e % A_BANKS][:].rearrange("p t c -> p c t"), SILU)
 
         def quantize_h(experts):
             q = experts[0] // 2
-            quantize(h_codes[q][:, columns(experts, C)], h_scales[q][:, columns(experts, C)],
-                     h_bf[q][:, columns(experts, PACK * C)])
+            quantize(h_codes[q][:, part(experts, C)], h_scales[q][:, part(experts, C)],
+                     h_bf[q][:, part(experts, PACK * C)])
 
         def round_w2(n):
             size = len(W2_GROUPS[n])
-            dst = w2_bf[n].rearrange("p (e c i j) -> p e c j i", e=size, i=LINE, j=PACK)
-            src = w2_raw[n][:].rearrange("p e j (c i) -> p e c j i", i=LINE)
-            if n in W2_ON_SCALAR:
-                nc.scalar.copy(dst, src)
-            else:
-                nc.vector.tensor_copy(dst, src)
+            copy(n not in (0, PAIRS - 2),
+                 w2_bf[n][:].rearrange("p (e c i j) -> p e c j i", e=size, i=LINE, j=PACK),
+                 w2_raw[n][:].rearrange("p e j (c i) -> p e c j i", i=LINE))
 
         def quantize_w2(n):
-            quantize(w2_codes[n][:], w2_scales[n][:], w2_bf[n])
+            quantize(w2_codes[n][:], w2_scales[n][:], w2_bf[n][:])
 
         def second_product(n):
             for r, e in enumerate(W2_GROUPS[n]):
                 b = [m for m, group in enumerate(Y_GROUPS) if e in group][0]
-                first_e = Y_GROUPS[b][0]
+                place = e - Y_GROUPS[b][0]
                 cols = slice(r * N, (r + 1) * N)
-                nc.tensor.matmul_mx(out=y_ps[b][:, (e - first_e) * C:(e - first_e + 1) * C],
+                nc.tensor.matmul_mx(out=y_ps[b][:, place * C:(place + 1) * C],
                                     lhsT=w2_codes[n][:, cols].bitcast(FP8X4), lhsT_scale=w2_scales[n][:, cols],
-                                    rhs=h_codes[e // 2][:, columns([e], C)].bitcast(FP8X4),
-                                    rhs_scale=h_scales[e // 2][:, columns([e], C)],
-                                    start=True, stop=True)
+                                    rhs=h_codes[e // 2][:, part([e], C)].bitcast(FP8X4),
+                                    rhs_scale=h_scales[e // 2][:, part([e], C)], start=True, stop=True)
 
         spread_gate()
-        for j in range(PACK - 1):
-            for n in range(len(runs)):
+        for j in range(PACK):
+            for n in range(len(RUNS)):
                 gather_x(n, j)
-        for n in range(len(runs)):
-            gather_x(n, PACK - 1)
-            if n not in X_HOST:
-                round_x(n)
-                quantize_x(n)
-        waiting = []
-        done = []
-        for e in range(E):
+                if j == PACK - 1 and n < LAST_RUN:
+                    round_and_quantize_x(n)
+
+        multiplied = 0
+        for e in range(E - 1):
             round_w1(e)
-            if e == E - 1:
-                w1_codes.append(held.tile([P, 2 * H], U32, name="last_codes", tag="w1_raw%d" % e, align_bytes=64))
-                quantize_w1([e - 1])
-                first_product(e - 1)
-            together = [e - 1, e] if e % 2 and e < SINGLY_FROM else [e] if e >= SINGLY_FROM and e != E - 2 else []
-            if together:
-                quantize_w1(together)
-            for n in X_HOST:
-                if X_HOST[n] == e:
-                    round_x(n)
-                    quantize_x(n)
-            ready = [q for q in range(PAIRS - 1) if host_of(q) == e]
-            for d in [d for d in waiting if X_HOST.get(run_of(d), 0) <= e]:
-                first_product(d)
-                waiting.remove(d)
+            if e % 2 == 1:
+                quantize_w1([e - 1, e])
+            if e == last_run_after:
+                round_and_quantize_x(LAST_RUN)
+            ready = [q for q in range(PAIRS - 1) if silu_after(q) == e]
             for q in ready:
                 activate(2 * q)
                 activate(2 * q + 1)
-            waiting.extend(together)
-            for d in [d for d in waiting if X_HOST.get(run_of(d), 0) <= e]:
-                first_product(d)
-                waiting.remove(d)
-            groups = w2_after(e) if e < E - 1 else []
-            for n in groups:
+            if e % 2 == 1:
+                first_product(e - 1)
+                first_product(e)
+            for n in w2_behind(e):
                 round_w2(n)
             for q in ready:
-                if q < PAIRS - 2:
+                if q in h_codes:
                     quantize_h([2 * q, 2 * q + 1])
-                    done.extend([2 * q, 2 * q + 1])
-            for n in groups:
+            for n in w2_behind(e):
                 quantize_w2(n)
-            for n in range(len(W2_GROUPS)):
-                if W2_AFTER[n] <= e < E - 1 and W2_GROUPS[n][-1] in done and "w%d" % n not in done:
-                    second_product(n)
-                    done.append("w%d" % n)
-        h_codes[PAIRS - 2] = held.tile([P, 2 * C], U32, name="late_codes", tag="w1_bf%d" % ((PAIRS - 1) % RING),
-                                       align_bytes=64)
+            while W2_GROUPS[multiplied][0] + W2_LAG <= e and silu_after(multiplied) <= e:
+                second_product(multiplied)
+                multiplied += 1
+
+        round_w1(E - 1)
+        w1_codes[PAIRS - 1] = words("w1_codes_last", 2 * H, tag="w1_raw%d" % (E - 1))
+        for e in (E - 2, E - 1):
+            quantize_w1([e])
+            first_product(e)
+        h_codes[PAIRS - 2] = words("h_codes_late", 2 * C, tag="w1_bf%d" % ((PAIRS - 1) % RING))
         quantize_h([E - 4, E - 3])
         activate(E - 2)
         activate(E - 1)
         quantize_h([E - 2])
-        tail = w2_after(E - 1)
-        round_w2(tail[0])
+        round_w2(multiplied)
         quantize_h([E - 1])
-        for n in tail:
-            if n + 1 in tail:
+        for n in range(multiplied, len(W2_GROUPS)):
+            if n + 1 < len(W2_GROUPS):
                 round_w2(n + 1)
             quantize_w2(n)
             second_product(n)
-        y_all = held.tile([P, S], F32, name="y_all", tag="w1_raw%d" % Y_AFTER, align_bytes=64)
-        for b, group in enumerate(Y_GROUPS):
-            dst, src = y_all[:, group[0] * C:(group[-1] + 1) * C], y_ps[b][:, 0:len(group) * C]
-            if group is Y_GROUPS[-1]:
-                nc.vector.tensor_copy(dst, src)
-            else:
-                nc.scalar.copy(dst, src)
 
-        halves = list(zip(OUT_CUTS[:-1], OUT_CUTS[1:]))
-        first = [held.tile([P, hi - lo], F32, name="first%d" % lo) for lo, hi in halves]
-        total = [held.tile([P, hi - lo], F32, name="total%d" % lo) for lo, hi in halves]
-        for n, (lo, hi) in enumerate(halves):
+        y_all = held.tile([P, S], F32, name="y_all", tag="w1_raw%d" % FIRST_Y_AFTER, align_bytes=64)
+        for b, group in enumerate(Y_GROUPS):
+            copy(b == len(Y_GROUPS) - 1, y_all[:, group[0] * C:(group[-1] + 1) * C], y_ps[b][:, 0:len(group) * C])
+
+        first = [held.tile([P, hi - lo], F32, name="first%d" % lo) for lo, hi in OUT_PARTS]
+        total = [held.tile([P, hi - lo], F32, name="total%d" % lo) for lo, hi in OUT_PARTS]
+        for n, (lo, hi) in enumerate(OUT_PARTS):
             nc.vector.tensor_copy(first[n][:], y_all[:].indirect(pos1_sb[:, lo // PER_COLUMN:hi // PER_COLUMN]))
-        for n, (lo, hi) in enumerate(halves):
+        for n, (lo, hi) in enumerate(OUT_PARTS):
             nc.vector.tensor_tensor(total[n][:], y_all[:].indirect(pos2_sb[:, lo // PER_COLUMN:hi // PER_COLUMN]),
                                     first[n][:], ADD)
             nc.sync.dma_start(out[:, lo:hi], total[n][:])

@@ -28,13 +28,13 @@ SILU = mybir.ActivationFunctionType.Silu
 RUNS = ((0, 2 * C), (2 * C, 2 * C + BANK), (2 * C + BANK, S))
 LAST_RUN = len(RUNS) - 1
 W2_GROUPS = tuple((2 * q, 2 * q + 1) for q in range(PAIRS - 1)) + ((E - 2,), (E - 1,))
-Y_GROUPS = (tuple(range(0, 4)), tuple(range(4, 8)), (E - 2,), (E - 1,))
+Y_GROUPS = tuple(tuple(range(e, min(e + BANK // C, E))) for e in range(0, E, BANK // C))
 OUT_PARTS = ((0, 384), (384, T))
 
 VECTOR_FROM = 5
 FIRST_SILU_AFTER = 4
-FIRST_Y_AFTER = 7
-W2_LAG = 3
+FIRST_W2_AFTER = 3
+W2_EVERY = 4
 RING = 2
 A_BANKS = 4
 
@@ -60,7 +60,7 @@ def tile_moe_pre_mlp_silu_kernel(tc, xT, w1, w2, gate, offs, pos1, pos2, out):
             nc.sync.dma_start(x_rows[j][:], xT.rearrange("(p j) t -> p j t", j=PACK)[:, j, :])
 
         def w2_behind(e):
-            return [n for n, group in enumerate(W2_GROUPS) if min(group[0] + W2_LAG, E - 1) == e]
+            return [n for n in range(len(W2_GROUPS)) if min(FIRST_W2_AFTER + W2_EVERY * n, E - 1) == e]
 
         nc.scalar.dma_start(gate_square[:], gate.rearrange("k (e c) -> (k e) c", c=C)[0:P, :])
         nc.sync.dma_start(offs_sb[:], offs)
@@ -193,7 +193,7 @@ def tile_moe_pre_mlp_silu_kernel(tc, xT, w1, w2, gate, offs, pos1, pos2, out):
 
         def round_w2(n):
             size = len(W2_GROUPS[n])
-            copy(n not in (0, PAIRS - 2),
+            copy(n == w2_behind(E - 1)[0] or size == 1,
                  w2_bf[n][:].rearrange("p (e c i j) -> p e c j i", e=size, i=LINE, j=PACK),
                  w2_raw[n][:].rearrange("p e j (c i) -> p e c j i", i=LINE))
 
@@ -217,7 +217,6 @@ def tile_moe_pre_mlp_silu_kernel(tc, xT, w1, w2, gate, offs, pos1, pos2, out):
                 if j == PACK - 1 and n < LAST_RUN:
                     round_and_quantize_x(n)
 
-        multiplied = 0
         for e in range(E - 1):
             round_w1(e)
             if e % 2 == 1:
@@ -238,9 +237,9 @@ def tile_moe_pre_mlp_silu_kernel(tc, xT, w1, w2, gate, offs, pos1, pos2, out):
                     quantize_h([2 * q, 2 * q + 1])
             for n in w2_behind(e):
                 quantize_w2(n)
-            while W2_GROUPS[multiplied][0] + W2_LAG <= e and silu_after(multiplied) <= e:
-                second_product(multiplied)
-                multiplied += 1
+            for n in range(w2_behind(E - 1)[0]):
+                if max(FIRST_W2_AFTER + W2_EVERY * n, silu_after(n)) == e:
+                    second_product(n)
 
         round_w1(E - 1)
         w1_codes[PAIRS - 1] = words("w1_codes_last", 2 * H, tag="w1_raw%d" % (E - 1))
@@ -252,15 +251,16 @@ def tile_moe_pre_mlp_silu_kernel(tc, xT, w1, w2, gate, offs, pos1, pos2, out):
         activate(E - 2)
         activate(E - 1)
         quantize_h([E - 2])
-        round_w2(multiplied)
+        last_groups = w2_behind(E - 1)
+        round_w2(last_groups[0])
         quantize_h([E - 1])
-        for n in range(multiplied, len(W2_GROUPS)):
-            if n + 1 < len(W2_GROUPS):
+        for n in last_groups:
+            if n + 1 in last_groups:
                 round_w2(n + 1)
             quantize_w2(n)
             second_product(n)
 
-        y_all = held.tile([P, S], F32, name="y_all", tag="w1_raw%d" % FIRST_Y_AFTER, align_bytes=64)
+        y_all = held.tile([P, S], F32, name="y_all", tag="w1_raw%d" % (E - 2), align_bytes=64)
         for b, group in enumerate(Y_GROUPS):
             copy(b == len(Y_GROUPS) - 1, y_all[:, group[0] * C:(group[-1] + 1) * C], y_ps[b][:, 0:len(group) * C])
 

@@ -7,7 +7,7 @@ S = E * C
 PAIRS = E // 2
 P = 128
 PACK = 4
-LINE = 4
+STEP = 2
 PER_COLUMN = 16
 QUADRANT = 32
 BANK = 512
@@ -159,8 +159,8 @@ def tile_moe_pre_mlp_silu_kernel(tc, xT, w1, w2, gate, offs, pos1, pos2, out):
             nc.vector.tensor_tensor(picked[n][:, j, :], tokens, gate_sb[n][:], MULT)
 
         def round_and_quantize_x(n):
-            nc.vector.tensor_copy(x_bf[n].rearrange("p (c i j) -> p c j i", i=LINE, j=PACK),
-                                  picked[n][:].rearrange("p j (c i) -> p c j i", i=LINE))
+            nc.vector.tensor_copy(x_bf[n].rearrange("p (c i j) -> p c j i", i=STEP, j=PACK),
+                                  picked[n][:].rearrange("p j (c i) -> p c j i", i=STEP))
             quantize(x_codes[n][:], x_scales[n][:], x_bf[n])
 
         def round_w1(e):
@@ -194,8 +194,8 @@ def tile_moe_pre_mlp_silu_kernel(tc, xT, w1, w2, gate, offs, pos1, pos2, out):
         def round_w2(n):
             size = len(W2_GROUPS[n])
             copy(n == w2_behind(E - 1)[0] or size == 1,
-                 w2_bf[n][:].rearrange("p (e c i j) -> p e c j i", e=size, i=LINE, j=PACK),
-                 w2_raw[n][:].rearrange("p e j (c i) -> p e c j i", i=LINE))
+                 w2_bf[n][:].rearrange("p (e c i j) -> p e c j i", e=size, i=STEP, j=PACK),
+                 w2_raw[n][:].rearrange("p e j (c i) -> p e c j i", i=STEP))
 
         def quantize_w2(n):
             quantize(w2_codes[n][:], w2_scales[n][:], w2_bf[n][:])

@@ -132,6 +132,8 @@ def tile_moe_pre_mlp_silu_kernel(tc, xT, w1, w2, gate, offs, pos1, pos2, out):
             row = held.tile([P, P], F32, name="row", align_bytes=64)
             identity = held.tile([P, P], F32, name="identity")
             nc.vector.memset(ones[:], 1.0)
+            warm = held.tile([P, 1], F32, name="warm")
+            nc.scalar.activation(warm[:], ones[:, 0:1], SILU)
             nc.vector.memset(identity[:], 0.0)
             nc.vector.tensor_tensor_scan(column[:], ones[:], ones[:], 0.0, MULT, ADD)
             nc.vector.transpose(row[:], column[:])

@@ -53,14 +53,15 @@ def tile_moe_pre_mlp_silu_kernel(tc, xT, w1, w2, gate, offs, pos1, pos2, out):
         gate_square = held.tile([P, P], F32, name="gate_square")
         w1_raw = [held.tile([P, PACK, H], F32, name="w1_raw%d" % e, tag="w1_raw%d" % e, align_bytes=64)
                   for e in range(E)]
-        w2_raw = [held.tile([P, len(group), PACK, N], F32, name="w2_raw%d" % group[0], align_bytes=64)
+        w2_raw = [held.tile([P, len(group), PACK, N], F32, name="w2_raw%d" % group[0], tag="w2_raw%d" % group[0],
+                            align_bytes=64)
                   for group in W2_GROUPS]
 
         def load_x(j):
             nc.sync.dma_start(x_rows[j][:], xT.rearrange("(p j) t -> p j t", j=PACK)[:, j, :])
 
         def w2_behind(e):
-            return [n for n in range(len(W2_GROUPS)) if min(FIRST_W2_AFTER + W2_EVERY * n, E - 1) == e]
+            return [n for n in range(len(W2_GROUPS)) if (FIRST_W2_AFTER if n == 0 else E - 1) == e]
 
         nc.scalar.dma_start(gate_square[:], gate.rearrange("k (e c) -> (k e) c", c=C)[0:P, :])
         nc.sync.dma_start(offs_sb[:], offs)
@@ -71,13 +72,13 @@ def tile_moe_pre_mlp_silu_kernel(tc, xT, w1, w2, gate, offs, pos1, pos2, out):
             nc.sync.dma_start(w1_raw[e][:], w1[e].rearrange("(p j) c -> p j c", j=PACK))
             if 2 <= e + 1 < PACK:
                 load_x(e + 1)
-            if e == 1:
-                nc.sync.dma_start(pos1_sb[:], pos1)
-                nc.sync.dma_start(pos2_sb[:], pos2)
             for n in w2_behind(e):
                 group = W2_GROUPS[n]
                 nc.sync.dma_start(w2_raw[n][:].rearrange("p e j n -> p e (j n)"),
                                   w2[group[0]:group[-1] + 1].rearrange("e (p j) n -> p e (j n)", j=PACK))
+
+        nc.sync.dma_start(pos1_sb[:], pos1)
+        nc.sync.dma_start(pos2_sb[:], pos2)
 
         def words(name, width, tag=None):
             return held.tile([P, width], U32, name=name, tag=tag or name, align_bytes=64)
@@ -126,14 +127,15 @@ def tile_moe_pre_mlp_silu_kernel(tc, xT, w1, w2, gate, offs, pos1, pos2, out):
         def part(experts, width):
             return slice(experts[0] % 2 * width, (experts[-1] % 2 + 1) * width)
 
+        def pair(q):
+            return [2 * q, 2 * q + 1]
+
         def build_identity():
             ones = held.tile([P, P], F32, name="ones")
             column = held.tile([P, P], F32, name="column", align_bytes=64)
             row = held.tile([P, P], F32, name="row", align_bytes=64)
             identity = held.tile([P, P], F32, name="identity")
             nc.vector.memset(ones[:], 1.0)
-            warm = held.tile([P, 1], F32, name="warm")
-            nc.scalar.activation(warm[:], ones[:, 0:1], SILU)
             nc.vector.memset(identity[:], 0.0)
             nc.vector.tensor_tensor_scan(column[:], ones[:], ones[:], 0.0, MULT, ADD)
             nc.vector.transpose(row[:], column[:])
@@ -148,6 +150,8 @@ def tile_moe_pre_mlp_silu_kernel(tc, xT, w1, w2, gate, offs, pos1, pos2, out):
             gate_columns = held.tile([P, E - skipped], F32, name="gate_columns")
             nc.tensor.transpose(a_ps[0][:, 0, :], gate_square[:], identity[:])
             nc.vector.tensor_copy(gate_columns[:], a_ps[0][:, 0, skipped:E])
+            warm = held.tile([P, 1], F32, name="warm")
+            nc.scalar.activation(warm[:], gate_columns[:, 0:1], SILU)
             for n in range(1, len(RUNS)):
                 lo, hi = RUNS[n]
                 for e in range(lo // C, hi // C):
@@ -160,9 +164,11 @@ def tile_moe_pre_mlp_silu_kernel(tc, xT, w1, w2, gate, offs, pos1, pos2, out):
             tokens = x_rows[j][:].indirect(offs_sb[:, lo // PER_COLUMN:hi // PER_COLUMN])
             nc.vector.tensor_tensor(picked[n][:, j, :], tokens, gate_sb[n][:], MULT)
 
-        def round_and_quantize_x(n):
+        def round_x(n):
             nc.vector.tensor_copy(x_bf[n].rearrange("p (c i j) -> p c j i", i=STEP, j=PACK),
                                   picked[n][:].rearrange("p j (c i) -> p c j i", i=STEP))
+
+        def quantize_x(n):
             quantize(x_codes[n][:], x_scales[n][:], x_bf[n])
 
         def round_w1(e):
@@ -195,7 +201,7 @@ def tile_moe_pre_mlp_silu_kernel(tc, xT, w1, w2, gate, offs, pos1, pos2, out):
 
         def round_w2(n):
             size = len(W2_GROUPS[n])
-            copy(n == w2_behind(E - 1)[0] or size == 1,
+            copy(n in (2, 3, 5),
                  w2_bf[n][:].rearrange("p (e c i j) -> p e c j i", e=size, i=STEP, j=PACK),
                  w2_raw[n][:].rearrange("p e j (c i) -> p e c j i", i=STEP))
 
@@ -213,35 +219,39 @@ def tile_moe_pre_mlp_silu_kernel(tc, xT, w1, w2, gate, offs, pos1, pos2, out):
                                     rhs_scale=h_scales[e // 2][:, part([e], C)], start=True, stop=True)
 
         spread_gate()
-        for j in range(PACK):
+        for j in range(PACK - 1):
             for n in range(len(RUNS)):
                 gather_x(n, j)
-                if j == PACK - 1 and n < LAST_RUN:
-                    round_and_quantize_x(n)
+        gather_x(0, PACK - 1)
+        gather_x(1, PACK - 1)
+        round_x(0)
+        round_x(1)
+        quantize_x(0)
+        gather_x(LAST_RUN, PACK - 1)
+        quantize_x(1)
 
+        waiting = []
         for e in range(E - 1):
             round_w1(e)
+            for q in range(PAIRS - 1):
+                if silu_after(q) == e:
+                    activate(2 * q)
+                    activate(2 * q + 1)
+                    waiting.append(q)
             if e % 2 == 1:
+                if waiting:
+                    quantize_h(pair(waiting.pop(0)))
                 quantize_w1([e - 1, e])
-            if e == last_run_after:
-                round_and_quantize_x(LAST_RUN)
-            ready = [q for q in range(PAIRS - 1) if silu_after(q) == e]
-            for q in ready:
-                activate(2 * q)
-                activate(2 * q + 1)
-            if e % 2 == 1:
                 first_product(e - 1)
                 first_product(e)
-            for n in w2_behind(e):
-                round_w2(n)
-            for q in ready:
-                if q in h_codes:
-                    quantize_h([2 * q, 2 * q + 1])
-            for n in w2_behind(e):
-                quantize_w2(n)
-            for n in range(w2_behind(E - 1)[0]):
-                if max(FIRST_W2_AFTER + W2_EVERY * n, silu_after(n)) == e:
-                    second_product(n)
+            if e == FIRST_W2_AFTER:
+                round_w2(0)
+                quantize_w2(0)
+            if e == last_run_after:
+                round_x(LAST_RUN)
+                quantize_h(pair(waiting.pop(0)))
+                quantize_x(LAST_RUN)
+                second_product(0)
 
         round_w1(E - 1)
         w1_codes[PAIRS - 1] = words("w1_codes_last", 2 * H, tag="w1_raw%d" % (E - 1))
@@ -249,20 +259,25 @@ def tile_moe_pre_mlp_silu_kernel(tc, xT, w1, w2, gate, offs, pos1, pos2, out):
             quantize_w1([e])
             first_product(e)
         h_codes[PAIRS - 2] = words("h_codes_late", 2 * C, tag="w1_bf%d" % ((PAIRS - 1) % RING))
-        quantize_h([E - 4, E - 3])
+        round_w2(1)
         activate(E - 2)
         activate(E - 1)
-        quantize_h([E - 2])
-        last_groups = w2_behind(E - 1)
-        round_w2(last_groups[0])
-        quantize_h([E - 1])
-        for n in last_groups:
-            if n + 1 in last_groups:
-                round_w2(n + 1)
+        quantize_h(pair(PAIRS - 2))
+        round_w2(2)
+        quantize_w2(1)
+        second_product(1)
+        round_w2(3)
+        quantize_w2(2)
+        quantize_h(pair(PAIRS - 1))
+        quantize_w2(3)
+        round_w2(4)
+        round_w2(5)
+        for n in (4, 5):
             quantize_w2(n)
+        for n in (2, 3, 4, 5):
             second_product(n)
 
-        y_all = held.tile([P, S], F32, name="y_all", tag="w1_raw%d" % (E - 2), align_bytes=64)
+        y_all = held.tile([P, S], F32, name="y_all", tag="w2_raw%d" % (E - 2), align_bytes=64)
         for b, group in enumerate(Y_GROUPS):
             copy(b == len(Y_GROUPS) - 1, y_all[:, group[0] * C:(group[-1] + 1) * C], y_ps[b][:, 0:len(group) * C])
 

@@ -35,7 +35,7 @@ VECTOR_FROM = 5
 FIRST_SILU_AFTER = 4
 FIRST_W2_AFTER = 3
 W2_EVERY = 4
-RING = 2
+RING = 3
 A_BANKS = 4
 
 
@@ -61,17 +61,16 @@ def tile_moe_pre_mlp_silu_kernel(tc, xT, w1, w2, gate, offs, pos1, pos2, out):
             nc.sync.dma_start(x_rows[j][:], xT.rearrange("(p j) t -> p j t", j=PACK)[:, j, :])
 
         def w2_behind(e):
-            return [n for n in range(len(W2_GROUPS)) if (FIRST_W2_AFTER if n == 0 else E - 1) == e]
+            return [n for n in range(len(W2_GROUPS)) if E - 1 == e]
 
         nc.scalar.dma_start(gate_square[:], gate.rearrange("k (e c) -> (k e) c", c=C)[0:P, :])
         nc.sync.dma_start(offs_sb[:], offs)
         load_x(0)
-        nc.sync.dma_start(gate_sb[0][:], gate[0:P, RUNS[0][0]:RUNS[0][1]])
-        load_x(1)
+        nc.scalar.dma_start(gate_sb[0][:], gate[0:P, RUNS[0][0]:RUNS[0][1]])
+        for j in range(1, PACK):
+            load_x(j)
         for e in range(E):
             nc.sync.dma_start(w1_raw[e][:], w1[e].rearrange("(p j) c -> p j c", j=PACK))
-            if 2 <= e + 1 < PACK:
-                load_x(e + 1)
             for n in w2_behind(e):
                 group = W2_GROUPS[n]
                 nc.sync.dma_start(w2_raw[n][:].rearrange("p e j n -> p e (j n)"),
@@ -100,15 +99,15 @@ def tile_moe_pre_mlp_silu_kernel(tc, xT, w1, w2, gate, offs, pos1, pos2, out):
         last_run_after = RUNS[LAST_RUN][0] // C - 1
         x_bf.append(freed(last_run_after, 0, PACK * BANK))
         h_width = 2 * PACK * C
-        h_bf = [freed(silu_after(q), q % 2 * h_width, h_width) for q in range(PAIRS - 1)]
-        h_bf.append(rounded("h_last", h_width)[:])
+        h_bf = [freed(silu_after(q), q % 2 * h_width, h_width) for q in range(PAIRS - 2)]
+        h_bf.extend([w2_raw[n][:].rearrange("p e j n -> p (e j n)").bitcast(BF16)[:, 0:h_width] for n in (0, 2)])
         w1_bf = [rounded("w1_bf%d" % r, 2 * PACK * H) for r in range(RING)]
         w2_bf = [rounded("w2_bf%d" % group[0], len(group) * PACK * N) for group in W2_GROUPS]
         x_codes = [words("x_codes%d" % lo, hi - lo) for lo, hi in RUNS]
         x_scales = [scale_bytes("x_scales%d" % lo, hi - lo) for lo, hi in RUNS]
         w1_codes = {q: words("w1_codes%d" % q, 2 * H) for q in range(PAIRS - 1)}
         w1_scales = [scale_bytes("w1_scales%d" % q, 2 * H) for q in range(PAIRS)]
-        h_codes = {q: words("h_codes%d" % q, 2 * C) for q in range(PAIRS) if q != PAIRS - 2}
+        h_codes = {q: words("h_codes%d" % q, 2 * C) for q in range(PAIRS - 2)}
         h_scales = [scale_bytes("h_scales%d" % q, 2 * C) for q in range(PAIRS)]
         w2_codes = [words("w2_codes%d" % group[0], len(group) * N) for group in W2_GROUPS]
         w2_scales = [scale_bytes("w2_scales%d" % group[0], len(group) * N) for group in W2_GROUPS]
@@ -150,13 +149,14 @@ def tile_moe_pre_mlp_silu_kernel(tc, xT, w1, w2, gate, offs, pos1, pos2, out):
             gate_columns = held.tile([P, E - skipped], F32, name="gate_columns")
             nc.tensor.transpose(a_ps[0][:, 0, :], gate_square[:], identity[:])
             nc.vector.tensor_copy(gate_columns[:], a_ps[0][:, 0, skipped:E])
-            warm = held.tile([P, 1], F32, name="warm")
-            nc.scalar.activation(warm[:], gate_columns[:, 0:1], SILU)
             for n in range(1, len(RUNS)):
                 lo, hi = RUNS[n]
                 for e in range(lo // C, hi // C):
                     nc.tensor.transpose(y_ps[n][:, e * C - lo:(e + 1) * C - lo],
                                         gate_columns[:, e - skipped:e - skipped + 1].to_broadcast([P, P]), identity[:])
+                if n == 1:
+                    warm = held.tile([P, 1], F32, name="warm")
+                    nc.scalar.activation(warm[:], y_ps[n][:, 0:1], SILU)
                 nc.scalar.copy(gate_sb[n][:], y_ps[n][:])
 
         def gather_x(n, j):
@@ -165,8 +165,8 @@ def tile_moe_pre_mlp_silu_kernel(tc, xT, w1, w2, gate, offs, pos1, pos2, out):
             nc.vector.tensor_tensor(picked[n][:, j, :], tokens, gate_sb[n][:], MULT)
 
         def round_x(n):
-            nc.vector.tensor_copy(x_bf[n].rearrange("p (c i j) -> p c j i", i=STEP, j=PACK),
-                                  picked[n][:].rearrange("p j (c i) -> p c j i", i=STEP))
+            copy(n > 0, x_bf[n].rearrange("p (c i j) -> p c j i", i=STEP, j=PACK),
+                 picked[n][:].rearrange("p j (c i) -> p c j i", i=STEP))
 
         def quantize_x(n):
             quantize(x_codes[n][:], x_scales[n][:], x_bf[n])
@@ -201,7 +201,7 @@ def tile_moe_pre_mlp_silu_kernel(tc, xT, w1, w2, gate, offs, pos1, pos2, out):
 
         def round_w2(n):
             size = len(W2_GROUPS[n])
-            copy(n in (2, 3, 5),
+            copy(n % 2 == 1,
                  w2_bf[n][:].rearrange("p (e c i j) -> p e c j i", e=size, i=STEP, j=PACK),
                  w2_raw[n][:].rearrange("p e j (c i) -> p e c j i", i=STEP))
 
@@ -219,21 +219,20 @@ def tile_moe_pre_mlp_silu_kernel(tc, xT, w1, w2, gate, offs, pos1, pos2, out):
                                     rhs_scale=h_scales[e // 2][:, part([e], C)], start=True, stop=True)
 
         spread_gate()
-        for j in range(PACK - 1):
-            for n in range(len(RUNS)):
+        for n in range(len(RUNS)):
+            for j in range(PACK):
                 gather_x(n, j)
-        gather_x(0, PACK - 1)
-        gather_x(1, PACK - 1)
-        round_x(0)
-        round_x(1)
-        quantize_x(0)
-        gather_x(LAST_RUN, PACK - 1)
-        quantize_x(1)
+                if n > 0 and j == 0 and n - 1 > 0:
+                    round_x(n - 1)
+                if n > 0 and j == 1:
+                    quantize_x(n - 1)
+            if n == 0:
+                round_x(n)
 
         waiting = []
         for e in range(E - 1):
             round_w1(e)
-            for q in range(PAIRS - 1):
+            for q in range(PAIRS - 2):
                 if silu_after(q) == e:
                     activate(2 * q)
                     activate(2 * q + 1)
@@ -244,14 +243,10 @@ def tile_moe_pre_mlp_silu_kernel(tc, xT, w1, w2, gate, offs, pos1, pos2, out):
                 quantize_w1([e - 1, e])
                 first_product(e - 1)
                 first_product(e)
-            if e == FIRST_W2_AFTER:
-                round_w2(0)
-                quantize_w2(0)
             if e == last_run_after:
                 round_x(LAST_RUN)
                 quantize_h(pair(waiting.pop(0)))
                 quantize_x(LAST_RUN)
-                second_product(0)
 
         round_w1(E - 1)
         w1_codes[PAIRS - 1] = words("w1_codes_last", 2 * H, tag="w1_raw%d" % (E - 1))
@@ -259,22 +254,28 @@ def tile_moe_pre_mlp_silu_kernel(tc, xT, w1, w2, gate, offs, pos1, pos2, out):
             quantize_w1([e])
             first_product(e)
         h_codes[PAIRS - 2] = words("h_codes_late", 2 * C, tag="w1_bf%d" % ((PAIRS - 1) % RING))
+        round_w2(0)
+        activate(E - 4)
+        activate(E - 3)
         round_w2(1)
+        quantize_w2(0)
+        quantize_w2(1)
+        second_product(0)
+        second_product(1)
+        round_w2(2)
         activate(E - 2)
         activate(E - 1)
         quantize_h(pair(PAIRS - 2))
-        round_w2(2)
-        quantize_w2(1)
-        second_product(1)
         round_w2(3)
         quantize_w2(2)
-        quantize_h(pair(PAIRS - 1))
         quantize_w2(3)
         round_w2(4)
         round_w2(5)
-        for n in (4, 5):
+        h_codes[PAIRS - 1] = words("h_codes_last", 2 * C, tag="w2_raw%d" % (E - 1))
+        quantize_h(pair(PAIRS - 1))
+        for n in (5, 4):
             quantize_w2(n)
-        for n in (2, 3, 4, 5):
+        for n in (2, 3, 5, 4):
             second_product(n)
 
         y_all = held.tile([P, S], F32, name="y_all", tag="w2_raw%d" % (E - 2), align_bytes=64)

@@ -50,9 +50,13 @@ def tile_moe_pre_mlp_silu_kernel(tc, xT, w1, w2, gate, offs, pos1, pos2, out):
         pos2_sb = held.tile([P, T // PER_COLUMN], U16, name="pos2_sb")
         x_rows = [held.tile([P, T], F32, name="x_rows%d" % j) for j in range(PACK)]
         gate_sb = [held.tile([P, hi - lo], F32, name="gate%d" % lo) for lo, hi in RUNS]
-        gate_square = held.tile([P, P], F32, name="gate_square")
-        w1_raw = [held.tile([P, PACK, H], F32, name="w1_raw%d" % e, tag="w1_raw%d" % e, align_bytes=64)
-                  for e in range(E)]
+        gate_few = {n: held.tile([P, PACK], F32, name="gate_few%d" % n) for n in range(1, len(RUNS))}
+        shared = held.tile([P, 2 * BANK + 2 * PACK * H], F32, name="shared", align_bytes=64)
+        w1_raw = {e: held.tile([P, PACK, H], F32, name="w1_raw%d" % e, tag="w1_raw%d" % e, align_bytes=64)[:]
+                  for e in range(E) if e not in (1, 3)}
+        for n, e in enumerate((1, 3)):
+            start = 2 * BANK + n * PACK * H
+            w1_raw[e] = shared[:, start:start + PACK * H].rearrange("p (j c) -> p j c", j=PACK)
         w2_raw = [held.tile([P, len(group), PACK, N], F32, name="w2_raw%d" % group[0], tag="w2_raw%d" % group[0],
                             align_bytes=64)
                   for group in W2_GROUPS]
@@ -63,14 +67,15 @@ def tile_moe_pre_mlp_silu_kernel(tc, xT, w1, w2, gate, offs, pos1, pos2, out):
         def w2_behind(e):
             return [n for n in range(len(W2_GROUPS)) if E - 1 == e]
 
-        nc.scalar.dma_start(gate_square[:], gate.rearrange("k (e c) -> (k e) c", c=C)[0:P, :])
+        nc.scalar.dma_start(gate_sb[0][:], gate[0:P, RUNS[0][0]:RUNS[0][1]])
+        for n in gate_few:
+            nc.scalar.dma_start(gate_few[n][:], gate[0, RUNS[n][0]:RUNS[n][1]].rearrange("(p r) -> p r", p=P))
         nc.sync.dma_start(offs_sb[:], offs)
         load_x(0)
-        nc.scalar.dma_start(gate_sb[0][:], gate[0:P, RUNS[0][0]:RUNS[0][1]])
         for j in range(1, PACK):
             load_x(j)
         for e in range(E):
-            nc.sync.dma_start(w1_raw[e][:], w1[e].rearrange("(p j) c -> p j c", j=PACK))
+            nc.sync.dma_start(w1_raw[e], w1[e].rearrange("(p j) c -> p j c", j=PACK))
             for n in w2_behind(e):
                 group = W2_GROUPS[n]
                 nc.sync.dma_start(w2_raw[n][:].rearrange("p e j n -> p e (j n)"),
@@ -89,27 +94,29 @@ def tile_moe_pre_mlp_silu_kernel(tc, xT, w1, w2, gate, offs, pos1, pos2, out):
             return held.tile([P, width], BF16, name=name, tag=name, align_bytes=64)
 
         def freed(e, start, width):
-            return w1_raw[e][:].rearrange("p j c -> p (j c)")[:, start // 2:(start + width) // 2].bitcast(BF16)
+            return w1_raw[e].rearrange("p j c -> p (j c)")[:, start // 2:(start + width) // 2].bitcast(BF16)
 
         def silu_after(q):
             return max(2 * q + 2, FIRST_SILU_AFTER)
 
-        picked = [held.tile([P, PACK, hi - lo], F32, name="picked%d" % lo) for lo, hi in RUNS]
+        picked = [held.tile([P, PACK, hi - lo], F32, name="picked%d" % lo)[:].rearrange("p (a b) c -> p a b c", a=2)
+                  for lo, hi in RUNS[:LAST_RUN]]
+        picked.append(shared[:].rearrange("p (a r) -> p a r", a=2)[:, :, 0:2 * BANK].rearrange("p a (b c) -> p a b c", b=2))
         x_bf = [rounded("x_bf%d" % lo, PACK * (hi - lo))[:] for lo, hi in RUNS[:LAST_RUN]]
         last_run_after = RUNS[LAST_RUN][0] // C - 1
         x_bf.append(freed(last_run_after, 0, PACK * BANK))
         h_width = 2 * PACK * C
-        h_bf = [freed(silu_after(q), q % 2 * h_width, h_width) for q in range(PAIRS - 2)]
-        h_bf.extend([w2_raw[n][:].rearrange("p e j n -> p (e j n)").bitcast(BF16)[:, 0:h_width] for n in (0, 2)])
+        h_bf = [freed(silu_after(q), q % 2 * h_width, h_width) for q in range(2)]
+        h_bf.extend([rounded("h_bf2", h_width)[:], freed(E - 2, 0, h_width), rounded("h_bf4", h_width)[:]])
         w1_bf = [rounded("w1_bf%d" % r, 2 * PACK * H) for r in range(RING)]
         w2_bf = [rounded("w2_bf%d" % group[0], len(group) * PACK * N) for group in W2_GROUPS]
         x_codes = [words("x_codes%d" % lo, hi - lo) for lo, hi in RUNS]
         x_scales = [scale_bytes("x_scales%d" % lo, hi - lo) for lo, hi in RUNS]
         w1_codes = {q: words("w1_codes%d" % q, 2 * H) for q in range(PAIRS - 1)}
         w1_scales = [scale_bytes("w1_scales%d" % q, 2 * H) for q in range(PAIRS)]
-        h_codes = {q: words("h_codes%d" % q, 2 * C) for q in range(PAIRS - 2)}
+        h_codes = {q: words("h_codes%d" % q, 2 * C) for q in range(PAIRS) if q != PAIRS - 2}
         h_scales = [scale_bytes("h_scales%d" % q, 2 * C) for q in range(PAIRS)]
-        w2_codes = [words("w2_codes%d" % group[0], len(group) * N) for group in W2_GROUPS]
+        w2_codes = {n: words("w2_codes%d" % group[0], len(group) * N) for n, group in enumerate(W2_GROUPS) if n != 3}
         w2_scales = [scale_bytes("w2_scales%d" % group[0], len(group) * N) for group in W2_GROUPS]
         a_ps = [psum.tile([P, PACK, C], F32, name="a_ps%d" % r) for r in range(A_BANKS)]
         y_ps = [psum.tile([P, BANK], F32, name="y_ps%d" % r) for r in range(len(Y_GROUPS))]
@@ -145,35 +152,33 @@ def tile_moe_pre_mlp_silu_kernel(tc, xT, w1, w2, gate, offs, pos1, pos2, out):
 
         def spread_gate():
             identity = build_identity()
-            skipped = RUNS[1][0] // C
-            gate_columns = held.tile([P, E - skipped], F32, name="gate_columns")
-            nc.tensor.transpose(a_ps[0][:, 0, :], gate_square[:], identity[:])
-            nc.vector.tensor_copy(gate_columns[:], a_ps[0][:, 0, skipped:E])
-            for n in range(1, len(RUNS)):
+            for n in gate_few:
                 lo, hi = RUNS[n]
-                for e in range(lo // C, hi // C):
-                    nc.tensor.transpose(y_ps[n][:, e * C - lo:(e + 1) * C - lo],
-                                        gate_columns[:, e - skipped:e - skipped + 1].to_broadcast([P, P]), identity[:])
+                few = (hi - lo) // P
+                for r in range(few):
+                    nc.tensor.transpose(y_ps[n][:, r * P:(r + 1) * P], gate_few[n][:, r:r + 1].to_broadcast([P, P]),
+                                        identity[:])
                 if n == 1:
                     warm = held.tile([P, 1], F32, name="warm")
                     nc.scalar.activation(warm[:], y_ps[n][:, 0:1], SILU)
-                nc.scalar.copy(gate_sb[n][:], y_ps[n][:])
+                copy(False, gate_sb[n][:].rearrange("k (p r) -> k p r", r=few),
+                     y_ps[n][:, 0:hi - lo].rearrange("k (r p) -> k p r", r=few))
 
         def gather_x(n, j):
             lo, hi = RUNS[n]
             tokens = x_rows[j][:].indirect(offs_sb[:, lo // PER_COLUMN:hi // PER_COLUMN])
-            nc.vector.tensor_tensor(picked[n][:, j, :], tokens, gate_sb[n][:], MULT)
+            nc.vector.tensor_tensor(picked[n][:, j // 2, j % 2, :], tokens, gate_sb[n][:], MULT)
 
         def round_x(n):
-            copy(n > 0, x_bf[n].rearrange("p (c i j) -> p c j i", i=STEP, j=PACK),
-                 picked[n][:].rearrange("p j (c i) -> p c j i", i=STEP))
+            copy(n > 0, x_bf[n].rearrange("p (c i a b) -> p c a b i", i=STEP, a=2, b=2),
+                 picked[n].rearrange("p a b (c i) -> p c a b i", i=STEP))
 
         def quantize_x(n):
             quantize(x_codes[n][:], x_scales[n][:], x_bf[n])
 
         def round_w1(e):
             dst = w1_bf[e // 2 % RING][:, part([e], PACK * H)].rearrange("p (u v m j) -> p u m j v", u=2, v=2, j=PACK)
-            copy(e % 2 == 1 and e >= VECTOR_FROM, dst, w1_raw[e][:].rearrange("p j (m u v) -> p u m j v", u=2, v=2))
+            copy(e % 2 == 1 and e >= VECTOR_FROM, dst, w1_raw[e].rearrange("p j (m u v) -> p u m j v", u=2, v=2))
 
         def quantize_w1(experts):
             q = experts[0] // 2
@@ -201,7 +206,7 @@ def tile_moe_pre_mlp_silu_kernel(tc, xT, w1, w2, gate, offs, pos1, pos2, out):
 
         def round_w2(n):
             size = len(W2_GROUPS[n])
-            copy(n % 2 == 1,
+            copy(n in (1, 2, 5),
                  w2_bf[n][:].rearrange("p (e c i j) -> p e c j i", e=size, i=STEP, j=PACK),
                  w2_raw[n][:].rearrange("p e j (c i) -> p e c j i", i=STEP))
 
@@ -220,7 +225,7 @@ def tile_moe_pre_mlp_silu_kernel(tc, xT, w1, w2, gate, offs, pos1, pos2, out):
 
         spread_gate()
         for n in range(len(RUNS)):
-            for j in range(PACK):
+            for j in range(PACK if n < LAST_RUN else 2):
                 gather_x(n, j)
                 if n > 0 and j == 0 and n - 1 > 0:
                     round_x(n - 1)
@@ -232,7 +237,10 @@ def tile_moe_pre_mlp_silu_kernel(tc, xT, w1, w2, gate, offs, pos1, pos2, out):
         waiting = []
         for e in range(E - 1):
             round_w1(e)
-            for q in range(PAIRS - 2):
+            if e == 6:
+                quantize_w1([e])
+                first_product(e)
+            for q in range(PAIRS - 1):
                 if silu_after(q) == e:
                     activate(2 * q)
                     activate(2 * q + 1)
@@ -240,9 +248,14 @@ def tile_moe_pre_mlp_silu_kernel(tc, xT, w1, w2, gate, offs, pos1, pos2, out):
             if e % 2 == 1:
                 if waiting:
                     quantize_h(pair(waiting.pop(0)))
-                quantize_w1([e - 1, e])
-                first_product(e - 1)
+                if e == 7:
+                    quantize_w1([e])
+                else:
+                    quantize_w1([e - 1, e])
+                    first_product(e - 1)
                 first_product(e)
+                if e < PACK:
+                    gather_x(LAST_RUN, 2 + e // 2)
             if e == last_run_after:
                 round_x(LAST_RUN)
                 quantize_h(pair(waiting.pop(0)))
@@ -253,27 +266,24 @@ def tile_moe_pre_mlp_silu_kernel(tc, xT, w1, w2, gate, offs, pos1, pos2, out):
         for e in (E - 2, E - 1):
             quantize_w1([e])
             first_product(e)
-        h_codes[PAIRS - 2] = words("h_codes_late", 2 * C, tag="w1_bf%d" % ((PAIRS - 1) % RING))
         round_w2(0)
-        activate(E - 4)
-        activate(E - 3)
+        activate(E - 2)
+        activate(E - 1)
+        h_codes[PAIRS - 2] = words("h_codes_late", 2 * C, tag="w1_bf%d" % ((PAIRS - 1) % RING))
         round_w2(1)
+        quantize_h(pair(PAIRS - 2))
         quantize_w2(0)
         quantize_w2(1)
         second_product(0)
         second_product(1)
         round_w2(2)
-        activate(E - 2)
-        activate(E - 1)
-        quantize_h(pair(PAIRS - 2))
-        round_w2(3)
+        quantize_h(pair(PAIRS - 1))
         quantize_w2(2)
-        quantize_w2(3)
+        round_w2(3)
         round_w2(4)
         round_w2(5)
-        h_codes[PAIRS - 1] = words("h_codes_last", 2 * C, tag="w2_raw%d" % (E - 1))
-        quantize_h(pair(PAIRS - 1))
-        for n in (5, 4):
+        w2_codes[3] = words("w2_codes_late", 2 * N, tag="w2_raw%d" % (E - 1))
+        for n in (3, 5, 4):
             quantize_w2(n)
         for n in (2, 3, 5, 4):
             second_product(n)

@@ -170,8 +170,11 @@ def tile_moe_pre_mlp_silu_kernel(tc, xT, w1, w2, gate, offs, pos1, pos2, out):
             nc.vector.tensor_tensor(picked[n][:, j // 2, j % 2, :], tokens, gate_sb[n][:], MULT)
 
         def round_x(n):
-            copy(n > 0, x_bf[n].rearrange("p (c i a b) -> p c a b i", i=STEP, a=2, b=2),
-                 picked[n].rearrange("p a b (c i) -> p c a b i", i=STEP))
+            count = RUNS[n][1] - RUNS[n][0]
+            shares = [(False, 0, count // 2), (True, count // 2, count)] if n == LAST_RUN else [(n > 0, 0, count)]
+            for on_vector, lo, hi in shares:
+                copy(on_vector, x_bf[n][:, PACK * lo:PACK * hi].rearrange("p (c i a b) -> p c a b i", i=STEP, a=2, b=2),
+                     picked[n][:, :, :, lo:hi].rearrange("p a b (c i) -> p c a b i", i=STEP))
 
         def quantize_x(n):
             quantize(x_codes[n][:], x_scales[n][:], x_bf[n])
@@ -288,7 +291,7 @@ def tile_moe_pre_mlp_silu_kernel(tc, xT, w1, w2, gate, offs, pos1, pos2, out):
         for n in (2, 3, 5, 4):
             second_product(n)
 
-        y_all = held.tile([P, S], F32, name="y_all", tag="w2_raw%d" % (E - 2), align_bytes=64)
+        y_all = held.tile([P, S], F32, name="y_all", tag="w2_raw%d" % (E - 4), align_bytes=64)
         for b, group in enumerate(Y_GROUPS):
             copy(b == len(Y_GROUPS) - 1, y_all[:, group[0] * C:(group[-1] + 1) * C], y_ps[b][:, 0:len(group) * C])
 

@@ -26,15 +26,18 @@ EQUAL = mybir.AluOpType.is_equal
 SILU = mybir.ActivationFunctionType.Silu
 
 RUNS = ((0, 2 * C), (2 * C, 2 * C + BANK), (2 * C + BANK, S))
-LAST_RUN = len(RUNS) - 1
+FIRST_RUN, MIDDLE_RUN, LAST_RUN = range(len(RUNS))
 W2_GROUPS = tuple((2 * q, 2 * q + 1) for q in range(PAIRS - 1)) + ((E - 2,), (E - 1,))
 Y_GROUPS = tuple(tuple(range(e, min(e + BANK // C, E))) for e in range(0, E, BANK // C))
-OUT_PARTS = ((0, 384), (384, T))
+HALVES = ((0, T // 2), (T // 2, T))
+OUT_PARTS = ((0, 256), (256, 512), (512, T))
 
 VECTOR_FROM = 5
 FIRST_SILU_AFTER = 4
-FIRST_W2_AFTER = 3
-W2_EVERY = 4
+SINGLY_FROM = 6
+HOSTS = (1, 3)
+SCALAR_SLOTS = C
+W2_ON_SCALAR = (0, 3, 4)
 RING = 3
 A_BANKS = 4
 
@@ -50,37 +53,28 @@ def tile_moe_pre_mlp_silu_kernel(tc, xT, w1, w2, gate, offs, pos1, pos2, out):
         pos2_sb = held.tile([P, T // PER_COLUMN], U16, name="pos2_sb")
         x_rows = [held.tile([P, T], F32, name="x_rows%d" % j) for j in range(PACK)]
         gate_sb = [held.tile([P, hi - lo], F32, name="gate%d" % lo) for lo, hi in RUNS]
-        gate_few = {n: held.tile([P, PACK], F32, name="gate_few%d" % n) for n in range(1, len(RUNS))}
+        gate_few = {n: held.tile([P, BANK // P], F32, name="gate_few%d" % n) for n in (MIDDLE_RUN, LAST_RUN)}
         shared = held.tile([P, 2 * BANK + 2 * PACK * H], F32, name="shared", align_bytes=64)
         w1_raw = {e: held.tile([P, PACK, H], F32, name="w1_raw%d" % e, tag="w1_raw%d" % e, align_bytes=64)[:]
-                  for e in range(E) if e not in (1, 3)}
-        for n, e in enumerate((1, 3)):
+                  for e in range(E) if e not in HOSTS}
+        for n, e in enumerate(HOSTS):
             start = 2 * BANK + n * PACK * H
             w1_raw[e] = shared[:, start:start + PACK * H].rearrange("p (j c) -> p j c", j=PACK)
         w2_raw = [held.tile([P, len(group), PACK, N], F32, name="w2_raw%d" % group[0], tag="w2_raw%d" % group[0],
                             align_bytes=64)
                   for group in W2_GROUPS]
 
-        def load_x(j):
-            nc.sync.dma_start(x_rows[j][:], xT.rearrange("(p j) t -> p j t", j=PACK)[:, j, :])
-
-        def w2_behind(e):
-            return [n for n in range(len(W2_GROUPS)) if E - 1 == e]
-
-        nc.scalar.dma_start(gate_sb[0][:], gate[0:P, RUNS[0][0]:RUNS[0][1]])
+        nc.scalar.dma_start(gate_sb[FIRST_RUN][:], gate[0:P, RUNS[FIRST_RUN][0]:RUNS[FIRST_RUN][1]])
         for n in gate_few:
             nc.scalar.dma_start(gate_few[n][:], gate[0, RUNS[n][0]:RUNS[n][1]].rearrange("(p r) -> p r", p=P))
         nc.sync.dma_start(offs_sb[:], offs)
-        load_x(0)
-        for j in range(1, PACK):
-            load_x(j)
+        for j in range(PACK):
+            nc.sync.dma_start(x_rows[j][:], xT.rearrange("(p j) t -> p j t", j=PACK)[:, j, :])
         for e in range(E):
             nc.sync.dma_start(w1_raw[e], w1[e].rearrange("(p j) c -> p j c", j=PACK))
-            for n in w2_behind(e):
-                group = W2_GROUPS[n]
-                nc.sync.dma_start(w2_raw[n][:].rearrange("p e j n -> p e (j n)"),
-                                  w2[group[0]:group[-1] + 1].rearrange("e (p j) n -> p e (j n)", j=PACK))
-
+        for n, group in enumerate(W2_GROUPS):
+            nc.sync.dma_start(w2_raw[n][:].rearrange("p e j n -> p e (j n)"),
+                              w2[group[0]:group[-1] + 1].rearrange("e (p j) n -> p e (j n)", j=PACK))
         nc.sync.dma_start(pos1_sb[:], pos1)
         nc.sync.dma_start(pos2_sb[:], pos2)
 
@@ -101,13 +95,14 @@ def tile_moe_pre_mlp_silu_kernel(tc, xT, w1, w2, gate, offs, pos1, pos2, out):
 
         picked = [held.tile([P, PACK, hi - lo], F32, name="picked%d" % lo)[:].rearrange("p (a b) c -> p a b c", a=2)
                   for lo, hi in RUNS[:LAST_RUN]]
-        picked.append(shared[:].rearrange("p (a r) -> p a r", a=2)[:, :, 0:2 * BANK].rearrange("p a (b c) -> p a b c", b=2))
+        halves = shared[:].rearrange("p (a r) -> p a r", a=2)
+        picked.append(halves[:, :, 0:2 * BANK].rearrange("p a (b c) -> p a b c", b=2))
         x_bf = [rounded("x_bf%d" % lo, PACK * (hi - lo))[:] for lo, hi in RUNS[:LAST_RUN]]
         last_run_after = RUNS[LAST_RUN][0] // C - 1
         x_bf.append(freed(last_run_after, 0, PACK * BANK))
         h_width = 2 * PACK * C
-        h_bf = [freed(silu_after(q), q % 2 * h_width, h_width) for q in range(2)]
-        h_bf.extend([rounded("h_bf2", h_width)[:], freed(E - 2, 0, h_width), rounded("h_bf4", h_width)[:]])
+        h_bf = [freed(silu_after(0), 0, h_width), freed(silu_after(1), h_width, h_width), rounded("h_bf2", h_width)[:],
+                freed(silu_after(3), 0, h_width), rounded("h_bf4", h_width)[:]]
         w1_bf = [rounded("w1_bf%d" % r, 2 * PACK * H) for r in range(RING)]
         w2_bf = [rounded("w2_bf%d" % group[0], len(group) * PACK * N) for group in W2_GROUPS]
         x_codes = [words("x_codes%d" % lo, hi - lo) for lo, hi in RUNS]
@@ -116,7 +111,7 @@ def tile_moe_pre_mlp_silu_kernel(tc, xT, w1, w2, gate, offs, pos1, pos2, out):
         w1_scales = [scale_bytes("w1_scales%d" % q, 2 * H) for q in range(PAIRS)]
         h_codes = {q: words("h_codes%d" % q, 2 * C) for q in range(PAIRS) if q != PAIRS - 2}
         h_scales = [scale_bytes("h_scales%d" % q, 2 * C) for q in range(PAIRS)]
-        w2_codes = {n: words("w2_codes%d" % group[0], len(group) * N) for n, group in enumerate(W2_GROUPS) if n != 3}
+        w2_codes = [words("w2_codes%d" % group[0], len(group) * N) for group in W2_GROUPS]
         w2_scales = [scale_bytes("w2_scales%d" % group[0], len(group) * N) for group in W2_GROUPS]
         a_ps = [psum.tile([P, PACK, C], F32, name="a_ps%d" % r) for r in range(A_BANKS)]
         y_ps = [psum.tile([P, BANK], F32, name="y_ps%d" % r) for r in range(len(Y_GROUPS))]
@@ -132,9 +127,6 @@ def tile_moe_pre_mlp_silu_kernel(tc, xT, w1, w2, gate, offs, pos1, pos2, out):
 
         def part(experts, width):
             return slice(experts[0] % 2 * width, (experts[-1] % 2 + 1) * width)
-
-        def pair(q):
-            return [2 * q, 2 * q + 1]
 
         def build_identity():
             ones = held.tile([P, P], F32, name="ones")
@@ -153,28 +145,23 @@ def tile_moe_pre_mlp_silu_kernel(tc, xT, w1, w2, gate, offs, pos1, pos2, out):
         def spread_gate():
             identity = build_identity()
             for n in gate_few:
-                lo, hi = RUNS[n]
-                few = (hi - lo) // P
-                for r in range(few):
+                for r in range(BANK // P):
                     nc.tensor.transpose(y_ps[n][:, r * P:(r + 1) * P], gate_few[n][:, r:r + 1].to_broadcast([P, P]),
                                         identity[:])
-                if n == 1:
+                if n == MIDDLE_RUN:
                     warm = held.tile([P, 1], F32, name="warm")
                     nc.scalar.activation(warm[:], y_ps[n][:, 0:1], SILU)
-                copy(False, gate_sb[n][:].rearrange("k (p r) -> k p r", r=few),
-                     y_ps[n][:, 0:hi - lo].rearrange("k (r p) -> k p r", r=few))
+                nc.scalar.copy(gate_sb[n][:].rearrange("k (p r) -> k p r", p=P),
+                               y_ps[n][:].rearrange("k (r p) -> k p r", p=P))
 
         def gather_x(n, j):
             lo, hi = RUNS[n]
             tokens = x_rows[j][:].indirect(offs_sb[:, lo // PER_COLUMN:hi // PER_COLUMN])
             nc.vector.tensor_tensor(picked[n][:, j // 2, j % 2, :], tokens, gate_sb[n][:], MULT)
 
-        def round_x(n):
-            count = RUNS[n][1] - RUNS[n][0]
-            shares = [(False, 0, count // 2), (True, count // 2, count)] if n == LAST_RUN else [(n > 0, 0, count)]
-            for on_vector, lo, hi in shares:
-                copy(on_vector, x_bf[n][:, PACK * lo:PACK * hi].rearrange("p (c i a b) -> p c a b i", i=STEP, a=2, b=2),
-                     picked[n][:, :, :, lo:hi].rearrange("p a b (c i) -> p c a b i", i=STEP))
+        def round_x(on_vector, n, lo, hi):
+            copy(on_vector, x_bf[n][:, PACK * lo:PACK * hi].rearrange("p (c i a b) -> p c a b i", i=STEP, a=2, b=2),
+                 picked[n][:, :, :, lo:hi].rearrange("p a b (c i) -> p c a b i", i=STEP))
 
         def quantize_x(n):
             quantize(x_codes[n][:], x_scales[n][:], x_bf[n])
@@ -183,34 +170,30 @@ def tile_moe_pre_mlp_silu_kernel(tc, xT, w1, w2, gate, offs, pos1, pos2, out):
             dst = w1_bf[e // 2 % RING][:, part([e], PACK * H)].rearrange("p (u v m j) -> p u m j v", u=2, v=2, j=PACK)
             copy(e % 2 == 1 and e >= VECTOR_FROM, dst, w1_raw[e].rearrange("p j (m u v) -> p u m j v", u=2, v=2))
 
-        def quantize_w1(experts):
+        def first_product(experts):
             q = experts[0] // 2
             quantize(w1_codes[q][:, part(experts, H)], w1_scales[q][:, part(experts, H)],
                      w1_bf[q % RING][:, part(experts, PACK * H)])
+            for e in experts:
+                n = max(m for m, (lo, hi) in enumerate(RUNS) if lo <= e * C)
+                slots = slice(e * C - RUNS[n][0], (e + 1) * C - RUNS[n][0])
+                for t in range(PACK):
+                    cols = slice(e % 2 * H + t * P, e % 2 * H + (t + 1) * P)
+                    nc.tensor.matmul_mx(out=a_ps[e % A_BANKS][:, t, :], lhsT=w1_codes[q][:, cols].bitcast(FP8X4),
+                                        lhsT_scale=w1_scales[q][:, cols], rhs=x_codes[n][:, slots].bitcast(FP8X4),
+                                        rhs_scale=x_scales[n][:, slots], start=True, stop=True)
 
-        def first_product(e):
-            n = max(m for m, (lo, hi) in enumerate(RUNS) if lo <= e * C)
-            slots = slice(e * C - RUNS[n][0], (e + 1) * C - RUNS[n][0])
-            for t in range(PACK):
-                cols = slice(e % 2 * H + t * P, e % 2 * H + (t + 1) * P)
-                nc.tensor.matmul_mx(out=a_ps[e % A_BANKS][:, t, :], lhsT=w1_codes[e // 2][:, cols].bitcast(FP8X4),
-                                    lhsT_scale=w1_scales[e // 2][:, cols],
-                                    rhs=x_codes[n][:, slots].bitcast(FP8X4),
-                                    rhs_scale=x_scales[n][:, slots], start=True, stop=True)
+        def activate(q):
+            for e in (2 * q, 2 * q + 1):
+                nc.scalar.activation(h_bf[q][:, part([e], PACK * C)].rearrange("p (c t) -> p c t", t=PACK),
+                                     a_ps[e % A_BANKS][:].rearrange("p t c -> p c t"), SILU)
 
-        def activate(e):
-            nc.scalar.activation(h_bf[e // 2][:, part([e], PACK * C)].rearrange("p (c t) -> p c t", t=PACK),
-                                 a_ps[e % A_BANKS][:].rearrange("p t c -> p c t"), SILU)
-
-        def quantize_h(experts):
-            q = experts[0] // 2
-            quantize(h_codes[q][:, part(experts, C)], h_scales[q][:, part(experts, C)],
-                     h_bf[q][:, part(experts, PACK * C)])
+        def quantize_h(q):
+            quantize(h_codes[q][:], h_scales[q][:], h_bf[q])
 
         def round_w2(n):
             size = len(W2_GROUPS[n])
-            copy(n in (1, 2, 5),
-                 w2_bf[n][:].rearrange("p (e c i j) -> p e c j i", e=size, i=STEP, j=PACK),
+            copy(n not in W2_ON_SCALAR, w2_bf[n][:].rearrange("p (e c i j) -> p e c j i", e=size, i=STEP, j=PACK),
                  w2_raw[n][:].rearrange("p e j (c i) -> p e c j i", i=STEP))
 
         def quantize_w2(n):
@@ -227,79 +210,74 @@ def tile_moe_pre_mlp_silu_kernel(tc, xT, w1, w2, gate, offs, pos1, pos2, out):
                                     rhs_scale=h_scales[e // 2][:, part([e], C)], start=True, stop=True)
 
         spread_gate()
-        for n in range(len(RUNS)):
-            for j in range(PACK if n < LAST_RUN else 2):
-                gather_x(n, j)
-                if n > 0 and j == 0 and n - 1 > 0:
-                    round_x(n - 1)
-                if n > 0 and j == 1:
-                    quantize_x(n - 1)
-            if n == 0:
-                round_x(n)
+        for j in range(PACK):
+            gather_x(FIRST_RUN, j)
+        round_x(False, FIRST_RUN, 0, 2 * C)
+        for j in range(PACK):
+            gather_x(MIDDLE_RUN, j)
+            if j == 1:
+                quantize_x(FIRST_RUN)
+        gather_x(LAST_RUN, 0)
+        round_x(True, MIDDLE_RUN, 0, BANK)
+        gather_x(LAST_RUN, 1)
+        quantize_x(MIDDLE_RUN)
 
         waiting = []
         for e in range(E - 1):
             round_w1(e)
-            if e == 6:
-                quantize_w1([e])
-                first_product(e)
+            if e == SINGLY_FROM:
+                first_product([e])
             for q in range(PAIRS - 1):
                 if silu_after(q) == e:
-                    activate(2 * q)
-                    activate(2 * q + 1)
+                    activate(q)
                     waiting.append(q)
             if e % 2 == 1:
                 if waiting:
-                    quantize_h(pair(waiting.pop(0)))
-                if e == 7:
-                    quantize_w1([e])
-                else:
-                    quantize_w1([e - 1, e])
-                    first_product(e - 1)
-                first_product(e)
-                if e < PACK:
-                    gather_x(LAST_RUN, 2 + e // 2)
+                    quantize_h(waiting.pop(0))
+                first_product([e - 1, e] if e < SINGLY_FROM else [e])
+            if e in HOSTS:
+                gather_x(LAST_RUN, 2 + HOSTS.index(e))
             if e == last_run_after:
-                round_x(LAST_RUN)
-                quantize_h(pair(waiting.pop(0)))
+                round_x(False, LAST_RUN, 0, SCALAR_SLOTS)
+                round_x(True, LAST_RUN, SCALAR_SLOTS, BANK)
+                quantize_h(waiting.pop(0))
                 quantize_x(LAST_RUN)
 
         round_w1(E - 1)
         w1_codes[PAIRS - 1] = words("w1_codes_last", 2 * H, tag="w1_raw%d" % (E - 1))
-        for e in (E - 2, E - 1):
-            quantize_w1([e])
-            first_product(e)
+        first_product([E - 2])
+        first_product([E - 1])
         round_w2(0)
-        activate(E - 2)
-        activate(E - 1)
+        activate(PAIRS - 1)
         h_codes[PAIRS - 2] = words("h_codes_late", 2 * C, tag="w1_bf%d" % ((PAIRS - 1) % RING))
+
         round_w2(1)
-        quantize_h(pair(PAIRS - 2))
-        quantize_w2(0)
-        quantize_w2(1)
-        second_product(0)
-        second_product(1)
-        round_w2(2)
-        quantize_h(pair(PAIRS - 1))
-        quantize_w2(2)
-        round_w2(3)
-        round_w2(4)
-        round_w2(5)
-        w2_codes[3] = words("w2_codes_late", 2 * N, tag="w2_raw%d" % (E - 1))
-        for n in (3, 5, 4):
+        quantize_h(PAIRS - 2)
+        for n in (0, 1):
             quantize_w2(n)
-        for n in (2, 3, 5, 4):
+        for n in (0, 1):
+            second_product(n)
+        round_w2(2)
+        quantize_h(PAIRS - 1)
+        quantize_w2(2)
+        rest = range(3, len(W2_GROUPS))
+        for n in rest:
+            round_w2(n)
+        for n in rest:
+            quantize_w2(n)
+        second_product(2)
+        for n in rest:
             second_product(n)
 
         y_all = held.tile([P, S], F32, name="y_all", tag="w2_raw%d" % (E - 4), align_bytes=64)
         for b, group in enumerate(Y_GROUPS):
             copy(b == len(Y_GROUPS) - 1, y_all[:, group[0] * C:(group[-1] + 1) * C], y_ps[b][:, 0:len(group) * C])
 
-        first = [held.tile([P, hi - lo], F32, name="first%d" % lo) for lo, hi in OUT_PARTS]
+        first = held.tile([P, T], F32, name="first")
         total = [held.tile([P, hi - lo], F32, name="total%d" % lo) for lo, hi in OUT_PARTS]
-        for n, (lo, hi) in enumerate(OUT_PARTS):
-            nc.vector.tensor_copy(first[n][:], y_all[:].indirect(pos1_sb[:, lo // PER_COLUMN:hi // PER_COLUMN]))
+        for lo, hi in HALVES:
+            nc.vector.tensor_copy(first[:, lo:hi], y_all[:].indirect(pos1_sb[:, lo // PER_COLUMN:hi // PER_COLUMN]))
         for n, (lo, hi) in enumerate(OUT_PARTS):
             nc.vector.tensor_tensor(total[n][:], y_all[:].indirect(pos2_sb[:, lo // PER_COLUMN:hi // PER_COLUMN]),
-                                    first[n][:], ADD)
+                                    first[:, lo:hi], ADD)
             nc.sync.dma_start(out[:, lo:hi], total[n][:])

@@ -23,13 +23,14 @@ FP8X4 = mybir.dt.float8_e4m3fn_x4
 MULT = mybir.AluOpType.mult
 ADD = mybir.AluOpType.add
 EQUAL = mybir.AluOpType.is_equal
+COPY = mybir.ActivationFunctionType.Copy
 SILU = mybir.ActivationFunctionType.Silu
 
 RUNS = ((0, 2 * C), (2 * C, 2 * C + BANK), (2 * C + BANK, S))
 FIRST_RUN, MIDDLE_RUN, LAST_RUN = range(len(RUNS))
 W2_GROUPS = tuple((2 * q, 2 * q + 1) for q in range(PAIRS - 1)) + ((E - 2,), (E - 1,))
 Y_GROUPS = tuple(tuple(range(e, min(e + BANK // C, E))) for e in range(0, E, BANK // C))
-HALVES = ((0, T // 2), (T // 2, T))
+PIECE = 128
 OUT_PARTS = ((0, 256), (256, 512), (512, T))
 
 VECTOR_FROM = 5
@@ -274,10 +275,11 @@ def tile_moe_pre_mlp_silu_kernel(tc, xT, w1, w2, gate, offs, pos1, pos2, out):
             copy(b == len(Y_GROUPS) - 1, y_all[:, group[0] * C:(group[-1] + 1) * C], y_ps[b][:, 0:len(group) * C])
 
         first = held.tile([P, T], F32, name="first")
-        total = [held.tile([P, hi - lo], F32, name="total%d" % lo) for lo, hi in OUT_PARTS]
-        for lo, hi in HALVES:
-            nc.vector.tensor_copy(first[:, lo:hi], y_all[:].indirect(pos1_sb[:, lo // PER_COLUMN:hi // PER_COLUMN]))
-        for n, (lo, hi) in enumerate(OUT_PARTS):
-            nc.vector.tensor_tensor(total[n][:], y_all[:].indirect(pos2_sb[:, lo // PER_COLUMN:hi // PER_COLUMN]),
-                                    first[:, lo:hi], ADD)
-            nc.sync.dma_start(out[:, lo:hi], total[n][:])
+        total = held.tile([P, T], F32, name="total")
+        for lo in range(0, T, PIECE):
+            cols = slice(lo // PER_COLUMN, (lo + PIECE) // PER_COLUMN)
+            nc.scalar.activation(first[:, lo:lo + PIECE], y_all[:].indirect(pos1_sb[:, cols]), COPY)
+            nc.vector.tensor_tensor(total[:, lo:lo + PIECE], y_all[:].indirect(pos2_sb[:, cols]),
+                                    first[:, lo:lo + PIECE], ADD)
+        for lo, hi in OUT_PARTS:
+            nc.sync.dma_start(out[:, lo:hi], total[:, lo:hi])

@@ -29,16 +29,13 @@ SILU = mybir.ActivationFunctionType.Silu
 RUNS = ((0, 2 * C), (2 * C, 2 * C + BANK), (2 * C + BANK, S))
 FIRST_RUN, MIDDLE_RUN, LAST_RUN = range(len(RUNS))
 W2_GROUPS = tuple((2 * q, 2 * q + 1) for q in range(PAIRS - 1)) + ((E - 2,), (E - 1,))
-Y_GROUPS = tuple(tuple(range(e, min(e + BANK // C, E))) for e in range(0, E, BANK // C))
+Y_GROUPS = ((0, 1, 2, 3), (4, 5), (6, 7), (8, 9))
 PIECE = 128
 OUT_PARTS = ((0, 256), (256, 512), (512, T))
 
-VECTOR_FROM = 5
-FIRST_SILU_AFTER = 4
-SINGLY_FROM = 6
-HOSTS = (1, 3)
-SCALAR_SLOTS = C
 W2_ON_SCALAR = (0, 3, 4)
+HOSTS = (5,)
+FIRST_W2_AFTER = 9
 RING = 3
 A_BANKS = 4
 
@@ -53,29 +50,35 @@ def tile_moe_pre_mlp_silu_kernel(tc, xT, w1, w2, gate, offs, pos1, pos2, out):
         pos1_sb = held.tile([P, T // PER_COLUMN], U16, name="pos1_sb")
         pos2_sb = held.tile([P, T // PER_COLUMN], U16, name="pos2_sb")
         x_rows = [held.tile([P, T], F32, name="x_rows%d" % j) for j in range(PACK)]
-        gate_sb = [held.tile([P, hi - lo], F32, name="gate%d" % lo) for lo, hi in RUNS]
+        gate_first = held.tile([P, 2 * C], F32, name="gate_first")
         gate_few = {n: held.tile([P, BANK // P], F32, name="gate_few%d" % n) for n in (MIDDLE_RUN, LAST_RUN)}
-        shared = held.tile([P, 2 * BANK + 2 * PACK * H], F32, name="shared", align_bytes=64)
         w1_raw = {e: held.tile([P, PACK, H], F32, name="w1_raw%d" % e, tag="w1_raw%d" % e, align_bytes=64)[:]
                   for e in range(E) if e not in HOSTS}
-        for n, e in enumerate(HOSTS):
-            start = 2 * BANK + n * PACK * H
-            w1_raw[e] = shared[:, start:start + PACK * H].rearrange("p (j c) -> p j c", j=PACK)
+        host = {e: held.tile([P, PACK * C // 2 + PACK * H], F32, name="host%d" % e, align_bytes=64) for e in HOSTS}
+        for e in HOSTS:
+            w1_raw[e] = host[e][:, PACK * C // 2:].rearrange("p (j c) -> p j c", j=PACK)
         w2_raw = [held.tile([P, len(group), PACK, N], F32, name="w2_raw%d" % group[0], tag="w2_raw%d" % group[0],
                             align_bytes=64)
                   for group in W2_GROUPS]
 
-        nc.scalar.dma_start(gate_sb[FIRST_RUN][:], gate[0:P, RUNS[FIRST_RUN][0]:RUNS[FIRST_RUN][1]])
+        nc.scalar.dma_start(gate_first[:], gate[0:P, RUNS[FIRST_RUN][0]:RUNS[FIRST_RUN][1]])
         for n in gate_few:
             nc.scalar.dma_start(gate_few[n][:], gate[0, RUNS[n][0]:RUNS[n][1]].rearrange("(p r) -> p r", p=P))
         nc.sync.dma_start(offs_sb[:], offs)
         for j in range(PACK):
             nc.sync.dma_start(x_rows[j][:], xT.rearrange("(p j) t -> p j t", j=PACK)[:, j, :])
-        for e in range(E):
-            nc.sync.dma_start(w1_raw[e], w1[e].rearrange("(p j) c -> p j c", j=PACK))
-        for n, group in enumerate(W2_GROUPS):
+
+        def load_w2(n):
+            group = W2_GROUPS[n]
             nc.sync.dma_start(w2_raw[n][:].rearrange("p e j n -> p e (j n)"),
                               w2[group[0]:group[-1] + 1].rearrange("e (p j) n -> p e (j n)", j=PACK))
+
+        for e in range(E):
+            nc.sync.dma_start(w1_raw[e], w1[e].rearrange("(p j) c -> p j c", j=PACK))
+            if e == FIRST_W2_AFTER:
+                load_w2(0)
+        for n in range(1, len(W2_GROUPS)):
+            load_w2(n)
         nc.sync.dma_start(pos1_sb[:], pos1)
         nc.sync.dma_start(pos2_sb[:], pos2)
 
@@ -86,33 +89,28 @@ def tile_moe_pre_mlp_silu_kernel(tc, xT, w1, w2, gate, offs, pos1, pos2, out):
             return held.tile([P, width], U8, name=name, align_bytes=64)
 
         def rounded(name, width):
-            return held.tile([P, width], BF16, name=name, tag=name, align_bytes=64)
+            return held.tile([P, width], BF16, name=name, align_bytes=64)
 
-        def freed(e, start, width):
-            return w1_raw[e].rearrange("p j c -> p (j c)")[:, start // 2:(start + width) // 2].bitcast(BF16)
+        def freed(e, width):
+            return w1_raw[e].rearrange("p j c -> p (j c)")[:, 0:width // 2].bitcast(BF16)
 
-        def silu_after(q):
-            return max(2 * q + 2, FIRST_SILU_AFTER)
-
-        picked = [held.tile([P, PACK, hi - lo], F32, name="picked%d" % lo)[:].rearrange("p (a b) c -> p a b c", a=2)
-                  for lo, hi in RUNS[:LAST_RUN]]
-        halves = shared[:].rearrange("p (a r) -> p a r", a=2)
-        picked.append(halves[:, :, 0:2 * BANK].rearrange("p a (b c) -> p a b c", b=2))
-        x_bf = [rounded("x_bf%d" % lo, PACK * (hi - lo))[:] for lo, hi in RUNS[:LAST_RUN]]
-        last_run_after = RUNS[LAST_RUN][0] // C - 1
-        x_bf.append(freed(last_run_after, 0, PACK * BANK))
+        picked_middle = held.tile([P, PACK, BANK], F32, name="picked_middle")
+        picked_last = held.tile([P, PACK, BANK], F32, name="picked_last")
+        picked = [picked_last[:, :, 0:2 * C], picked_middle[:], picked_last[:]]
+        x_bf = [rounded("x_bf0", PACK * 2 * C)[:], freed(0, PACK * BANK), freed(1, PACK * BANK)]
         h_width = 2 * PACK * C
-        h_bf = [freed(silu_after(0), 0, h_width), freed(silu_after(1), h_width, h_width), rounded("h_bf2", h_width)[:],
-                freed(silu_after(3), 0, h_width), rounded("h_bf4", h_width)[:]]
+        h_bf = [rounded("h_bf0", h_width)[:], host[5][:, 0:h_width // 2].bitcast(BF16),
+                host[5][:, h_width // 2:h_width].bitcast(BF16), freed(7, h_width),
+                rounded("h_bf4", h_width)[:]]
         w1_bf = [rounded("w1_bf%d" % r, 2 * PACK * H) for r in range(RING)]
         w2_bf = [rounded("w2_bf%d" % group[0], len(group) * PACK * N) for group in W2_GROUPS]
         x_codes = [words("x_codes%d" % lo, hi - lo) for lo, hi in RUNS]
         x_scales = [scale_bytes("x_scales%d" % lo, hi - lo) for lo, hi in RUNS]
-        w1_codes = {q: words("w1_codes%d" % q, 2 * H) for q in range(PAIRS - 1)}
-        w1_scales = [scale_bytes("w1_scales%d" % q, 2 * H) for q in range(PAIRS)]
-        h_codes = {q: words("h_codes%d" % q, 2 * C) for q in range(PAIRS) if q != PAIRS - 2}
+        w1_codes = {}
+        w1_scales = [scale_bytes("w1_scales%d" % e, H) for e in range(E)]
+        h_codes = {}
         h_scales = [scale_bytes("h_scales%d" % q, 2 * C) for q in range(PAIRS)]
-        w2_codes = [words("w2_codes%d" % group[0], len(group) * N) for group in W2_GROUPS]
+        w2_codes = {}
         w2_scales = [scale_bytes("w2_scales%d" % group[0], len(group) * N) for group in W2_GROUPS]
         a_ps = [psum.tile([P, PACK, C], F32, name="a_ps%d" % r) for r in range(A_BANKS)]
         y_ps = [psum.tile([P, BANK], F32, name="y_ps%d" % r) for r in range(len(Y_GROUPS))]
@@ -135,6 +133,8 @@ def tile_moe_pre_mlp_silu_kernel(tc, xT, w1, w2, gate, offs, pos1, pos2, out):
             row = held.tile([P, P], F32, name="row", align_bytes=64)
             identity = held.tile([P, P], F32, name="identity")
             nc.vector.memset(ones[:], 1.0)
+            warm = held.tile([P, 1], F32, name="warm")
+            nc.scalar.activation(warm[:], ones[:, 0:1], SILU)
             nc.vector.memset(identity[:], 0.0)
             nc.vector.tensor_tensor_scan(column[:], ones[:], ones[:], 0.0, MULT, ADD)
             nc.vector.transpose(row[:], column[:])
@@ -147,49 +147,48 @@ def tile_moe_pre_mlp_silu_kernel(tc, xT, w1, w2, gate, offs, pos1, pos2, out):
             identity = build_identity()
             for n in gate_few:
                 for r in range(BANK // P):
-                    nc.tensor.transpose(y_ps[n][:, r * P:(r + 1) * P], gate_few[n][:, r:r + 1].to_broadcast([P, P]),
-                                        identity[:])
-                if n == MIDDLE_RUN:
-                    warm = held.tile([P, 1], F32, name="warm")
-                    nc.scalar.activation(warm[:], y_ps[n][:, 0:1], SILU)
-                nc.scalar.copy(gate_sb[n][:].rearrange("k (p r) -> k p r", p=P),
-                               y_ps[n][:].rearrange("k (r p) -> k p r", p=P))
+                    nc.tensor.transpose(y_ps[n - 1][:].rearrange("k (p r) -> k r p", p=P)[:, r, :],
+                                        gate_few[n][:, r:r + 1].to_broadcast([P, P]), identity[:])
 
-        def gather_x(n, j):
+        def tokens(n, j):
             lo, hi = RUNS[n]
-            tokens = x_rows[j][:].indirect(offs_sb[:, lo // PER_COLUMN:hi // PER_COLUMN])
-            nc.vector.tensor_tensor(picked[n][:, j // 2, j % 2, :], tokens, gate_sb[n][:], MULT)
+            return x_rows[j][:].indirect(offs_sb[:, lo // PER_COLUMN:hi // PER_COLUMN])
 
-        def round_x(on_vector, n, lo, hi):
-            copy(on_vector, x_bf[n][:, PACK * lo:PACK * hi].rearrange("p (c i a b) -> p c a b i", i=STEP, a=2, b=2),
-                 picked[n][:, :, :, lo:hi].rearrange("p a b (c i) -> p c a b i", i=STEP))
+        def by_slot(n):
+            return (x_bf[n].rearrange("p (c i j) -> p c j i", i=STEP, j=PACK),
+                    picked[n].rearrange("p j (c i) -> p c j i", i=STEP))
+
+        def weigh_x(n):
+            dst, src = by_slot(n)
+            weight = y_ps[n - 1][:].rearrange("p (c i) -> p c i", i=STEP).unsqueeze(2)
+            nc.vector.tensor_tensor(dst, src, weight.to_broadcast([P, BANK // STEP, PACK, STEP]), MULT)
 
         def quantize_x(n):
             quantize(x_codes[n][:], x_scales[n][:], x_bf[n])
 
-        def round_w1(e):
+        def round_w1(e, on_vector, lo=0, hi=P):
             dst = w1_bf[e // 2 % RING][:, part([e], PACK * H)].rearrange("p (u v m j) -> p u m j v", u=2, v=2, j=PACK)
-            copy(e % 2 == 1 and e >= VECTOR_FROM, dst, w1_raw[e].rearrange("p j (m u v) -> p u m j v", u=2, v=2))
+            src = w1_raw[e].rearrange("p j (m u v) -> p u m j v", u=2, v=2)
+            copy(on_vector, dst[:, :, lo:hi, :, :], src[:, :, lo:hi, :, :])
 
-        def first_product(experts):
-            q = experts[0] // 2
-            quantize(w1_codes[q][:, part(experts, H)], w1_scales[q][:, part(experts, H)],
-                     w1_bf[q % RING][:, part(experts, PACK * H)])
-            for e in experts:
-                n = max(m for m, (lo, hi) in enumerate(RUNS) if lo <= e * C)
-                slots = slice(e * C - RUNS[n][0], (e + 1) * C - RUNS[n][0])
-                for t in range(PACK):
-                    cols = slice(e % 2 * H + t * P, e % 2 * H + (t + 1) * P)
-                    nc.tensor.matmul_mx(out=a_ps[e % A_BANKS][:, t, :], lhsT=w1_codes[q][:, cols].bitcast(FP8X4),
-                                        lhsT_scale=w1_scales[q][:, cols], rhs=x_codes[n][:, slots].bitcast(FP8X4),
-                                        rhs_scale=x_scales[n][:, slots], start=True, stop=True)
+        def first_product(e, after=None):
+            tag = "w1_codes%d" % (e % RING if e < 6 else e) if after is None else "w1_raw%d" % after
+            w1_codes[e] = words("w1_codes%d" % e, H, tag)
+            quantize(w1_codes[e][:], w1_scales[e][:], w1_bf[e // 2 % RING][:, part([e], PACK * H)])
+            n = max(m for m, (lo, hi) in enumerate(RUNS) if lo <= e * C)
+            slots = slice(e * C - RUNS[n][0], (e + 1) * C - RUNS[n][0])
+            for t in range(PACK):
+                cols = slice(t * P, (t + 1) * P)
+                nc.tensor.matmul_mx(out=a_ps[e % A_BANKS][:, t, :], lhsT=w1_codes[e][:, cols].bitcast(FP8X4),
+                                    lhsT_scale=w1_scales[e][:, cols], rhs=x_codes[n][:, slots].bitcast(FP8X4),
+                                    rhs_scale=x_scales[n][:, slots], start=True, stop=True)
 
-        def activate(q):
-            for e in (2 * q, 2 * q + 1):
-                nc.scalar.activation(h_bf[q][:, part([e], PACK * C)].rearrange("p (c t) -> p c t", t=PACK),
-                                     a_ps[e % A_BANKS][:].rearrange("p t c -> p c t"), SILU)
+        def activate(e):
+            nc.scalar.activation(h_bf[e // 2][:, part([e], PACK * C)].rearrange("p (c t) -> p c t", t=PACK),
+                                 a_ps[e % A_BANKS][:].rearrange("p t c -> p c t"), SILU)
 
-        def quantize_h(q):
+        def quantize_h(q, tag=None):
+            h_codes[q] = words("h_codes%d" % q, 2 * C, tag)
             quantize(h_codes[q][:], h_scales[q][:], h_bf[q])
 
         def round_w2(n):
@@ -197,10 +196,9 @@ def tile_moe_pre_mlp_silu_kernel(tc, xT, w1, w2, gate, offs, pos1, pos2, out):
             copy(n not in W2_ON_SCALAR, w2_bf[n][:].rearrange("p (e c i j) -> p e c j i", e=size, i=STEP, j=PACK),
                  w2_raw[n][:].rearrange("p e j (c i) -> p e c j i", i=STEP))
 
-        def quantize_w2(n):
+        def second_product(n, tag=None):
+            w2_codes[n] = words("w2_codes%d" % n, len(W2_GROUPS[n]) * N, tag)
             quantize(w2_codes[n][:], w2_scales[n][:], w2_bf[n][:])
-
-        def second_product(n):
             for r, e in enumerate(W2_GROUPS[n]):
                 b = [m for m, group in enumerate(Y_GROUPS) if e in group][0]
                 place = e - Y_GROUPS[b][0]
@@ -212,65 +210,66 @@ def tile_moe_pre_mlp_silu_kernel(tc, xT, w1, w2, gate, offs, pos1, pos2, out):
 
         spread_gate()
         for j in range(PACK):
-            gather_x(FIRST_RUN, j)
-        round_x(False, FIRST_RUN, 0, 2 * C)
+            nc.vector.tensor_tensor(picked[FIRST_RUN][:, j, :], tokens(FIRST_RUN, j), gate_first[:], MULT)
+            nc.scalar.activation(picked[MIDDLE_RUN][:, j, :], tokens(MIDDLE_RUN, j), COPY)
+        nc.vector.tensor_copy(*by_slot(FIRST_RUN))
+        quantize_x(FIRST_RUN)
         for j in range(PACK):
-            gather_x(MIDDLE_RUN, j)
-            if j == 1:
-                quantize_x(FIRST_RUN)
-        gather_x(LAST_RUN, 0)
-        round_x(True, MIDDLE_RUN, 0, BANK)
-        gather_x(LAST_RUN, 1)
+            nc.scalar.activation(picked[LAST_RUN][:, j, :], tokens(LAST_RUN, j), COPY)
+
+        round_w1(0, True)
+        weigh_x(MIDDLE_RUN)
+        round_w1(1, True)
+        first_product(0)
         quantize_x(MIDDLE_RUN)
-
-        waiting = []
-        for e in range(E - 1):
-            round_w1(e)
-            if e == SINGLY_FROM:
-                first_product([e])
-            for q in range(PAIRS - 1):
-                if silu_after(q) == e:
-                    activate(q)
-                    waiting.append(q)
-            if e % 2 == 1:
-                if waiting:
-                    quantize_h(waiting.pop(0))
-                first_product([e - 1, e] if e < SINGLY_FROM else [e])
-            if e in HOSTS:
-                gather_x(LAST_RUN, 2 + HOSTS.index(e))
-            if e == last_run_after:
-                round_x(False, LAST_RUN, 0, SCALAR_SLOTS)
-                round_x(True, LAST_RUN, SCALAR_SLOTS, BANK)
-                quantize_h(waiting.pop(0))
-                quantize_x(LAST_RUN)
-
-        round_w1(E - 1)
-        w1_codes[PAIRS - 1] = words("w1_codes_last", 2 * H, tag="w1_raw%d" % (E - 1))
-        first_product([E - 2])
-        first_product([E - 1])
+        first_product(1)
+        weigh_x(LAST_RUN)
+        round_w1(2, False)
+        activate(0)
+        activate(1)
+        first_product(2)
+        quantize_x(LAST_RUN)
+        round_w1(3, False)
+        quantize_h(0)
+        round_w1(4, True)
+        activate(2)
+        first_product(3)
+        first_product(4)
+        round_w1(5, False)
+        activate(3)
+        activate(4)
+        round_w1(6, True)
+        first_product(6)
+        first_product(5, after=6)
+        round_w1(7, False)
+        activate(5)
+        activate(6)
+        round_w1(8, True)
+        quantize_h(1, "w1_codes6")
+        quantize_h(2)
+        first_product(7, after=8)
+        first_product(8)
+        activate(7)
+        activate(8)
+        round_w1(9, True)
+        quantize_h(3)
+        first_product(9)
         round_w2(0)
-        activate(PAIRS - 1)
-        h_codes[PAIRS - 2] = words("h_codes_late", 2 * C, tag="w1_bf%d" % ((PAIRS - 1) % RING))
-
+        activate(9)
         round_w2(1)
-        quantize_h(PAIRS - 2)
-        for n in (0, 1):
-            quantize_w2(n)
-        for n in (0, 1):
-            second_product(n)
+        second_product(1)
+        second_product(0, "w2_raw2")
         round_w2(2)
-        quantize_h(PAIRS - 1)
-        quantize_w2(2)
-        rest = range(3, len(W2_GROUPS))
-        for n in rest:
-            round_w2(n)
-        for n in rest:
-            quantize_w2(n)
         second_product(2)
-        for n in rest:
-            second_product(n)
+        quantize_h(4, "w2_raw4")
+        round_w2(3)
+        round_w2(4)
+        round_w2(5)
+        second_product(3)
+        second_product(5)
+        second_product(4)
 
-        y_all = held.tile([P, S], F32, name="y_all", tag="w2_raw%d" % (E - 4), align_bytes=64)
+        y_all = held.tile([P, S], F32, name="y_all", tag="w2_raw8", align_bytes=64)
         for b, group in enumerate(Y_GROUPS):
             copy(b == len(Y_GROUPS) - 1, y_all[:, group[0] * C:(group[-1] + 1) * C], y_ps[b][:, 0:len(group) * C])
 

@@ -29,7 +29,8 @@ SILU = mybir.ActivationFunctionType.Silu
 RUNS = ((0, 2 * C), (2 * C, 2 * C + BANK), (2 * C + BANK, S))
 FIRST_RUN, MIDDLE_RUN, LAST_RUN = range(len(RUNS))
 W2_GROUPS = tuple((2 * q, 2 * q + 1) for q in range(PAIRS - 1)) + ((E - 2,), (E - 1,))
-Y_GROUPS = ((0, 1, 2, 3), (4, 5), (6, 7), (8, 9))
+Y_GROUPS = ((0, 1, 2, 3), (4, 5), (6, 7), (9,), (8,))
+Y_ON_VECTOR = (0, 3)
 PIECE = 128
 OUT_PARTS = ((0, 256), (256, 512), (512, T))
 
@@ -50,8 +51,9 @@ def tile_moe_pre_mlp_silu_kernel(tc, xT, w1, w2, gate, offs, pos1, pos2, out):
         pos1_sb = held.tile([P, T // PER_COLUMN], U16, name="pos1_sb")
         pos2_sb = held.tile([P, T // PER_COLUMN], U16, name="pos2_sb")
         x_rows = [held.tile([P, T], F32, name="x_rows%d" % j) for j in range(PACK)]
-        gate_first = held.tile([P, 2 * C], F32, name="gate_first")
-        gate_few = {n: held.tile([P, BANK // P], F32, name="gate_few%d" % n) for n in (MIDDLE_RUN, LAST_RUN)}
+        gate_first = held.tile([P, 2 * C // P], F32, name="gate_first")
+        gate_rest = held.tile([P, 2, BANK // P], F32, name="gate_rest")
+        gate_few = [gate_first[:], gate_rest[:, 0, :], gate_rest[:, 1, :]]
         w1_raw = {e: held.tile([P, PACK, H], F32, name="w1_raw%d" % e, tag="w1_raw%d" % e, align_bytes=64)[:]
                   for e in range(E) if e not in HOSTS}
         host = {e: held.tile([P, PACK * C // 2 + PACK * H], F32, name="host%d" % e, align_bytes=64) for e in HOSTS}
@@ -61,12 +63,12 @@ def tile_moe_pre_mlp_silu_kernel(tc, xT, w1, w2, gate, offs, pos1, pos2, out):
                             align_bytes=64)
                   for group in W2_GROUPS]
 
-        nc.scalar.dma_start(gate_first[:], gate[0:P, RUNS[FIRST_RUN][0]:RUNS[FIRST_RUN][1]])
-        for n in gate_few:
-            nc.scalar.dma_start(gate_few[n][:], gate[0, RUNS[n][0]:RUNS[n][1]].rearrange("(p r) -> p r", p=P))
-        nc.sync.dma_start(offs_sb[:], offs)
+        nc.scalar.dma_start(gate_first[:], gate[0, 0:2 * C].rearrange("(p r) -> p r", p=P))
+        nc.scalar.dma_start(gate_rest[:], gate[0, 2 * C:S].rearrange("(n p r) -> p n r", n=2, p=P))
         for j in range(PACK):
             nc.sync.dma_start(x_rows[j][:], xT.rearrange("(p j) t -> p j t", j=PACK)[:, j, :])
+            if j == 0:
+                nc.sync.dma_start(offs_sb[:], offs)
 
         def load_w2(n):
             group = W2_GROUPS[n]
@@ -113,7 +115,8 @@ def tile_moe_pre_mlp_silu_kernel(tc, xT, w1, w2, gate, offs, pos1, pos2, out):
         w2_codes = {}
         w2_scales = [scale_bytes("w2_scales%d" % group[0], len(group) * N) for group in W2_GROUPS]
         a_ps = [psum.tile([P, PACK, C], F32, name="a_ps%d" % r) for r in range(A_BANKS)]
-        y_ps = [psum.tile([P, BANK], F32, name="y_ps%d" % r) for r in range(len(Y_GROUPS))]
+        y_ps = [psum.tile([P, BANK], F32, name="y_ps%d" % r)[:] for r in range(len(Y_GROUPS) - 1)]
+        y_ps.append(a_ps[0][:].rearrange("p t c -> p (t c)"))
 
         def copy(on_vector, dst, src):
             if on_vector:
@@ -145,9 +148,9 @@ def tile_moe_pre_mlp_silu_kernel(tc, xT, w1, w2, gate, offs, pos1, pos2, out):
 
         def spread_gate():
             identity = build_identity()
-            for n in gate_few:
-                for r in range(BANK // P):
-                    nc.tensor.transpose(y_ps[n - 1][:].rearrange("k (p r) -> k r p", p=P)[:, r, :],
+            for n, (lo, hi) in enumerate(RUNS):
+                for r in range((hi - lo) // P):
+                    nc.tensor.transpose(y_ps[n][:, 0:hi - lo].rearrange("k (p r) -> k r p", p=P)[:, r, :],
                                         gate_few[n][:, r:r + 1].to_broadcast([P, P]), identity[:])
 
         def tokens(n, j):
@@ -160,8 +163,9 @@ def tile_moe_pre_mlp_silu_kernel(tc, xT, w1, w2, gate, offs, pos1, pos2, out):
 
         def weigh_x(n):
             dst, src = by_slot(n)
-            weight = y_ps[n - 1][:].rearrange("p (c i) -> p c i", i=STEP).unsqueeze(2)
-            nc.vector.tensor_tensor(dst, src, weight.to_broadcast([P, BANK // STEP, PACK, STEP]), MULT)
+            lo, hi = RUNS[n]
+            weight = y_ps[n][:, 0:hi - lo].rearrange("p (c i) -> p c i", i=STEP).unsqueeze(2)
+            nc.vector.tensor_tensor(dst, src, weight.to_broadcast([P, (hi - lo) // STEP, PACK, STEP]), MULT)
 
         def quantize_x(n):
             quantize(x_codes[n][:], x_scales[n][:], x_bf[n])
@@ -210,9 +214,9 @@ def tile_moe_pre_mlp_silu_kernel(tc, xT, w1, w2, gate, offs, pos1, pos2, out):
 
         spread_gate()
         for j in range(PACK):
-            nc.vector.tensor_tensor(picked[FIRST_RUN][:, j, :], tokens(FIRST_RUN, j), gate_first[:], MULT)
+            nc.vector.tensor_copy(picked[FIRST_RUN][:, j, :], tokens(FIRST_RUN, j))
             nc.scalar.activation(picked[MIDDLE_RUN][:, j, :], tokens(MIDDLE_RUN, j), COPY)
-        nc.vector.tensor_copy(*by_slot(FIRST_RUN))
+        weigh_x(FIRST_RUN)
         quantize_x(FIRST_RUN)
         for j in range(PACK):
             nc.scalar.activation(picked[LAST_RUN][:, j, :], tokens(LAST_RUN, j), COPY)
@@ -271,7 +275,7 @@ def tile_moe_pre_mlp_silu_kernel(tc, xT, w1, w2, gate, offs, pos1, pos2, out):
 
         y_all = held.tile([P, S], F32, name="y_all", tag="w2_raw8", align_bytes=64)
         for b, group in enumerate(Y_GROUPS):
-            copy(b == len(Y_GROUPS) - 1, y_all[:, group[0] * C:(group[-1] + 1) * C], y_ps[b][:, 0:len(group) * C])
+            copy(b in Y_ON_VECTOR, y_all[:, group[0] * C:(group[-1] + 1) * C], y_ps[b][:, 0:len(group) * C])
 
         first = held.tile([P, T], F32, name="first")
         total = held.tile([P, T], F32, name="total")

@@ -28,15 +28,14 @@ SILU = mybir.ActivationFunctionType.Silu
 
 RUNS = ((0, 2 * C), (2 * C, 2 * C + BANK), (2 * C + BANK, S))
 FIRST_RUN, MIDDLE_RUN, LAST_RUN = range(len(RUNS))
+W1_ON_SCALAR = (2,) + tuple(range(3, E - 1, 2))
+HOST = 5
 W2_GROUPS = tuple((2 * q, 2 * q + 1) for q in range(PAIRS - 1)) + ((E - 2,), (E - 1,))
-Y_GROUPS = ((0, 1, 2, 3), (4, 5), (6, 7), (9,), (8,))
+W2_ON_SCALAR = (0, 3, 4)
+Y_GROUPS = ((0, 1, 2, 3), (4, 5), (6, 7), (E - 1,), (E - 2,))
 Y_ON_VECTOR = (0, 3)
 PIECE = 128
-OUT_PARTS = ((0, 256), (256, 512), (512, T))
-
-W2_ON_SCALAR = (0, 3, 4)
-HOSTS = (5,)
-FIRST_W2_AFTER = 9
+OUT_PARTS = ((0, 2 * PIECE), (2 * PIECE, 4 * PIECE), (4 * PIECE, T))
 RING = 3
 A_BANKS = 4
 
@@ -55,13 +54,12 @@ def tile_moe_pre_mlp_silu_kernel(tc, xT, w1, w2, gate, offs, pos1, pos2, out):
         gate_rest = held.tile([P, 2, BANK // P], F32, name="gate_rest")
         gate_few = [gate_first[:], gate_rest[:, 0, :], gate_rest[:, 1, :]]
         w1_raw = {e: held.tile([P, PACK, H], F32, name="w1_raw%d" % e, tag="w1_raw%d" % e, align_bytes=64)[:]
-                  for e in range(E) if e not in HOSTS}
-        host = {e: held.tile([P, PACK * C // 2 + PACK * H], F32, name="host%d" % e, align_bytes=64) for e in HOSTS}
-        for e in HOSTS:
-            w1_raw[e] = host[e][:, PACK * C // 2:].rearrange("p (j c) -> p j c", j=PACK)
-        w2_raw = [held.tile([P, len(group), PACK, N], F32, name="w2_raw%d" % group[0], tag="w2_raw%d" % group[0],
-                            align_bytes=64)
-                  for group in W2_GROUPS]
+                  for e in range(E) if e != HOST}
+        h_words = PACK * C // 2
+        host = held.tile([P, h_words + PACK * H], F32, name="host", align_bytes=64)
+        w1_raw[HOST] = host[:, h_words:].rearrange("p (j c) -> p j c", j=PACK)
+        w2_raw = [held.tile([P, len(group), PACK, N], F32, name="w2_raw%d" % n, tag="w2_raw%d" % n, align_bytes=64)
+                  for n, group in enumerate(W2_GROUPS)]
 
         nc.scalar.dma_start(gate_first[:], gate[0, 0:2 * C].rearrange("(p r) -> p r", p=P))
         nc.scalar.dma_start(gate_rest[:], gate[0, 2 * C:S].rearrange("(n p r) -> p n r", n=2, p=P))
@@ -69,23 +67,16 @@ def tile_moe_pre_mlp_silu_kernel(tc, xT, w1, w2, gate, offs, pos1, pos2, out):
             nc.sync.dma_start(x_rows[j][:], xT.rearrange("(p j) t -> p j t", j=PACK)[:, j, :])
             if j == 0:
                 nc.sync.dma_start(offs_sb[:], offs)
-
-        def load_w2(n):
-            group = W2_GROUPS[n]
-            nc.sync.dma_start(w2_raw[n][:].rearrange("p e j n -> p e (j n)"),
-                              w2[group[0]:group[-1] + 1].rearrange("e (p j) n -> p e (j n)", j=PACK))
-
         for e in range(E):
             nc.sync.dma_start(w1_raw[e], w1[e].rearrange("(p j) c -> p j c", j=PACK))
-            if e == FIRST_W2_AFTER:
-                load_w2(0)
-        for n in range(1, len(W2_GROUPS)):
-            load_w2(n)
+        for n, group in enumerate(W2_GROUPS):
+            nc.sync.dma_start(w2_raw[n][:].rearrange("p e j n -> p e (j n)"),
+                              w2[group[0]:group[-1] + 1].rearrange("e (p j) n -> p e (j n)", j=PACK))
         nc.sync.dma_start(pos1_sb[:], pos1)
         nc.sync.dma_start(pos2_sb[:], pos2)
 
-        def words(name, width, tag=None):
-            return held.tile([P, width], U32, name=name, tag=tag or name, align_bytes=64)
+        def words(name, width, tag):
+            return held.tile([P, width], U32, name=name, tag=tag, align_bytes=64)
 
         def scale_bytes(name, width):
             return held.tile([P, width], U8, name=name, align_bytes=64)
@@ -101,22 +92,19 @@ def tile_moe_pre_mlp_silu_kernel(tc, xT, w1, w2, gate, offs, pos1, pos2, out):
         picked = [picked_last[:, :, 0:2 * C], picked_middle[:], picked_last[:]]
         x_bf = [rounded("x_bf0", PACK * 2 * C)[:], freed(0, PACK * BANK), freed(1, PACK * BANK)]
         h_width = 2 * PACK * C
-        h_bf = [rounded("h_bf0", h_width)[:], host[5][:, 0:h_width // 2].bitcast(BF16),
-                host[5][:, h_width // 2:h_width].bitcast(BF16), freed(7, h_width),
-                rounded("h_bf4", h_width)[:]]
+        h_bf = [rounded("h_bf0", h_width)[:], host[:, 0:2 * h_words].bitcast(BF16),
+                host[:, 2 * h_words:4 * h_words].bitcast(BF16), freed(HOST + 2, h_width), rounded("h_bf4", h_width)[:]]
         w1_bf = [rounded("w1_bf%d" % r, 2 * PACK * H) for r in range(RING)]
-        w2_bf = [rounded("w2_bf%d" % group[0], len(group) * PACK * N) for group in W2_GROUPS]
-        x_codes = [words("x_codes%d" % lo, hi - lo) for lo, hi in RUNS]
+        w2_bf = [rounded("w2_bf%d" % n, len(group) * PACK * N) for n, group in enumerate(W2_GROUPS)]
+        x_codes = [words("x_codes%d" % lo, hi - lo, "x_codes%d" % lo) for lo, hi in RUNS]
         x_scales = [scale_bytes("x_scales%d" % lo, hi - lo) for lo, hi in RUNS]
-        w1_codes = {}
         w1_scales = [scale_bytes("w1_scales%d" % e, H) for e in range(E)]
         h_codes = {}
         h_scales = [scale_bytes("h_scales%d" % q, 2 * C) for q in range(PAIRS)]
-        w2_codes = {}
-        w2_scales = [scale_bytes("w2_scales%d" % group[0], len(group) * N) for group in W2_GROUPS]
+        w2_scales = [scale_bytes("w2_scales%d" % n, len(group) * N) for n, group in enumerate(W2_GROUPS)]
         a_ps = [psum.tile([P, PACK, C], F32, name="a_ps%d" % r) for r in range(A_BANKS)]
-        y_ps = [psum.tile([P, BANK], F32, name="y_ps%d" % r)[:] for r in range(len(Y_GROUPS) - 1)]
-        y_ps.append(a_ps[0][:].rearrange("p t c -> p (t c)"))
+        y_ps = [psum.tile([P, BANK], F32, name="y_ps%d" % b)[:] for b in range(len(Y_GROUPS) - 1)]
+        y_ps.append(a_ps[Y_GROUPS[-1][0] % A_BANKS][:].rearrange("p t c -> p (t c)"))
 
         def copy(on_vector, dst, src):
             if on_vector:
@@ -127,8 +115,8 @@ def tile_moe_pre_mlp_silu_kernel(tc, xT, w1, w2, gate, offs, pos1, pos2, out):
         def quantize(codes, scales, src):
             nc.vector.quantize_mx(out=codes.bitcast(FP8X4), scales=scales, in_=src)
 
-        def part(experts, width):
-            return slice(experts[0] % 2 * width, (experts[-1] % 2 + 1) * width)
+        def part(e, width):
+            return slice(e % 2 * width, (e % 2 + 1) * width)
 
         def build_identity():
             ones = held.tile([P, P], F32, name="ones")
@@ -153,45 +141,45 @@ def tile_moe_pre_mlp_silu_kernel(tc, xT, w1, w2, gate, offs, pos1, pos2, out):
                     nc.tensor.transpose(y_ps[n][:, 0:hi - lo].rearrange("k (p r) -> k r p", p=P)[:, r, :],
                                         gate_few[n][:, r:r + 1].to_broadcast([P, P]), identity[:])
 
-        def tokens(n, j):
+        def gather_x(n, j):
             lo, hi = RUNS[n]
-            return x_rows[j][:].indirect(offs_sb[:, lo // PER_COLUMN:hi // PER_COLUMN])
-
-        def by_slot(n):
-            return (x_bf[n].rearrange("p (c i j) -> p c j i", i=STEP, j=PACK),
-                    picked[n].rearrange("p j (c i) -> p c j i", i=STEP))
+            tokens = x_rows[j][:].indirect(offs_sb[:, lo // PER_COLUMN:hi // PER_COLUMN])
+            if n == FIRST_RUN:
+                nc.vector.tensor_copy(picked[n][:, j, :], tokens)
+            else:
+                nc.scalar.activation(picked[n][:, j, :], tokens, COPY)
 
         def weigh_x(n):
-            dst, src = by_slot(n)
-            lo, hi = RUNS[n]
-            weight = y_ps[n][:, 0:hi - lo].rearrange("p (c i) -> p c i", i=STEP).unsqueeze(2)
-            nc.vector.tensor_tensor(dst, src, weight.to_broadcast([P, (hi - lo) // STEP, PACK, STEP]), MULT)
+            size = RUNS[n][1] - RUNS[n][0]
+            weight = y_ps[n][:, 0:size].rearrange("p (c i) -> p c i", i=STEP).unsqueeze(2)
+            nc.vector.tensor_tensor(x_bf[n].rearrange("p (c i j) -> p c j i", i=STEP, j=PACK),
+                                    picked[n].rearrange("p j (c i) -> p c j i", i=STEP),
+                                    weight.to_broadcast([P, size // STEP, PACK, STEP]), MULT)
 
         def quantize_x(n):
             quantize(x_codes[n][:], x_scales[n][:], x_bf[n])
 
-        def round_w1(e, on_vector, lo=0, hi=P):
-            dst = w1_bf[e // 2 % RING][:, part([e], PACK * H)].rearrange("p (u v m j) -> p u m j v", u=2, v=2, j=PACK)
-            src = w1_raw[e].rearrange("p j (m u v) -> p u m j v", u=2, v=2)
-            copy(on_vector, dst[:, :, lo:hi, :, :], src[:, :, lo:hi, :, :])
+        def round_w1(e):
+            dst = w1_bf[e // 2 % RING][:, part(e, PACK * H)].rearrange("p (u v m j) -> p u m j v", u=2, v=2, j=PACK)
+            copy(e not in W1_ON_SCALAR, dst, w1_raw[e].rearrange("p j (m u v) -> p u m j v", u=2, v=2))
 
-        def first_product(e, after=None):
-            tag = "w1_codes%d" % (e % RING if e < 6 else e) if after is None else "w1_raw%d" % after
-            w1_codes[e] = words("w1_codes%d" % e, H, tag)
-            quantize(w1_codes[e][:], w1_scales[e][:], w1_bf[e // 2 % RING][:, part([e], PACK * H)])
+        def first_product(e):
+            behind_next = e in W1_ON_SCALAR and e >= HOST
+            codes = words("w1_codes%d" % e, H, "w1_raw%d" % (e + 1) if behind_next else "w1_ring%d" % (e % RING))
+            quantize(codes[:], w1_scales[e][:], w1_bf[e // 2 % RING][:, part(e, PACK * H)])
             n = max(m for m, (lo, hi) in enumerate(RUNS) if lo <= e * C)
             slots = slice(e * C - RUNS[n][0], (e + 1) * C - RUNS[n][0])
             for t in range(PACK):
                 cols = slice(t * P, (t + 1) * P)
-                nc.tensor.matmul_mx(out=a_ps[e % A_BANKS][:, t, :], lhsT=w1_codes[e][:, cols].bitcast(FP8X4),
+                nc.tensor.matmul_mx(out=a_ps[e % A_BANKS][:, t, :], lhsT=codes[:, cols].bitcast(FP8X4),
                                     lhsT_scale=w1_scales[e][:, cols], rhs=x_codes[n][:, slots].bitcast(FP8X4),
                                     rhs_scale=x_scales[n][:, slots], start=True, stop=True)
 
         def activate(e):
-            nc.scalar.activation(h_bf[e // 2][:, part([e], PACK * C)].rearrange("p (c t) -> p c t", t=PACK),
+            nc.scalar.activation(h_bf[e // 2][:, part(e, PACK * C)].rearrange("p (c t) -> p c t", t=PACK),
                                  a_ps[e % A_BANKS][:].rearrange("p t c -> p c t"), SILU)
 
-        def quantize_h(q, tag=None):
+        def quantize_h(q, tag):
             h_codes[q] = words("h_codes%d" % q, 2 * C, tag)
             quantize(h_codes[q][:], h_scales[q][:], h_bf[q])
 
@@ -200,80 +188,69 @@ def tile_moe_pre_mlp_silu_kernel(tc, xT, w1, w2, gate, offs, pos1, pos2, out):
             copy(n not in W2_ON_SCALAR, w2_bf[n][:].rearrange("p (e c i j) -> p e c j i", e=size, i=STEP, j=PACK),
                  w2_raw[n][:].rearrange("p e j (c i) -> p e c j i", i=STEP))
 
-        def second_product(n, tag=None):
-            w2_codes[n] = words("w2_codes%d" % n, len(W2_GROUPS[n]) * N, tag)
-            quantize(w2_codes[n][:], w2_scales[n][:], w2_bf[n][:])
+        def second_product(n, tag):
+            codes = words("w2_codes%d" % n, len(W2_GROUPS[n]) * N, tag)
+            quantize(codes[:], w2_scales[n][:], w2_bf[n][:])
             for r, e in enumerate(W2_GROUPS[n]):
                 b = [m for m, group in enumerate(Y_GROUPS) if e in group][0]
                 place = e - Y_GROUPS[b][0]
                 cols = slice(r * N, (r + 1) * N)
-                nc.tensor.matmul_mx(out=y_ps[b][:, place * C:(place + 1) * C],
-                                    lhsT=w2_codes[n][:, cols].bitcast(FP8X4), lhsT_scale=w2_scales[n][:, cols],
-                                    rhs=h_codes[e // 2][:, part([e], C)].bitcast(FP8X4),
-                                    rhs_scale=h_scales[e // 2][:, part([e], C)], start=True, stop=True)
+                nc.tensor.matmul_mx(out=y_ps[b][:, place * C:(place + 1) * C], lhsT=codes[:, cols].bitcast(FP8X4),
+                                    lhsT_scale=w2_scales[n][:, cols], rhs=h_codes[e // 2][:, part(e, C)].bitcast(FP8X4),
+                                    rhs_scale=h_scales[e // 2][:, part(e, C)], start=True, stop=True)
 
         spread_gate()
         for j in range(PACK):
-            nc.vector.tensor_copy(picked[FIRST_RUN][:, j, :], tokens(FIRST_RUN, j))
-            nc.scalar.activation(picked[MIDDLE_RUN][:, j, :], tokens(MIDDLE_RUN, j), COPY)
+            gather_x(FIRST_RUN, j)
+            gather_x(MIDDLE_RUN, j)
         weigh_x(FIRST_RUN)
         quantize_x(FIRST_RUN)
         for j in range(PACK):
-            nc.scalar.activation(picked[LAST_RUN][:, j, :], tokens(LAST_RUN, j), COPY)
+            gather_x(LAST_RUN, j)
 
-        round_w1(0, True)
+        round_w1(0)
         weigh_x(MIDDLE_RUN)
-        round_w1(1, True)
+        round_w1(1)
         first_product(0)
         quantize_x(MIDDLE_RUN)
         first_product(1)
         weigh_x(LAST_RUN)
-        round_w1(2, False)
+        round_w1(2)
         activate(0)
         activate(1)
         first_product(2)
         quantize_x(LAST_RUN)
-        round_w1(3, False)
-        quantize_h(0)
-        round_w1(4, True)
-        activate(2)
-        first_product(3)
-        first_product(4)
-        round_w1(5, False)
-        activate(3)
-        activate(4)
-        round_w1(6, True)
-        first_product(6)
-        first_product(5, after=6)
-        round_w1(7, False)
-        activate(5)
-        activate(6)
-        round_w1(8, True)
-        quantize_h(1, "w1_codes6")
-        quantize_h(2)
-        first_product(7, after=8)
-        first_product(8)
-        activate(7)
-        activate(8)
-        round_w1(9, True)
-        quantize_h(3)
-        first_product(9)
-        round_w2(0)
-        activate(9)
-        round_w2(1)
-        second_product(1)
-        second_product(0, "w2_raw2")
-        round_w2(2)
-        second_product(2)
-        quantize_h(4, "w2_raw4")
-        round_w2(3)
-        round_w2(4)
-        round_w2(5)
-        second_product(3)
-        second_product(5)
-        second_product(4)
 
-        y_all = held.tile([P, S], F32, name="y_all", tag="w2_raw8", align_bytes=64)
+        activated = 2
+        for q, e in enumerate(range(3, E - 1, 2)):
+            round_w1(e)
+            for before in range(activated, e):
+                activate(before)
+            activated = e
+            round_w1(e + 1)
+            quantize_h(q, "h_codes%d" % q)
+            first_product(e)
+            first_product(e + 1)
+        for before in range(activated, E - 1):
+            activate(before)
+        round_w1(E - 1)
+        quantize_h(PAIRS - 2, "h_codes%d" % (PAIRS - 2))
+        first_product(E - 1)
+
+        round_w2(0)
+        activate(E - 1)
+        round_w2(1)
+        second_product(1, "w2_codes1")
+        second_product(0, "w2_raw1")
+        round_w2(2)
+        second_product(2, "w2_codes2")
+        quantize_h(PAIRS - 1, "w2_raw2")
+        for n in (3, 4, 5):
+            round_w2(n)
+        for n in (3, 5, 4):
+            second_product(n, "w2_codes%d" % n)
+
+        y_all = held.tile([P, S], F32, name="y_all", tag="w2_raw%d" % W2_ON_SCALAR[-1], align_bytes=64)
         for b, group in enumerate(Y_GROUPS):
             copy(b in Y_ON_VECTOR, y_all[:, group[0] * C:(group[-1] + 1) * C], y_ps[b][:, 0:len(group) * C])
 

@@ -34,8 +34,8 @@ W2_GROUPS = tuple((2 * q, 2 * q + 1) for q in range(PAIRS - 1)) + ((E - 2,), (E 
 W2_ON_SCALAR = (0, 3, 4)
 Y_GROUPS = ((0, 1, 2, 3), (4, 5), (6, 7), (E - 1,), (E - 2,))
 Y_ON_VECTOR = (0, 3)
-PIECE = 128
-OUT_PARTS = ((0, 2 * PIECE), (2 * PIECE, 4 * PIECE), (4 * PIECE, T))
+FUSED = ((0, 192), (192, 384))
+PLAIN = (384, T)
 RING = 3
 A_BANKS = 4
 
@@ -70,8 +70,9 @@ def tile_moe_pre_mlp_silu_kernel(tc, xT, w1, w2, gate, offs, pos1, pos2, out):
         for e in range(E):
             nc.sync.dma_start(w1_raw[e], w1[e].rearrange("(p j) c -> p j c", j=PACK))
         for n, group in enumerate(W2_GROUPS):
-            nc.sync.dma_start(w2_raw[n][:].rearrange("p e j n -> p e (j n)"),
-                              w2[group[0]:group[-1] + 1].rearrange("e (p j) n -> p e (j n)", j=PACK))
+            for r, e in enumerate(group):
+                nc.sync.dma_start(w2_raw[n][:, r].rearrange("p j n -> p (j n)"),
+                                  w2[e].rearrange("(p j) n -> p (j n)", j=PACK))
         nc.sync.dma_start(pos1_sb[:], pos1)
         nc.sync.dma_start(pos2_sb[:], pos2)
 
@@ -255,11 +256,18 @@ def tile_moe_pre_mlp_silu_kernel(tc, xT, w1, w2, gate, offs, pos1, pos2, out):
             copy(b in Y_ON_VECTOR, y_all[:, group[0] * C:(group[-1] + 1) * C], y_ps[b][:, 0:len(group) * C])
 
         first = held.tile([P, T], F32, name="first")
+        second = held.tile([P, PLAIN[1] - PLAIN[0]], F32, name="second")
         total = held.tile([P, T], F32, name="total")
-        for lo in range(0, T, PIECE):
-            cols = slice(lo // PER_COLUMN, (lo + PIECE) // PER_COLUMN)
-            nc.scalar.activation(first[:, lo:lo + PIECE], y_all[:].indirect(pos1_sb[:, cols]), COPY)
-            nc.vector.tensor_tensor(total[:, lo:lo + PIECE], y_all[:].indirect(pos2_sb[:, cols]),
-                                    first[:, lo:lo + PIECE], ADD)
-        for lo, hi in OUT_PARTS:
+
+        def looked_up(positions, lo, hi):
+            return y_all[:].indirect(positions[:, lo // PER_COLUMN:hi // PER_COLUMN])
+
+        nc.vector.tensor_copy(second[:], looked_up(pos2_sb, *PLAIN))
+        for lo, hi in FUSED + (PLAIN,):
+            nc.scalar.activation(first[:, lo:hi], looked_up(pos1_sb, lo, hi), COPY)
+        for lo, hi in FUSED:
+            nc.vector.tensor_tensor(total[:, lo:hi], looked_up(pos2_sb, lo, hi), first[:, lo:hi], ADD)
             nc.sync.dma_start(out[:, lo:hi], total[:, lo:hi])
+        lo, hi = PLAIN
+        nc.vector.tensor_tensor(total[:, lo:hi], second[:], first[:, lo:hi], ADD)
+        nc.sync.dma_start(out[:, lo:hi], total[:, lo:hi])

@@ -34,8 +34,9 @@ W2_GROUPS = tuple((2 * q, 2 * q + 1) for q in range(PAIRS - 1)) + ((E - 2,), (E 
 W2_ON_SCALAR = (0, 3, 4)
 Y_GROUPS = ((0, 1, 2, 3), (4, 5), (6, 7), (E - 1,), (E - 2,))
 Y_ON_VECTOR = (0, 3)
-FUSED = ((0, 192), (192, 384))
-PLAIN = (384, T)
+OWN = 96
+FUSED = ((0, 224), (224, 384), (384, 512))
+PLAIN = 512
 RING = 3
 A_BANKS = 4
 
@@ -50,9 +51,10 @@ def tile_moe_pre_mlp_silu_kernel(tc, xT, w1, w2, gate, offs, pos1, pos2, out):
         pos1_sb = held.tile([P, T // PER_COLUMN], U16, name="pos1_sb")
         pos2_sb = held.tile([P, T // PER_COLUMN], U16, name="pos2_sb")
         x_rows = [held.tile([P, T], F32, name="x_rows%d" % j) for j in range(PACK)]
-        gate_first = held.tile([P, 2 * C // P], F32, name="gate_first")
-        gate_rest = held.tile([P, 2, BANK // P], F32, name="gate_rest")
-        gate_few = [gate_first[:], gate_rest[:, 0, :], gate_rest[:, 1, :]]
+        gate_rows = held.tile([P, C], F32, name="gate_rows")
+        gate_few = held.tile([P, E], F32, name="gate_few")
+        nc.vector.memset(gate_rows[0:P - QUADRANT, :], 0.0)
+        nc.vector.memset(gate_rows[P - QUADRANT:P - E, :], 0.0)
         w1_raw = {e: held.tile([P, PACK, H], F32, name="w1_raw%d" % e, tag="w1_raw%d" % e, align_bytes=64)[:]
                   for e in range(E) if e != HOST}
         h_words = PACK * C // 2
@@ -61,15 +63,19 @@ def tile_moe_pre_mlp_silu_kernel(tc, xT, w1, w2, gate, offs, pos1, pos2, out):
         w2_raw = [held.tile([P, len(group), PACK, N], F32, name="w2_raw%d" % n, tag="w2_raw%d" % n, align_bytes=64)
                   for n, group in enumerate(W2_GROUPS)]
 
-        nc.scalar.dma_start(gate_first[:], gate[0, 0:2 * C].rearrange("(p r) -> p r", p=P))
-        nc.scalar.dma_start(gate_rest[:], gate[0, 2 * C:S].rearrange("(n p r) -> p n r", n=2, p=P))
         for j in range(PACK):
             nc.sync.dma_start(x_rows[j][:], xT.rearrange("(p j) t -> p j t", j=PACK)[:, j, :])
             if j == 0:
                 nc.sync.dma_start(offs_sb[:], offs)
+            if j == 1:
+                for lo, hi in ((0, 2), (2, E)):
+                    nc.sync.dma_start(gate_rows[P - E + lo:P - E + hi, :],
+                                      gate[0, lo * C:hi * C].rearrange("(e c) -> e c", c=C))
         for e in range(E):
             nc.sync.dma_start(w1_raw[e], w1[e].rearrange("(p j) c -> p j c", j=PACK))
-        for n, group in enumerate(W2_GROUPS):
+        nc.sync.dma_start(w2_raw[0][:].rearrange("p e j n -> p e (j n)"),
+                          w2[0:2].rearrange("e (p j) n -> p e (j n)", j=PACK))
+        for n, group in list(enumerate(W2_GROUPS))[1:]:
             for r, e in enumerate(group):
                 nc.sync.dma_start(w2_raw[n][:, r].rearrange("p j n -> p (j n)"),
                                   w2[e].rearrange("(p j) n -> p (j n)", j=PACK))
@@ -137,10 +143,12 @@ def tile_moe_pre_mlp_silu_kernel(tc, xT, w1, w2, gate, offs, pos1, pos2, out):
 
         def spread_gate():
             identity = build_identity()
+            nc.tensor.transpose(a_ps[0][:, 0, :], gate_rows[:], identity[:])
+            nc.vector.tensor_copy(gate_few[:], a_ps[0][:, 0, P - E:P])
             for n, (lo, hi) in enumerate(RUNS):
-                for r in range((hi - lo) // P):
-                    nc.tensor.transpose(y_ps[n][:, 0:hi - lo].rearrange("k (p r) -> k r p", p=P)[:, r, :],
-                                        gate_few[n][:, r:r + 1].to_broadcast([P, P]), identity[:])
+                for e in range(lo // C, hi // C):
+                    nc.tensor.transpose(y_ps[n][:, e * C - lo:(e + 1) * C - lo],
+                                        gate_few[:, e:e + 1].to_broadcast([P, P]), identity[:])
 
         def gather_x(n, j):
             lo, hi = RUNS[n]
@@ -256,18 +264,18 @@ def tile_moe_pre_mlp_silu_kernel(tc, xT, w1, w2, gate, offs, pos1, pos2, out):
             copy(b in Y_ON_VECTOR, y_all[:, group[0] * C:(group[-1] + 1) * C], y_ps[b][:, 0:len(group) * C])
 
         first = held.tile([P, T], F32, name="first")
-        second = held.tile([P, PLAIN[1] - PLAIN[0]], F32, name="second")
+        second = held.tile([P, T - PLAIN], F32, name="second")
         total = held.tile([P, T], F32, name="total")
 
         def looked_up(positions, lo, hi):
             return y_all[:].indirect(positions[:, lo // PER_COLUMN:hi // PER_COLUMN])
 
-        nc.vector.tensor_copy(second[:], looked_up(pos2_sb, *PLAIN))
-        for lo, hi in FUSED + (PLAIN,):
-            nc.scalar.activation(first[:, lo:hi], looked_up(pos1_sb, lo, hi), COPY)
+        nc.vector.tensor_copy(first[:, 0:OWN], looked_up(pos1_sb, 0, OWN))
+        nc.vector.tensor_copy(second[:], looked_up(pos2_sb, PLAIN, T))
+        for lo, hi in FUSED + ((PLAIN, T),):
+            nc.scalar.activation(first[:, max(lo, OWN):hi], looked_up(pos1_sb, max(lo, OWN), hi), COPY)
         for lo, hi in FUSED:
             nc.vector.tensor_tensor(total[:, lo:hi], looked_up(pos2_sb, lo, hi), first[:, lo:hi], ADD)
             nc.sync.dma_start(out[:, lo:hi], total[:, lo:hi])
-        lo, hi = PLAIN
-        nc.vector.tensor_tensor(total[:, lo:hi], second[:], first[:, lo:hi], ADD)
-        nc.sync.dma_start(out[:, lo:hi], total[:, lo:hi])
+        nc.vector.tensor_tensor(total[:, PLAIN:T], second[:], first[:, PLAIN:T], ADD)
+        nc.sync.dma_start(out[:, PLAIN:T], total[:, PLAIN:T])

from contextlib import ExitStack

import concourse.mybir as mybir

K, T, E, C, H, N = 512, 640, 10, 128, 512, 128
S = E * C
PAIRS = E // 2
P = 128
PACK = 4
STEP = 2
PER_COLUMN = 16
QUADRANT = 32
BANK = 512
FLOPS = 2 * S * (K * H + H * N)
BYTES = 4 * (K * T + E * K * H + E * H * N + S + N * T) + 2 * P * (S + 2 * T) // PER_COLUMN

F32 = mybir.dt.float32
BF16 = mybir.dt.bfloat16
U32 = mybir.dt.uint32
U16 = mybir.dt.uint16
U8 = mybir.dt.uint8
FP8X4 = mybir.dt.float8_e4m3fn_x4
MULT = mybir.AluOpType.mult
ADD = mybir.AluOpType.add
EQUAL = mybir.AluOpType.is_equal
COPY = mybir.ActivationFunctionType.Copy
SILU = mybir.ActivationFunctionType.Silu

RUNS = ((0, 2 * C), (2 * C, 2 * C + BANK), (2 * C + BANK, S))
FIRST_RUN, MIDDLE_RUN, LAST_RUN = range(len(RUNS))
W1_ON_SCALAR = (2,) + tuple(range(3, E - 1, 2))
HOST = 5
W2_GROUPS = tuple((2 * q, 2 * q + 1) for q in range(PAIRS - 1)) + ((E - 2,), (E - 1,))
W2_ON_SCALAR = (0, 3, 4)
Y_GROUPS = ((0, 1, 2, 3), (4, 5), (6, 7), (E - 1,), (E - 2,))
Y_ON_VECTOR = (0, 3)
OWN = 96
FUSED = ((0, 224), (224, 384), (384, 512))
PLAIN = 512
RING = 3
A_BANKS = 4


def tile_moe_pre_mlp_silu_kernel(tc, xT, w1, w2, gate, offs, pos1, pos2, out):
    nc = tc.nc
    with ExitStack() as ctx:
        held = ctx.enter_context(tc.tile_pool(name="held", bufs=1))
        psum = ctx.enter_context(tc.psum_pool(name="psum", bufs=1))

        offs_sb = held.tile([P, S // PER_COLUMN], U16, name="offs_sb")
        pos1_sb = held.tile([P, T // PER_COLUMN], U16, name="pos1_sb")
        pos2_sb = held.tile([P, T // PER_COLUMN], U16, name="pos2_sb")
        x_rows = [held.tile([P, T], F32, name="x_rows%d" % j) for j in range(PACK)]
        gate_rows = held.tile([P, C], F32, name="gate_rows")
        gate_few = held.tile([P, E], F32, name="gate_few")
        nc.vector.memset(gate_rows[0:P - QUADRANT, :], 0.0)
        nc.vector.memset(gate_rows[P - QUADRANT:P - E, :], 0.0)
        w1_raw = {e: held.tile([P, PACK, H], F32, name="w1_raw%d" % e, tag="w1_raw%d" % e, align_bytes=64)[:]
                  for e in range(E) if e != HOST}
        h_words = PACK * C // 2
        host = held.tile([P, h_words + PACK * H], F32, name="host", align_bytes=64)
        w1_raw[HOST] = host[:, h_words:].rearrange("p (j c) -> p j c", j=PACK)
        w2_raw = [held.tile([P, len(group), PACK, N], F32, name="w2_raw%d" % n, tag="w2_raw%d" % n, align_bytes=64)
                  for n, group in enumerate(W2_GROUPS)]

        for j in range(PACK):
            nc.sync.dma_start(x_rows[j][:], xT.rearrange("(p j) t -> p j t", j=PACK)[:, j, :])
            if j == 0:
                nc.sync.dma_start(offs_sb[:], offs)
            if j == 1:
                for lo, hi in ((0, 2), (2, E)):
                    nc.sync.dma_start(gate_rows[P - E + lo:P - E + hi, :],
                                      gate[0, lo * C:hi * C].rearrange("(e c) -> e c", c=C))
        for e in range(E):
            nc.sync.dma_start(w1_raw[e], w1[e].rearrange("(p j) c -> p j c", j=PACK))
        nc.sync.dma_start(w2_raw[0][:].rearrange("p e j n -> p e (j n)"),
                          w2[0:2].rearrange("e (p j) n -> p e (j n)", j=PACK))
        for n, group in list(enumerate(W2_GROUPS))[1:]:
            for r, e in enumerate(group):
                nc.sync.dma_start(w2_raw[n][:, r].rearrange("p j n -> p (j n)"),
                                  w2[e].rearrange("(p j) n -> p (j n)", j=PACK))
        nc.sync.dma_start(pos1_sb[:], pos1)
        nc.sync.dma_start(pos2_sb[:], pos2)

        def words(name, width, tag):
            return held.tile([P, width], U32, name=name, tag=tag, align_bytes=64)

        def scale_bytes(name, width):
            return held.tile([P, width], U8, name=name, align_bytes=64)

        def rounded(name, width):
            return held.tile([P, width], BF16, name=name, align_bytes=64)

        def freed(e, width):
            return w1_raw[e].rearrange("p j c -> p (j c)")[:, 0:width // 2].bitcast(BF16)

        picked_middle = held.tile([P, PACK, BANK], F32, name="picked_middle")
        picked_last = held.tile([P, PACK, BANK], F32, name="picked_last")
        picked = [picked_last[:, :, 0:2 * C], picked_middle[:], picked_last[:]]
        x_bf = [rounded("x_bf0", PACK * 2 * C)[:], freed(0, PACK * BANK), freed(1, PACK * BANK)]
        h_width = 2 * PACK * C
        h_bf = [rounded("h_bf0", h_width)[:], host[:, 0:2 * h_words].bitcast(BF16),
                host[:, 2 * h_words:4 * h_words].bitcast(BF16), freed(HOST + 2, h_width), rounded("h_bf4", h_width)[:]]
        w1_bf = [rounded("w1_bf%d" % r, 2 * PACK * H) for r in range(RING)]
        w2_bf = [rounded("w2_bf%d" % n, len(group) * PACK * N) for n, group in enumerate(W2_GROUPS)]
        x_codes = [words("x_codes%d" % lo, hi - lo, "x_codes%d" % lo) for lo, hi in RUNS]
        x_scales = [scale_bytes("x_scales%d" % lo, hi - lo) for lo, hi in RUNS]
        w1_scales = [scale_bytes("w1_scales%d" % e, H) for e in range(E)]
        h_codes = {}
        h_scales = [scale_bytes("h_scales%d" % q, 2 * C) for q in range(PAIRS)]
        w2_scales = [scale_bytes("w2_scales%d" % n, len(group) * N) for n, group in enumerate(W2_GROUPS)]
        a_ps = [psum.tile([P, PACK, C], F32, name="a_ps%d" % r) for r in range(A_BANKS)]
        y_ps = [psum.tile([P, BANK], F32, name="y_ps%d" % b)[:] for b in range(len(Y_GROUPS) - 1)]
        y_ps.append(a_ps[Y_GROUPS[-1][0] % A_BANKS][:].rearrange("p t c -> p (t c)"))

        def copy(on_vector, dst, src):
            if on_vector:
                nc.vector.tensor_copy(dst, src)
            else:
                nc.scalar.copy(dst, src)

        def quantize(codes, scales, src):
            nc.vector.quantize_mx(out=codes.bitcast(FP8X4), scales=scales, in_=src)

        def part(e, width):
            return slice(e % 2 * width, (e % 2 + 1) * width)

        def build_identity():
            ones = held.tile([P, P], F32, name="ones")
            column = held.tile([P, P], F32, name="column", align_bytes=64)
            row = held.tile([P, P], F32, name="row", align_bytes=64)
            identity = held.tile([P, P], F32, name="identity")
            nc.vector.memset(ones[:], 1.0)
            warm = held.tile([P, 1], F32, name="warm")
            nc.scalar.activation(warm[:], ones[:, 0:1], SILU)
            nc.vector.memset(identity[:], 0.0)
            nc.vector.tensor_tensor_scan(column[:], ones[:], ones[:], 0.0, MULT, ADD)
            nc.vector.transpose(row[:], column[:])
            for start in range(0, P, QUADRANT):
                block = slice(start, start + QUADRANT)
                nc.vector.tensor_tensor(identity[block, block], column[block, block], row[block, block], EQUAL)
            return identity

        def spread_gate():
            identity = build_identity()
            nc.tensor.transpose(a_ps[0][:, 0, :], gate_rows[:], identity[:])
            nc.vector.tensor_copy(gate_few[:], a_ps[0][:, 0, P - E:P])
            for n, (lo, hi) in enumerate(RUNS):
                for e in range(lo // C, hi // C):
                    nc.tensor.transpose(y_ps[n][:, e * C - lo:(e + 1) * C - lo],
                                        gate_few[:, e:e + 1].to_broadcast([P, P]), identity[:])

        def gather_x(n, j):
            lo, hi = RUNS[n]
            tokens = x_rows[j][:].indirect(offs_sb[:, lo // PER_COLUMN:hi // PER_COLUMN])
            if n == FIRST_RUN:
                nc.vector.tensor_copy(picked[n][:, j, :], tokens)
            else:
                nc.scalar.activation(picked[n][:, j, :], tokens, COPY)

        def weigh_x(n):
            size = RUNS[n][1] - RUNS[n][0]
            weight = y_ps[n][:, 0:size].rearrange("p (c i) -> p c i", i=STEP).unsqueeze(2)
            nc.vector.tensor_tensor(x_bf[n].rearrange("p (c i j) -> p c j i", i=STEP, j=PACK),
                                    picked[n].rearrange("p j (c i) -> p c j i", i=STEP),
                                    weight.to_broadcast([P, size // STEP, PACK, STEP]), MULT)

        def quantize_x(n):
            quantize(x_codes[n][:], x_scales[n][:], x_bf[n])

        def round_w1(e):
            dst = w1_bf[e // 2 % RING][:, part(e, PACK * H)].rearrange("p (u v m j) -> p u m j v", u=2, v=2, j=PACK)
            copy(e not in W1_ON_SCALAR, dst, w1_raw[e].rearrange("p j (m u v) -> p u m j v", u=2, v=2))

        def first_product(e):
            behind_next = e in W1_ON_SCALAR and e >= HOST
            codes = words("w1_codes%d" % e, H, "w1_raw%d" % (e + 1) if behind_next else "w1_ring%d" % (e % RING))
            quantize(codes[:], w1_scales[e][:], w1_bf[e // 2 % RING][:, part(e, PACK * H)])
            n = max(m for m, (lo, hi) in enumerate(RUNS) if lo <= e * C)
            slots = slice(e * C - RUNS[n][0], (e + 1) * C - RUNS[n][0])
            for t in range(PACK):
                cols = slice(t * P, (t + 1) * P)
                nc.tensor.matmul_mx(out=a_ps[e % A_BANKS][:, t, :], lhsT=codes[:, cols].bitcast(FP8X4),
                                    lhsT_scale=w1_scales[e][:, cols], rhs=x_codes[n][:, slots].bitcast(FP8X4),
                                    rhs_scale=x_scales[n][:, slots], start=True, stop=True)

        def activate(e):
            nc.scalar.activation(h_bf[e // 2][:, part(e, PACK * C)].rearrange("p (c t) -> p c t", t=PACK),
                                 a_ps[e % A_BANKS][:].rearrange("p t c -> p c t"), SILU)

        def quantize_h(q, tag):
            h_codes[q] = words("h_codes%d" % q, 2 * C, tag)
            quantize(h_codes[q][:], h_scales[q][:], h_bf[q])

        def round_w2(n):
            size = len(W2_GROUPS[n])
            copy(n not in W2_ON_SCALAR, w2_bf[n][:].rearrange("p (e c i j) -> p e c j i", e=size, i=STEP, j=PACK),
                 w2_raw[n][:].rearrange("p e j (c i) -> p e c j i", i=STEP))

        def second_product(n, tag):
            codes = words("w2_codes%d" % n, len(W2_GROUPS[n]) * N, tag)
            quantize(codes[:], w2_scales[n][:], w2_bf[n][:])
            for r, e in enumerate(W2_GROUPS[n]):
                b = [m for m, group in enumerate(Y_GROUPS) if e in group][0]
                place = e - Y_GROUPS[b][0]
                cols = slice(r * N, (r + 1) * N)
                nc.tensor.matmul_mx(out=y_ps[b][:, place * C:(place + 1) * C], lhsT=codes[:, cols].bitcast(FP8X4),
                                    lhsT_scale=w2_scales[n][:, cols], rhs=h_codes[e // 2][:, part(e, C)].bitcast(FP8X4),
                                    rhs_scale=h_scales[e // 2][:, part(e, C)], start=True, stop=True)

        spread_gate()
        for j in range(PACK):
            gather_x(FIRST_RUN, j)
            gather_x(MIDDLE_RUN, j)
        weigh_x(FIRST_RUN)
        quantize_x(FIRST_RUN)
        for j in range(PACK):
            gather_x(LAST_RUN, j)

        round_w1(0)
        weigh_x(MIDDLE_RUN)
        round_w1(1)
        first_product(0)
        quantize_x(MIDDLE_RUN)
        first_product(1)
        weigh_x(LAST_RUN)
        round_w1(2)
        activate(0)
        activate(1)
        first_product(2)
        quantize_x(LAST_RUN)

        activated = 2
        for q, e in enumerate(range(3, E - 1, 2)):
            round_w1(e)
            for before in range(activated, e):
                activate(before)
            activated = e
            round_w1(e + 1)
            quantize_h(q, "h_codes%d" % q)
            first_product(e)
            first_product(e + 1)
        for before in range(activated, E - 1):
            activate(before)
        round_w1(E - 1)
        quantize_h(PAIRS - 2, "h_codes%d" % (PAIRS - 2))
        first_product(E - 1)

        round_w2(0)
        activate(E - 1)
        round_w2(1)
        second_product(1, "w2_codes1")
        second_product(0, "w2_raw1")
        round_w2(2)
        second_product(2, "w2_codes2")
        quantize_h(PAIRS - 1, "w2_raw2")
        for n in (3, 4, 5):
            round_w2(n)
        for n in (3, 5, 4):
            second_product(n, "w2_codes%d" % n)

        y_all = held.tile([P, S], F32, name="y_all", tag="w2_raw%d" % W2_ON_SCALAR[-1], align_bytes=64)
        for b, group in enumerate(Y_GROUPS):
            copy(b in Y_ON_VECTOR, y_all[:, group[0] * C:(group[-1] + 1) * C], y_ps[b][:, 0:len(group) * C])

        first = held.tile([P, T], F32, name="first")
        second = held.tile([P, T - PLAIN], F32, name="second")
        total = held.tile([P, T], F32, name="total")

        def looked_up(positions, lo, hi):
            return y_all[:].indirect(positions[:, lo // PER_COLUMN:hi // PER_COLUMN])

        nc.vector.tensor_copy(first[:, 0:OWN], looked_up(pos1_sb, 0, OWN))
        nc.vector.tensor_copy(second[:], looked_up(pos2_sb, PLAIN, T))
        for lo, hi in FUSED + ((PLAIN, T),):
            nc.scalar.activation(first[:, max(lo, OWN):hi], looked_up(pos1_sb, max(lo, OWN), hi), COPY)
        for lo, hi in FUSED:
            nc.vector.tensor_tensor(total[:, lo:hi], looked_up(pos2_sb, lo, hi), first[:, lo:hi], ADD)
            nc.sync.dma_start(out[:, lo:hi], total[:, lo:hi])
        nc.vector.tensor_tensor(total[:, PLAIN:T], second[:], first[:, PLAIN:T], ADD)
        nc.sync.dma_start(out[:, PLAIN:T], total[:, PLAIN:T])
